import numpy as np
import ml_dtypes


def mxq(x, axis, fmt="e4m3"):
    dtype, down = {"e4m3": (ml_dtypes.float8_e4m3fn, 7), "e5m2": (ml_dtypes.float8_e5m2, 14)}[fmt]
    v = np.moveaxis(np.asarray(x, np.float32).astype(ml_dtypes.bfloat16).astype(np.float64), axis, -1)
    blocks = v.reshape(v.shape[:-1] + (-1, 32))
    amax = np.abs(blocks).max(-1, keepdims=True)
    byte = np.maximum(np.where(amax > 0, np.frexp(amax)[1] - 1 + 127, 0) - down, 1)
    scale = np.exp2(byte - 127.0)
    codes = (blocks / scale).astype(np.float32).astype(dtype).astype(np.float64)
    return np.moveaxis((codes * scale).reshape(v.shape), -1, axis)


WIDE = False


def mx_kscale(k):
    if not WIDE:
        return np.ones(k)
    levels = np.array([10, -10, 5, -5, 0])
    if k % 512:
        return np.exp2(np.random.permutation(np.resize(levels, k // 32))).repeat(32)
    a = np.empty((k // 512, 16))
    for p in range(k // 512):
        a[p, :8] = np.random.permutation(np.resize(levels, 8))
        for g in range(8):
            far = levels[np.abs(levels - a[p, g]) >= 10]
            a[p, g + 8] = far[np.random.randint(len(far))]
    return np.exp2(a.ravel()).repeat(32)


def f64(x):
    return np.asarray(x).astype(np.float64)


def striped(idx):
    return np.tile(idx.reshape(-1, 16).T, (8, 1)).astype(np.uint16)


def unstriped(offs):
    return offs[:16].T.reshape(-1).astype(np.int64)


def pack_weight(w):
    k, n = w.shape
    w = f64(np.asarray(w, np.float32).astype(ml_dtypes.bfloat16)).reshape(k // 32, 32, n)
    amax = np.abs(w).max(1)
    byte = np.clip(np.where(amax > 0, np.frexp(amax)[1] - 1 + 127 - 7, 1), 1, 254)
    scaled = (w * np.exp2(127.0 - byte)[:, None, :]).reshape(k, n).astype(np.float32)
    words = np.ascontiguousarray(scaled.reshape(k // 512, 128, 4, n).transpose(0, 1, 3, 2)).astype(ml_dtypes.float8_e4m3fn).view(np.uint8)
    return words, np.ascontiguousarray(byte.astype(np.uint8).reshape(k // 512, 16, n))


def unpack_weight(words, scales):
    g, p, n, _ = words.shape
    vals = np.ascontiguousarray(words).view(ml_dtypes.float8_e4m3fn).astype(np.float64) * np.repeat(np.exp2(scales.astype(np.float64) - 127.0), 8, axis=1)[..., None]
    return vals.transpose(0, 1, 3, 2).reshape(g * 512, n)


def relu(v):
    return np.maximum(v, 0.0)


def sigmoid(v):
    return 1.0 / (1.0 + np.exp(-np.maximum(v, -700.0)))

def planes(y):
    n, m = y.shape
    v = y.astype(np.float32).astype(ml_dtypes.bfloat16).astype(np.float64).reshape(n // 32, 32, m)
    top = np.abs(v).max(1)
    byte = np.clip(np.where(top > 0, np.frexp(top)[1] - 1 + 127 - 7, 1), 1, 254)
    codes = (v * np.exp2(127.0 - byte)[:, None, :]).reshape(n, m).astype(np.float32).astype(ml_dtypes.float8_e4m3fn).view(np.uint8)
    words = codes.reshape(n // 512, 128, 4, m).transpose(0, 1, 3, 2)
    return np.ascontiguousarray(words), np.ascontiguousarray(byte.astype(np.uint8).reshape(n // 512, 16, m))


K, T, N, U = 512, 512, 512, 1024


def setup_inputs():
    n = np.random.standard_normal
    s = mx_kscale(K)[:, None]
    packed_xT = pack_weight(n((K, T)) * s)
    return {
        "x_words": packed_xT[0],
        "x_scales": packed_xT[1],
        "mem": n((N, U)).astype(np.float32),
        "w1": (n((K, N)) / np.sqrt(K) / s).astype(np.float32),
        "w2": (n((K, N)) / np.sqrt(K) / s).astype(np.float32),
        "slot": striped(np.random.permutation(U)[:T]),
    }


def reference(x_words, x_scales, mem, w1, w2, slot):
    old = f64(mem)[:, unstriped(slot)]
    xq = unpack_weight(x_words, x_scales)
    g = sigmoid(mxq(f64(w2), 0, "e4m3").T @ xq)
    y = relu(mxq(f64(w1), 0, "e4m3").T @ xq)
    out = f64(mem).copy()
    out[:, unstriped(slot)] = old + g * (y - old)
    return (out,) + planes(out)

@@ -1,0 +1,146 @@
+from contextlib import ExitStack
+
+import concourse.mybir as mybir
+
+K, T, N, U = 512, 512, 512, 1024
+FLOPS = 2 * 2 * K * N * T
+
+F32 = mybir.dt.float32
+BF16 = mybir.dt.bfloat16
+I32 = mybir.dt.int32
+U32 = mybir.dt.uint32
+U16 = mybir.dt.uint16
+U8 = mybir.dt.uint8
+FP8X4 = mybir.dt.float8_e4m3fn_x4
+ALU = mybir.AluOpType
+ACT = mybir.ActivationFunctionType
+
+P = 128
+PACK = 4
+HALF = U // 2
+QUARTER = U // 4
+
+
+def tile_picked_wgmem_relu_lo_kernel(tc, x_words, x_scales, mem, w1, w2, slot, out_0, out_1, out_2):
+    nc = tc.nc
+    with ExitStack() as ctx:
+        keep = ctx.enter_context(tc.tile_pool(name="keep", bufs=1))
+        psum = ctx.enter_context(tc.psum_pool(name="psum", bufs=1))
+
+        def sb(name, shape, dtype):
+            return keep.tile(shape, dtype, name=name, align_bytes=64)
+
+        offsets = keep.tile([P, T // 16], U16, name="offsets")
+        x_codes = sb("x_codes", [P, T], U32)
+        x_plane = sb("x_plane", [P, T], U8)
+        w1_raw = sb("w1_raw", [P, PACK, N], F32)
+        w2_raw = sb("w2_raw", [P, PACK, N], F32)
+        window = [sb("window%d" % t, [P, U], F32) for t in range(PACK)]
+        mem_rows = mem.rearrange("(p t) u -> t p u", t=PACK)
+        out_rows = out_0.rearrange("(p t) u -> t p u", t=PACK)
+
+        warm = sb("warm", [P, 8], F32)
+        nc.vector.memset(warm[:], 0.0)
+        nc.vector.memset(x_plane[:].bitcast(I32), 0)
+        nc.scalar.activation(warm[:, 0:1], warm[:, 1:2], ACT.Sigmoid)
+
+        nc.sync.dma_start(w2_raw[:], w2.rearrange("(p j) n -> p j n", j=PACK))
+        for q in range(4):
+            nc.scalar.dma_start(
+                x_plane[32 * q : 32 * q + 4, :].bitcast(I32), x_scales[0, 4 * q : 4 * q + 4, :].bitcast(I32)
+            )
+        nc.sync.dma_start(x_codes[:].bitcast(I32), x_words[0].rearrange("p n r -> p (n r)").bitcast(I32))
+        nc.sync.dma_start(offsets[:], slot)
+        nc.sync.dma_start(window[0][:], mem_rows[0])
+        nc.sync.dma_start(w1_raw[:], w1.rearrange("(p j) n -> p j n", j=PACK))
+        for t in range(1, PACK):
+            nc.sync.dma_start(window[t][:], mem_rows[t])
+
+        def deal(engine_copy, name, raw, t0, t1):
+            dealt = sb(name, [P, t1 - t0, P, PACK], BF16)
+            engine_copy(
+                dealt[:].rearrange("p t m j -> p m j t"),
+                raw[:].rearrange("p j (m t) -> p m j t", t=PACK)[:, :, :, t0:t1],
+            )
+            return dealt
+
+        def project(name, dealt_t):
+            codes = sb(name + "_codes", [P, P], U32)
+            plane = sb(name + "_plane", [P, P], U8)
+            nc.vector.quantize_mx(out=codes[:].bitcast(FP8X4), scales=plane[:], in_=dealt_t.rearrange("p m j -> p (m j)"))
+            acc = psum.tile([P, T], F32, name=name + "_acc")
+            nc.tensor.matmul_mx(
+                out=acc[:], lhsT=codes[:].bitcast(FP8X4), lhsT_scale=plane[:],
+                rhs=x_codes[:].bitcast(FP8X4), rhs_scale=x_plane[:], start=True, stop=True,
+            )
+            return acc
+
+        gate, stay = [], []
+
+        def gates(t, dealt_t):
+            acc = project("u%d" % t, dealt_t)
+            stay.append(sb("stay%d" % t, [P, T], F32))
+            gate.append(sb("gate%d" % t, [P, T], F32))
+            nc.scalar.activation(stay[t][:], acc[:], ACT.Sigmoid, scale=-1.0)
+            nc.scalar.activation(gate[t][:], acc[:], ACT.Sigmoid)
+
+        w2_first = deal(nc.vector.tensor_copy, "w2_first", w2_raw, 0, 1)
+        gates(0, w2_first[:, 0])
+        w2_rest = deal(nc.vector.tensor_copy, "w2_rest", w2_raw, 1, PACK)
+        for t in range(1, PACK):
+            gates(t, w2_rest[:, t - 1])
+
+        kept = [sb("kept%d" % t, [P, T], F32) for t in range(PACK)]
+        fresh = [sb("fresh%d" % t, [P, T], F32) for t in range(PACK)]
+
+        def look_up(t):
+            nc.vector.tensor_tensor(kept[t][:], window[t][:].indirect(offsets[:]), stay[t][:], ALU.mult)
+
+        def candidate(t, acc):
+            nc.vector.scalar_tensor_tensor(fresh[t][:], acc[:], 0.0, gate[t][:], ALU.max, ALU.mult)
+
+        low = sb("low", [P, HALF, PACK], BF16)
+        high = sb("high", [P, HALF, PACK], BF16)
+
+        def put(t):
+            nc.vector.tensor_tensor(window[t][:].indirect(offsets[:]), kept[t][:], fresh[t][:], ALU.add)
+            nc.sync.dma_start(out_rows[t], window[t][:])
+
+        look_up(0)
+        w1_first = deal(nc.vector.tensor_copy, "w1_first", w1_raw, 0, 1)
+        y_acc = [project("y0", w1_first[:, 0])]
+        w1_rest = deal(nc.scalar.copy, "w1_rest", w1_raw, 1, PACK)
+        look_up(1)
+        candidate(0, y_acc[0])
+        for t in range(1, PACK):
+            y_acc.append(project("y%d" % t, w1_rest[:, t - 1]))
+        for t in range(PACK - 1):
+            put(t)
+            nc.scalar.copy(low[:, :, t], window[t][:, 0:HALF])
+            if t == PACK - 2:
+                nc.scalar.copy(high[:, :, t : t + 2], window[t][:, HALF:U].unsqueeze(2).to_broadcast([P, HALF, 2]))
+            else:
+                nc.scalar.copy(high[:, :, t], window[t][:, HALF:U])
+            candidate(t + 1, y_acc[t + 1])
+            if t + 2 < PACK:
+                look_up(t + 2)
+        last = PACK - 1
+        put(last)
+
+        out_plane = sb("out_plane", [P, U], U8)
+        out_words = out_1[0].rearrange("p c r -> p (c r)").bitcast(I32)
+
+        def pack(name, source, c0, width):
+            codes = sb(name, [P, width], U32)
+            nc.vector.quantize_mx(out=codes[:].bitcast(FP8X4), scales=out_plane[:, c0 : c0 + width], in_=source.rearrange("p c t -> p (c t)"))
+            nc.sync.dma_start(out_words[:, c0 : c0 + width], codes[:].bitcast(I32))
+
+        nc.scalar.copy(low[:, 0:QUARTER, last], window[last][:, 0:QUARTER])
+        nc.scalar.copy(low[:, QUARTER:HALF, last], window[last][:, QUARTER:HALF])
+        nc.vector.tensor_copy(high[:, :, last], window[last][:, HALF:U])
+        pack("codes0", low[:, 0:QUARTER], 0, QUARTER)
+        pack("codes2", high[:], HALF, HALF)
+        pack("codes1", low[:, QUARTER:HALF], QUARTER, QUARTER)
+        for q in range(4):
+            queue = nc.scalar if q % 2 else nc.sync
+            queue.dma_start(out_2[0, 4 * q : 4 * q + 4, :].bitcast(I32), out_plane[32 * q : 32 * q + 4, :].bitcast(I32))

@@ -33,35 +33,40 @@ def tile_picked_wgmem_relu_lo_kernel(tc, x_words, x_scales, mem, w1, w2, slot, o
         offsets = keep.tile([P, T // 16], U16, name="offsets")
         x_codes = sb("x_codes", [P, T], U32)
         x_plane = sb("x_plane", [P, T], U8)
-        w1_raw = sb("w1_raw", [P, PACK, N], F32)
-        w2_raw = sb("w2_raw", [P, PACK, N], F32)
+        w1_raw = [sb("w1_raw%d" % h, [P, PACK, N // 2], F32) for h in range(2)]
+        w2_raw = [sb("w2_raw%d" % h, [P, PACK, N // 2], F32) for h in range(2)]
         window = [sb("window%d" % t, [P, U], F32) for t in range(PACK)]
         mem_rows = mem.rearrange("(p t) u -> t p u", t=PACK)
         out_rows = out_0.rearrange("(p t) u -> t p u", t=PACK)
 
         warm = sb("warm", [P, 8], F32)
         nc.vector.memset(warm[:], 0.0)
-        nc.vector.memset(x_plane[:].bitcast(I32), 0)
+        nc.gpsimd.memset(x_plane[:].bitcast(I32), 0)
         nc.scalar.activation(warm[:, 0:1], warm[:, 1:2], ACT.Sigmoid)
 
-        nc.sync.dma_start(w2_raw[:], w2.rearrange("(p j) n -> p j n", j=PACK))
+        def load_weight(raw, w):
+            for h in range(2):
+                nc.sync.dma_start(raw[h][:], w.rearrange("(p j) n -> p j n", j=PACK)[:, :, h * (N // 2) : (h + 1) * (N // 2)])
+
+        load_weight(w2_raw, w2)
         for q in range(4):
-            nc.scalar.dma_start(
+            nc.sync.dma_start(
                 x_plane[32 * q : 32 * q + 4, :].bitcast(I32), x_scales[0, 4 * q : 4 * q + 4, :].bitcast(I32)
             )
         nc.sync.dma_start(x_codes[:].bitcast(I32), x_words[0].rearrange("p n r -> p (n r)").bitcast(I32))
         nc.sync.dma_start(offsets[:], slot)
         nc.sync.dma_start(window[0][:], mem_rows[0])
-        nc.sync.dma_start(w1_raw[:], w1.rearrange("(p j) n -> p j n", j=PACK))
+        load_weight(w1_raw, w1)
         for t in range(1, PACK):
             nc.sync.dma_start(window[t][:], mem_rows[t])
 
         def deal(engine_copy, name, raw, t0, t1):
             dealt = sb(name, [P, t1 - t0, P, PACK], BF16)
-            engine_copy(
-                dealt[:].rearrange("p t m j -> p m j t"),
-                raw[:].rearrange("p j (m t) -> p m j t", t=PACK)[:, :, :, t0:t1],
-            )
+            for h in range(2):
+                engine_copy(
+                    dealt[:, :, h * (P // 2) : (h + 1) * (P // 2), :].rearrange("p t m j -> p m j t"),
+                    raw[h][:].rearrange("p j (m t) -> p m j t", t=PACK)[:, :, :, t0:t1],
+                )
             return dealt
 
         def project(name, dealt_t):
@@ -75,20 +80,20 @@ def tile_picked_wgmem_relu_lo_kernel(tc, x_words, x_scales, mem, w1, w2, slot, o
             )
             return acc
 
-        gate, stay = [], []
+        gate = [sb("gate%d" % t, [P, T], F32) for t in range(PACK)]
+        stay = [sb("stay%d" % t, [P, T], F32) for t in range(PACK)]
 
-        def gates(t, dealt_t):
-            acc = project("u%d" % t, dealt_t)
-            stay.append(sb("stay%d" % t, [P, T], F32))
-            gate.append(sb("gate%d" % t, [P, T], F32))
-            nc.scalar.activation(stay[t][:], acc[:], ACT.Sigmoid, scale=-1.0)
-            nc.scalar.activation(gate[t][:], acc[:], ACT.Sigmoid)
+        def gates(t):
+            nc.scalar.activation(stay[t][:], u_acc[t][:], ACT.Sigmoid, scale=-1.0)
+            nc.scalar.activation(gate[t][:], u_acc[t][:], ACT.Sigmoid)
 
         w2_first = deal(nc.vector.tensor_copy, "w2_first", w2_raw, 0, 1)
-        gates(0, w2_first[:, 0])
-        w2_rest = deal(nc.vector.tensor_copy, "w2_rest", w2_raw, 1, PACK)
+        w2_rest = deal(nc.scalar.copy, "w2_rest", w2_raw, 1, PACK)
+        u_acc = [project("u0", w2_first[:, 0])]
         for t in range(1, PACK):
-            gates(t, w2_rest[:, t - 1])
+            u_acc.append(project("u%d" % t, w2_rest[:, t - 1]))
+        gates(0)
+        gates(1)
 
         kept = [sb("kept%d" % t, [P, T], F32) for t in range(PACK)]
         fresh = [sb("fresh%d" % t, [P, T], F32) for t in range(PACK)]
@@ -106,24 +111,34 @@ def tile_picked_wgmem_relu_lo_kernel(tc, x_words, x_scales, mem, w1, w2, slot, o
             nc.vector.tensor_tensor(window[t][:].indirect(offsets[:]), kept[t][:], fresh[t][:], ALU.add)
             nc.sync.dma_start(out_rows[t], window[t][:])
 
-        look_up(0)
-        w1_first = deal(nc.vector.tensor_copy, "w1_first", w1_raw, 0, 1)
-        y_acc = [project("y0", w1_first[:, 0])]
-        w1_rest = deal(nc.scalar.copy, "w1_rest", w1_raw, 1, PACK)
-        look_up(1)
-        candidate(0, y_acc[0])
-        for t in range(1, PACK):
-            y_acc.append(project("y%d" % t, w1_rest[:, t - 1]))
-        for t in range(PACK - 1):
-            put(t)
-            nc.scalar.copy(low[:, :, t], window[t][:, 0:HALF])
+        def regroup(t):
             if t == PACK - 2:
                 nc.scalar.copy(high[:, :, t : t + 2], window[t][:, HALF:U].unsqueeze(2).to_broadcast([P, HALF, 2]))
             else:
                 nc.scalar.copy(high[:, :, t], window[t][:, HALF:U])
-            candidate(t + 1, y_acc[t + 1])
-            if t + 2 < PACK:
-                look_up(t + 2)
+            nc.scalar.copy(low[:, :, t], window[t][:, 0:HALF])
+
+        look_up(0)
+        w1_first = deal(nc.vector.tensor_copy, "w1_first", w1_raw, 0, 1)
+        y_acc = [project("y0", w1_first[:, 0])]
+        w1_rest = deal(nc.scalar.copy, "w1_rest", w1_raw, 1, PACK)
+        gates(2)
+        gates(3)
+        look_up(1)
+        candidate(0, y_acc[0])
+        look_up(2)
+        for t in range(1, PACK):
+            y_acc.append(project("y%d" % t, w1_rest[:, t - 1]))
+        put(0)
+        regroup(0)
+        candidate(1, y_acc[1])
+        look_up(3)
+        put(1)
+        regroup(1)
+        candidate(2, y_acc[2])
+        candidate(3, y_acc[3])
+        put(2)
+        regroup(2)
         last = PACK - 1
         put(last)
 

@@ -27,36 +27,37 @@ def tile_picked_wgmem_relu_lo_kernel(tc, x_words, x_scales, mem, w1, w2, slot, o
         keep = ctx.enter_context(tc.tile_pool(name="keep", bufs=1))
         psum = ctx.enter_context(tc.psum_pool(name="psum", bufs=1))
 
-        def sb(name, shape, dtype):
-            return keep.tile(shape, dtype, name=name, align_bytes=64)
+        def sb(name, shape, dtype, tag=None):
+            return keep.tile(shape, dtype, name=name, tag=tag or name, align_bytes=64)
 
         offsets = keep.tile([P, T // 16], U16, name="offsets")
         x_codes = sb("x_codes", [P, T], U32)
         x_plane = sb("x_plane", [P, T], U8)
-        w1_raw = [sb("w1_raw%d" % h, [P, PACK, N // 2], F32) for h in range(2)]
-        w2_raw = [sb("w2_raw%d" % h, [P, PACK, N // 2], F32) for h in range(2)]
+        w1_raw = [sb("w1_raw%d" % h, [P, 2, N], F32) for h in range(2)]
+        w2_raw = [sb("w2_raw%d" % h, [P, 2, N], F32) for h in range(2)]
         window = [sb("window%d" % t, [P, U], F32) for t in range(PACK)]
         mem_rows = mem.rearrange("(p t) u -> t p u", t=PACK)
         out_rows = out_0.rearrange("(p t) u -> t p u", t=PACK)
 
         warm = sb("warm", [P, 8], F32)
+        nc.vector.memset(x_plane[:].bitcast(I32), 0)
         nc.vector.memset(warm[:], 0.0)
-        nc.gpsimd.memset(x_plane[:].bitcast(I32), 0)
         nc.scalar.activation(warm[:, 0:1], warm[:, 1:2], ACT.Sigmoid)
 
-        def load_weight(raw, w):
-            for h in range(2):
-                nc.sync.dma_start(raw[h][:], w.rearrange("(p j) n -> p j n", j=PACK)[:, :, h * (N // 2) : (h + 1) * (N // 2)])
+        def load_weight(raw, w, h):
+            nc.sync.dma_start(raw[h][:], w.rearrange("(p j) n -> p j n", j=PACK)[:, 2 * h : 2 * h + 2, :])
 
-        load_weight(w2_raw, w2)
+        nc.sync.dma_start(offsets[:], slot)
+        load_weight(w2_raw, w2, 0)
         for q in range(4):
             nc.sync.dma_start(
                 x_plane[32 * q : 32 * q + 4, :].bitcast(I32), x_scales[0, 4 * q : 4 * q + 4, :].bitcast(I32)
             )
+        load_weight(w2_raw, w2, 1)
         nc.sync.dma_start(x_codes[:].bitcast(I32), x_words[0].rearrange("p n r -> p (n r)").bitcast(I32))
-        nc.sync.dma_start(offsets[:], slot)
         nc.sync.dma_start(window[0][:], mem_rows[0])
-        load_weight(w1_raw, w1)
+        load_weight(w1_raw, w1, 0)
+        load_weight(w1_raw, w1, 1)
         for t in range(1, PACK):
             nc.sync.dma_start(window[t][:], mem_rows[t])
 
@@ -64,21 +65,25 @@ def tile_picked_wgmem_relu_lo_kernel(tc, x_words, x_scales, mem, w1, w2, slot, o
             dealt = sb(name, [P, t1 - t0, P, PACK], BF16)
             for h in range(2):
                 engine_copy(
-                    dealt[:, :, h * (P // 2) : (h + 1) * (P // 2), :].rearrange("p t m j -> p m j t"),
-                    raw[h][:].rearrange("p j (m t) -> p m j t", t=PACK)[:, :, :, t0:t1],
+                    dealt[:, :, :, 2 * h : 2 * h + 2].rearrange("p t m j -> p m t j"),
+                    raw[h][:].rearrange("p j (m t) -> p m t j", t=PACK)[:, :, t0:t1, :],
                 )
             return dealt
 
-        def project(name, dealt_t):
-            codes = sb(name + "_codes", [P, P], U32)
-            plane = sb(name + "_plane", [P, P], U8)
-            nc.vector.quantize_mx(out=codes[:].bitcast(FP8X4), scales=plane[:], in_=dealt_t.rearrange("p m j -> p (m j)"))
-            acc = psum.tile([P, T], F32, name=name + "_acc")
-            nc.tensor.matmul_mx(
-                out=acc[:], lhsT=codes[:].bitcast(FP8X4), lhsT_scale=plane[:],
-                rhs=x_codes[:].bitcast(FP8X4), rhs_scale=x_plane[:], start=True, stop=True,
-            )
-            return acc
+        def project(name, dealt):
+            count = dealt.shape[1]
+            codes = sb(name + "_codes", [P, count * P], U32)
+            plane = sb(name + "_plane", [P, count * P], U8)
+            nc.vector.quantize_mx(out=codes[:].bitcast(FP8X4), scales=plane[:], in_=dealt.rearrange("p t m j -> p (t m j)"))
+            sums = []
+            for i in range(count):
+                acc = psum.tile([P, T], F32, name="%s_acc%d" % (name, i))
+                nc.tensor.matmul_mx(
+                    out=acc[:], lhsT=codes[:, i * P : (i + 1) * P].bitcast(FP8X4), lhsT_scale=plane[:, i * P : (i + 1) * P],
+                    rhs=x_codes[:].bitcast(FP8X4), rhs_scale=x_plane[:], start=True, stop=True,
+                )
+                sums.append(acc)
+            return sums
 
         gate = [sb("gate%d" % t, [P, T], F32) for t in range(PACK)]
         stay = [sb("stay%d" % t, [P, T], F32) for t in range(PACK)]
@@ -87,29 +92,20 @@ def tile_picked_wgmem_relu_lo_kernel(tc, x_words, x_scales, mem, w1, w2, slot, o
             nc.scalar.activation(stay[t][:], u_acc[t][:], ACT.Sigmoid, scale=-1.0)
             nc.scalar.activation(gate[t][:], u_acc[t][:], ACT.Sigmoid)
 
-        w2_first = deal(nc.vector.tensor_copy, "w2_first", w2_raw, 0, 1)
-        w2_rest = deal(nc.scalar.copy, "w2_rest", w2_raw, 1, PACK)
-        u_acc = [project("u0", w2_first[:, 0])]
-        for t in range(1, PACK):
-            u_acc.append(project("u%d" % t, w2_rest[:, t - 1]))
+        w2_0 = deal(nc.vector.tensor_copy, "w2_0", w2_raw, 0, 1)
+        w2_1 = deal(nc.vector.tensor_copy, "w2_1", w2_raw, 1, 2)
+        w2_23 = deal(nc.scalar.copy, "w2_23", w2_raw, 2, PACK)
+        u_acc = project("u0", w2_0[:]) + project("u1", w2_1[:]) + project("u23", w2_23[:])
         gates(0)
         gates(1)
 
         kept = [sb("kept%d" % t, [P, T], F32) for t in range(PACK)]
-        fresh = [sb("fresh%d" % t, [P, T], F32) for t in range(PACK)]
 
         def look_up(t):
             nc.vector.tensor_tensor(kept[t][:], window[t][:].indirect(offsets[:]), stay[t][:], ALU.mult)
 
-        def candidate(t, acc):
-            nc.vector.scalar_tensor_tensor(fresh[t][:], acc[:], 0.0, gate[t][:], ALU.max, ALU.mult)
-
         low = sb("low", [P, HALF, PACK], BF16)
         high = sb("high", [P, HALF, PACK], BF16)
-
-        def put(t):
-            nc.vector.tensor_tensor(window[t][:].indirect(offsets[:]), kept[t][:], fresh[t][:], ALU.add)
-            nc.sync.dma_start(out_rows[t], window[t][:])
 
         def regroup(t):
             if t == PACK - 2:
@@ -119,28 +115,37 @@ def tile_picked_wgmem_relu_lo_kernel(tc, x_words, x_scales, mem, w1, w2, slot, o
             nc.scalar.copy(low[:, :, t], window[t][:, 0:HALF])
 
         look_up(0)
-        w1_first = deal(nc.vector.tensor_copy, "w1_first", w1_raw, 0, 1)
-        y_acc = [project("y0", w1_first[:, 0])]
+        w1_0 = deal(nc.vector.tensor_copy, "w1_0", w1_raw, 0, 1)
+        y_acc = project("y0", w1_0[:])
         w1_rest = deal(nc.scalar.copy, "w1_rest", w1_raw, 1, PACK)
         gates(2)
         gates(3)
-        look_up(1)
-        candidate(0, y_acc[0])
-        look_up(2)
-        for t in range(1, PACK):
-            y_acc.append(project("y%d" % t, w1_rest[:, t - 1]))
-        put(0)
-        regroup(0)
-        candidate(1, y_acc[1])
-        look_up(3)
-        put(1)
-        regroup(1)
-        candidate(2, y_acc[2])
-        candidate(3, y_acc[3])
-        put(2)
-        regroup(2)
         last = PACK - 1
-        put(last)
+        new = [sb("new%d" % t, [P, T], F32) for t in range(PACK)]
+        fresh0 = sb("fresh0", [P, T], F32)
+
+        def put(t):
+            nc.vector.tensor_copy(window[t][:].indirect(offsets[:]), new[t][:])
+            nc.sync.dma_start(out_rows[t], window[t][:])
+
+        look_up(1)
+        y_acc = y_acc + project("y1", w1_rest[:, 0:1]) + project("y23", w1_rest[:, 1:3])
+        nc.vector.scalar_tensor_tensor(fresh0[:], y_acc[0][:], 0.0, gate[0][:], ALU.max, ALU.mult)
+        look_up(2)
+        nc.vector.tensor_tensor(new[0][:], kept[0][:], fresh0[:], ALU.add)
+        look_up(3)
+        put(0)
+        cand = [None]
+        for t in range(1, PACK):
+            cand.append(sb("cand%d" % t, [P, T], F32))
+            nc.scalar.activation(cand[t][:], y_acc[t][:], ACT.Relu)
+        for t in range(1, PACK):
+            fresh = sb("fresh%d" % t, [P, T], F32, tag="stay%d" % last)
+            nc.gpsimd.tensor_tensor(fresh[:], cand[t][:], gate[t][:], ALU.mult)
+            nc.gpsimd.tensor_tensor(new[t][:], kept[t][:], fresh[:], ALU.add)
+        for t in range(1, PACK):
+            regroup(t - 1)
+            put(t)
 
         out_plane = sb("out_plane", [P, U], U8)
         out_words = out_1[0].rearrange("p c r -> p (c r)").bitcast(I32)

@@ -55,49 +55,57 @@ def tile_picked_wgmem_relu_lo_kernel(tc, x_words, x_scales, mem, w1, w2, slot, o
             )
         load_weight(w2_raw, w2, 1)
         nc.sync.dma_start(x_codes[:].bitcast(I32), x_words[0].rearrange("p n r -> p (n r)").bitcast(I32))
-        nc.sync.dma_start(window[0][:], mem_rows[0])
-        load_weight(w1_raw, w1, 0)
-        load_weight(w1_raw, w1, 1)
-        for t in range(1, PACK):
+        for t in range(PACK - 1):
             nc.sync.dma_start(window[t][:], mem_rows[t])
+        load_weight(w1_raw, w1, 0)
+        nc.sync.dma_start(window[PACK - 1][:], mem_rows[PACK - 1])
+        load_weight(w1_raw, w1, 1)
 
-        def deal(engine_copy, name, raw, t0, t1):
-            dealt = sb(name, [P, t1 - t0, P, PACK], BF16)
-            for h in range(2):
-                engine_copy(
-                    dealt[:, :, :, 2 * h : 2 * h + 2].rearrange("p t m j -> p m t j"),
-                    raw[h][:].rearrange("p j (m t) -> p m t j", t=PACK)[:, :, t0:t1, :],
-                )
-            return dealt
+        def deal(engine_copy, dealt, raw, h, t0):
+            engine_copy(
+                dealt[:, :, :, 2 * h : 2 * h + 2].rearrange("p t m j -> p m t j"),
+                raw[h][:].rearrange("p j (m t) -> p m t j", t=PACK)[:, :, t0 : t0 + dealt.shape[1], :],
+            )
 
-        def project(name, dealt):
+        def quantise(name, dealt):
             count = dealt.shape[1]
             codes = sb(name + "_codes", [P, count * P], U32)
             plane = sb(name + "_plane", [P, count * P], U8)
-            nc.vector.quantize_mx(out=codes[:].bitcast(FP8X4), scales=plane[:], in_=dealt.rearrange("p t m j -> p (t m j)"))
-            sums = []
-            for i in range(count):
-                acc = psum.tile([P, T], F32, name="%s_acc%d" % (name, i))
-                nc.tensor.matmul_mx(
-                    out=acc[:], lhsT=codes[:, i * P : (i + 1) * P].bitcast(FP8X4), lhsT_scale=plane[:, i * P : (i + 1) * P],
-                    rhs=x_codes[:].bitcast(FP8X4), rhs_scale=x_plane[:], start=True, stop=True,
-                )
-                sums.append(acc)
-            return sums
+            nc.vector.quantize_mx(out=codes[:].bitcast(FP8X4), scales=plane[:], in_=dealt[:].rearrange("p t m j -> p (t m j)"))
+            return [(codes[:, i * P : (i + 1) * P], plane[:, i * P : (i + 1) * P]) for i in range(count)]
+
+        def multiply(operand, bank, c0, c1):
+            acc = psum.tile([P, c1 - c0], F32, name="acc", tag="bank%d" % bank)
+            nc.tensor.matmul_mx(
+                out=acc[:], lhsT=operand[0].bitcast(FP8X4), lhsT_scale=operand[1],
+                rhs=x_codes[:, c0:c1].bitcast(FP8X4), rhs_scale=x_plane[:, c0:c1], start=True, stop=True,
+            )
+            return acc
+
+        def dealt_tiles(name):
+            return [sb(name + "_0", [P, 1, P, PACK], BF16), sb(name + "_1", [P, 1, P, PACK], BF16), sb(name + "_23", [P, 2, P, PACK], BF16)]
 
         gate = [sb("gate%d" % t, [P, T], F32) for t in range(PACK)]
         stay = [sb("stay%d" % t, [P, T], F32) for t in range(PACK)]
 
-        def gates(t):
+        dealt = dealt_tiles("w2")
+        for h in range(2):
+            deal(nc.vector.tensor_copy, dealt[0], w2_raw, h, 0)
+            deal(nc.vector.tensor_copy, dealt[1], w2_raw, h, 1)
+            deal(nc.scalar.copy, dealt[2], w2_raw, h, 2)
+        halves = [slice(h * (T // 2), (h + 1) * (T // 2)) for h in range(2)]
+        offset_halves = [offsets[:, h * (T // 32) : (h + 1) * (T // 32)] for h in range(2)]
+        first = quantise("u0", dealt[0])[0]
+        u_first = [multiply(first, h, halves[h].start, halves[h].stop) for h in range(2)]
+        u_acc = [None]
+        for operand in quantise("u1", dealt[1]) + quantise("u2", dealt[2]):
+            u_acc.append(multiply(operand, len(u_acc) + 1, 0, T))
+        for h in range(2):
+            nc.scalar.activation(stay[0][:, halves[h]], u_first[h][:], ACT.Sigmoid, scale=-1.0)
+        for t in range(1, PACK):
             nc.scalar.activation(stay[t][:], u_acc[t][:], ACT.Sigmoid, scale=-1.0)
-            nc.scalar.activation(gate[t][:], u_acc[t][:], ACT.Sigmoid)
-
-        w2_0 = deal(nc.vector.tensor_copy, "w2_0", w2_raw, 0, 1)
-        w2_1 = deal(nc.vector.tensor_copy, "w2_1", w2_raw, 1, 2)
-        w2_23 = deal(nc.scalar.copy, "w2_23", w2_raw, 2, PACK)
-        u_acc = project("u0", w2_0[:]) + project("u1", w2_1[:]) + project("u23", w2_23[:])
-        gates(0)
-        gates(1)
+        for h in range(2):
+            nc.scalar.activation(gate[0][:, halves[h]], u_first[h][:], ACT.Sigmoid)
 
         kept = [sb("kept%d" % t, [P, T], F32) for t in range(PACK)]
 
@@ -114,38 +122,48 @@ def tile_picked_wgmem_relu_lo_kernel(tc, x_words, x_scales, mem, w1, w2, slot, o
                 nc.scalar.copy(high[:, :, t], window[t][:, HALF:U])
             nc.scalar.copy(low[:, :, t], window[t][:, 0:HALF])
 
-        look_up(0)
-        w1_0 = deal(nc.vector.tensor_copy, "w1_0", w1_raw, 0, 1)
-        y_acc = project("y0", w1_0[:])
-        w1_rest = deal(nc.scalar.copy, "w1_rest", w1_raw, 1, PACK)
-        gates(2)
-        gates(3)
         last = PACK - 1
-        new = [sb("new%d" % t, [P, T], F32) for t in range(PACK)]
-        fresh0 = sb("fresh0", [P, T], F32)
-
-        def put(t):
-            nc.vector.tensor_copy(window[t][:].indirect(offsets[:]), new[t][:])
-            nc.sync.dma_start(out_rows[t], window[t][:])
-
+        for h in range(2):
+            nc.vector.tensor_tensor(kept[0][:, halves[h]], window[0][:].indirect(offset_halves[h]), stay[0][:, halves[h]], ALU.mult)
         look_up(1)
-        y_acc = y_acc + project("y1", w1_rest[:, 0:1]) + project("y23", w1_rest[:, 1:3])
-        nc.vector.scalar_tensor_tensor(fresh0[:], y_acc[0][:], 0.0, gate[0][:], ALU.max, ALU.mult)
         look_up(2)
-        nc.vector.tensor_tensor(new[0][:], kept[0][:], fresh0[:], ALU.add)
+        dealt = dealt_tiles("w1")
+        deal(nc.vector.tensor_copy, dealt[0], w1_raw, 0, 0)
         look_up(3)
-        put(0)
-        cand = [None]
+        deal(nc.scalar.copy, dealt[1], w1_raw, 0, 1)
+        deal(nc.scalar.copy, dealt[2], w1_raw, 0, 2)
+        deal(nc.vector.tensor_copy, dealt[0], w1_raw, 1, 0)
+        deal(nc.vector.tensor_copy, dealt[1], w1_raw, 1, 1)
+        deal(nc.scalar.copy, dealt[2], w1_raw, 1, 2)
         for t in range(1, PACK):
-            cand.append(sb("cand%d" % t, [P, T], F32))
-            nc.scalar.activation(cand[t][:], y_acc[t][:], ACT.Relu)
+            nc.scalar.activation(gate[t][:], u_acc[t][:], ACT.Sigmoid)
+        first = quantise("y0", dealt[0])[0]
+        y_first = [multiply(first, 5 + h, halves[h].start, halves[h].stop) for h in range(2)]
+        y_acc = [None, multiply(quantise("y1", dealt[1])[0], 7, 0, T)]
+        rest = quantise("y2", dealt[2])
+        y_acc.append(multiply(rest[0], 0, 0, T))
+        y_acc.append(multiply(rest[1], 1, 0, T))
+
+        fresh0 = sb("fresh0", [P, T], F32)
+        for h in range(2):
+            nc.vector.scalar_tensor_tensor(fresh0[:, halves[h]], y_first[h][:], 0.0, gate[0][:, halves[h]], ALU.max, ALU.mult)
+        new0 = sb("new0", [P, T], F32, tag="w1_23")
+        nc.vector.tensor_tensor(new0[:], kept[0][:], fresh0[:], ALU.add)
+        nc.vector.tensor_copy(window[0][:].indirect(offsets[:]), new0[:])
+        nc.sync.dma_start(out_rows[0], window[0][:])
+
+        new = [None]
         for t in range(1, PACK):
-            fresh = sb("fresh%d" % t, [P, T], F32, tag="stay%d" % last)
-            nc.gpsimd.tensor_tensor(fresh[:], cand[t][:], gate[t][:], ALU.mult)
+            cand = sb("cand%d" % t, [P, T], F32)
+            nc.scalar.activation(cand[:], y_acc[t][:], ACT.Relu)
+            fresh = sb("fresh%d" % t, [P, T], F32, tag="kept0")
+            new.append(sb("new%d" % t, [P, T], F32))
+            nc.gpsimd.tensor_tensor(fresh[:], cand[:], gate[t][:], ALU.mult)
             nc.gpsimd.tensor_tensor(new[t][:], kept[t][:], fresh[:], ALU.add)
         for t in range(1, PACK):
             regroup(t - 1)
-            put(t)
+            nc.vector.tensor_copy(window[t][:].indirect(offsets[:]), new[t][:])
+            nc.sync.dma_start(out_rows[t], window[t][:])
 
         out_plane = sb("out_plane", [P, U], U8)
         out_words = out_1[0].rearrange("p c r -> p (c r)").bitcast(I32)

@@ -17,8 +17,12 @@ ACT = mybir.ActivationFunctionType
 
 P = 128
 PACK = 4
-HALF = U // 2
-QUARTER = U // 4
+LAST = PACK - 1
+QUADRANTS = 4
+ENTRIES_PER_COLUMN = 16
+HALF_T = T // 2
+HALF_U = U // 2
+QUARTER_U = U // 4
 
 
 def tile_picked_wgmem_relu_lo_kernel(tc, x_words, x_scales, mem, w1, w2, slot, out_0, out_1, out_2):
@@ -27,39 +31,42 @@ def tile_picked_wgmem_relu_lo_kernel(tc, x_words, x_scales, mem, w1, w2, slot, o
         keep = ctx.enter_context(tc.tile_pool(name="keep", bufs=1))
         psum = ctx.enter_context(tc.psum_pool(name="psum", bufs=1))
 
-        def sb(name, shape, dtype, tag=None):
-            return keep.tile(shape, dtype, name=name, tag=tag or name, align_bytes=64)
+        def sb(name, shape, dtype, reuses=None):
+            return keep.tile(shape, dtype, name=name, tag=reuses or name, align_bytes=64)
 
-        offsets = keep.tile([P, T // 16], U16, name="offsets")
+        offsets = keep.tile([P, T // ENTRIES_PER_COLUMN], U16, name="offsets")
         x_codes = sb("x_codes", [P, T], U32)
-        x_plane = sb("x_plane", [P, T], U8)
+        x_scale_tile = sb("x_scale_tile", [P, T], U8)
         w1_raw = [sb("w1_raw%d" % h, [P, 2, N], F32) for h in range(2)]
         w2_raw = [sb("w2_raw%d" % h, [P, 2, N], F32) for h in range(2)]
         window = [sb("window%d" % t, [P, U], F32) for t in range(PACK)]
         mem_rows = mem.rearrange("(p t) u -> t p u", t=PACK)
         out_rows = out_0.rearrange("(p t) u -> t p u", t=PACK)
 
-        warm = sb("warm", [P, 8], F32)
-        nc.vector.memset(x_plane[:].bitcast(I32), 0)
-        nc.vector.memset(warm[:], 0.0)
-        nc.scalar.activation(warm[:, 0:1], warm[:, 1:2], ACT.Sigmoid)
-
         def load_weight(raw, w, h):
             nc.sync.dma_start(raw[h][:], w.rearrange("(p j) n -> p j n", j=PACK)[:, 2 * h : 2 * h + 2, :])
 
+        nc.vector.memset(x_scale_tile[:].bitcast(I32), 0)
         nc.sync.dma_start(offsets[:], slot)
         load_weight(w2_raw, w2, 0)
-        for q in range(4):
+        for q in range(QUADRANTS):
             nc.sync.dma_start(
-                x_plane[32 * q : 32 * q + 4, :].bitcast(I32), x_scales[0, 4 * q : 4 * q + 4, :].bitcast(I32)
+                x_scale_tile[32 * q : 32 * q + 4, :].bitcast(I32), x_scales[0, 4 * q : 4 * q + 4, :].bitcast(I32)
             )
         load_weight(w2_raw, w2, 1)
         nc.sync.dma_start(x_codes[:].bitcast(I32), x_words[0].rearrange("p n r -> p (n r)").bitcast(I32))
-        for t in range(PACK - 1):
+        for t in range(LAST):
             nc.sync.dma_start(window[t][:], mem_rows[t])
         load_weight(w1_raw, w1, 0)
-        nc.sync.dma_start(window[PACK - 1][:], mem_rows[PACK - 1])
+        nc.sync.dma_start(window[LAST][:], mem_rows[LAST])
         load_weight(w1_raw, w1, 1)
+
+        def dealt_tiles(name):
+            return [
+                sb(name + "_group0", [P, 1, P, PACK], BF16),
+                sb(name + "_group1", [P, 1, P, PACK], BF16),
+                sb(name + "_groups23", [P, 2, P, PACK], BF16),
+            ]
 
         def deal(engine_copy, dealt, raw, h, t0):
             engine_copy(
@@ -68,117 +75,146 @@ def tile_picked_wgmem_relu_lo_kernel(tc, x_words, x_scales, mem, w1, w2, slot, o
             )
 
         def quantise(name, dealt):
-            count = dealt.shape[1]
-            codes = sb(name + "_codes", [P, count * P], U32)
-            plane = sb(name + "_plane", [P, count * P], U8)
-            nc.vector.quantize_mx(out=codes[:].bitcast(FP8X4), scales=plane[:], in_=dealt[:].rearrange("p t m j -> p (t m j)"))
-            return [(codes[:, i * P : (i + 1) * P], plane[:, i * P : (i + 1) * P]) for i in range(count)]
+            groups = dealt.shape[1]
+            codes = sb(name + "_codes", [P, groups * P], U32)
+            scales = sb(name + "_scales", [P, groups * P], U8)
+            nc.vector.quantize_mx(
+                out=codes[:].bitcast(FP8X4), scales=scales[:], in_=dealt[:].rearrange("p t m j -> p (t m j)")
+            )
+            return [(codes[:, i * P : (i + 1) * P], scales[:, i * P : (i + 1) * P]) for i in range(groups)]
 
-        def multiply(operand, bank, c0, c1):
-            acc = psum.tile([P, c1 - c0], F32, name="acc", tag="bank%d" % bank)
+        def multiply(weights, bank, messages):
+            acc = psum.tile([P, messages.stop - messages.start], F32, name="acc", tag="bank%d" % bank)
             nc.tensor.matmul_mx(
-                out=acc[:], lhsT=operand[0].bitcast(FP8X4), lhsT_scale=operand[1],
-                rhs=x_codes[:, c0:c1].bitcast(FP8X4), rhs_scale=x_plane[:, c0:c1], start=True, stop=True,
+                out=acc[:],
+                lhsT=weights[0].bitcast(FP8X4),
+                lhsT_scale=weights[1],
+                rhs=x_codes[:, messages].bitcast(FP8X4),
+                rhs_scale=x_scale_tile[:, messages],
+                start=True,
+                stop=True,
             )
             return acc
 
-        def dealt_tiles(name):
-            return [sb(name + "_0", [P, 1, P, PACK], BF16), sb(name + "_1", [P, 1, P, PACK], BF16), sb(name + "_23", [P, 2, P, PACK], BF16)]
+        everything = slice(0, T)
+        halves = [slice(h * HALF_T, (h + 1) * HALF_T) for h in range(2)]
+        offset_halves = [
+            offsets[:, half.start // ENTRIES_PER_COLUMN : half.stop // ENTRIES_PER_COLUMN] for half in halves
+        ]
 
-        gate = [sb("gate%d" % t, [P, T], F32) for t in range(PACK)]
+        w2_dealt = dealt_tiles("w2")
+        for i in range(len(w2_dealt)):
+            deal(nc.vector.tensor_copy, w2_dealt[i], w2_raw, 0, i)
+        for i in range(2):
+            deal(nc.vector.tensor_copy, w2_dealt[i], w2_raw, 1, i)
+        u_weights = quantise("u0", w2_dealt[0])
+        u0_halves = [multiply(u_weights[0], h, halves[h]) for h in range(2)]
+        u_weights = u_weights + quantise("u1", w2_dealt[1])
+        for t in range(2, PACK):
+            deal(nc.vector.tensor_copy, w2_dealt[2][:, t - 2 : t - 1], w2_raw, 1, t)
+        u_weights = u_weights + quantise("u23", w2_dealt[2])
+        u_acc = {t: multiply(u_weights[t], t + 1, everything) for t in range(1, PACK)}
         stay = [sb("stay%d" % t, [P, T], F32) for t in range(PACK)]
-
-        dealt = dealt_tiles("w2")
+        gate = [sb("gate%d" % t, [P, T], F32) for t in range(2)]
         for h in range(2):
-            deal(nc.vector.tensor_copy, dealt[0], w2_raw, h, 0)
-            deal(nc.vector.tensor_copy, dealt[1], w2_raw, h, 1)
-            deal(nc.scalar.copy, dealt[2], w2_raw, h, 2)
-        halves = [slice(h * (T // 2), (h + 1) * (T // 2)) for h in range(2)]
-        offset_halves = [offsets[:, h * (T // 32) : (h + 1) * (T // 32)] for h in range(2)]
-        first = quantise("u0", dealt[0])[0]
-        u_first = [multiply(first, h, halves[h].start, halves[h].stop) for h in range(2)]
-        u_acc = [None]
-        for operand in quantise("u1", dealt[1]) + quantise("u2", dealt[2]):
-            u_acc.append(multiply(operand, len(u_acc) + 1, 0, T))
-        for h in range(2):
-            nc.scalar.activation(stay[0][:, halves[h]], u_first[h][:], ACT.Sigmoid, scale=-1.0)
+            nc.scalar.activation(stay[0][:, halves[h]], u0_halves[h][:], ACT.Sigmoid, scale=-1.0)
         for t in range(1, PACK):
             nc.scalar.activation(stay[t][:], u_acc[t][:], ACT.Sigmoid, scale=-1.0)
         for h in range(2):
-            nc.scalar.activation(gate[0][:, halves[h]], u_first[h][:], ACT.Sigmoid)
+            nc.scalar.activation(gate[0][:, halves[h]], u0_halves[h][:], ACT.Sigmoid)
 
         kept = [sb("kept%d" % t, [P, T], F32) for t in range(PACK)]
-
-        def look_up(t):
+        for h in range(2):
+            nc.vector.tensor_tensor(
+                kept[0][:, halves[h]], window[0][:].indirect(offset_halves[h]), stay[0][:, halves[h]], ALU.mult
+            )
+        for t in range(1, PACK):
             nc.vector.tensor_tensor(kept[t][:], window[t][:].indirect(offsets[:]), stay[t][:], ALU.mult)
 
-        low = sb("low", [P, HALF, PACK], BF16)
-        high = sb("high", [P, HALF, PACK], BF16)
-
-        def regroup(t):
-            if t == PACK - 2:
-                nc.scalar.copy(high[:, :, t : t + 2], window[t][:, HALF:U].unsqueeze(2).to_broadcast([P, HALF, 2]))
-            else:
-                nc.scalar.copy(high[:, :, t], window[t][:, HALF:U])
-            nc.scalar.copy(low[:, :, t], window[t][:, 0:HALF])
-
-        last = PACK - 1
-        for h in range(2):
-            nc.vector.tensor_tensor(kept[0][:, halves[h]], window[0][:].indirect(offset_halves[h]), stay[0][:, halves[h]], ALU.mult)
-        look_up(1)
-        look_up(2)
-        dealt = dealt_tiles("w1")
-        deal(nc.vector.tensor_copy, dealt[0], w1_raw, 0, 0)
-        look_up(3)
-        deal(nc.scalar.copy, dealt[1], w1_raw, 0, 1)
-        deal(nc.scalar.copy, dealt[2], w1_raw, 0, 2)
-        deal(nc.vector.tensor_copy, dealt[0], w1_raw, 1, 0)
-        deal(nc.vector.tensor_copy, dealt[1], w1_raw, 1, 1)
-        deal(nc.scalar.copy, dealt[2], w1_raw, 1, 2)
-        for t in range(1, PACK):
+        w1_dealt = dealt_tiles("w1")
+        for i in range(len(w1_dealt)):
+            deal(nc.scalar.copy, w1_dealt[i], w1_raw, 0, i)
+        deal(nc.vector.tensor_copy, w1_dealt[0], w1_raw, 1, 0)
+        deal(nc.vector.tensor_copy, w1_dealt[1], w1_raw, 1, 1)
+        deal(nc.scalar.copy, w1_dealt[2], w1_raw, 1, 2)
+        nc.scalar.activation(gate[1][:], u_acc[1][:], ACT.Sigmoid)
+        y0_weights = quantise("y0", w1_dealt[0])[0]
+        y0_halves = [multiply(y0_weights, 5 + h, halves[h]) for h in range(2)]
+        y_acc = {1: multiply(quantise("y1", w1_dealt[1])[0], 7, everything)}
+        gate.append(sb("gate2", [P, T], F32, reuses="w1_raw1"))
+        gate.append(sb("gate3", [P, T], F32, reuses="w1_group1"))
+        for t in range(2, PACK):
             nc.scalar.activation(gate[t][:], u_acc[t][:], ACT.Sigmoid)
-        first = quantise("y0", dealt[0])[0]
-        y_first = [multiply(first, 5 + h, halves[h].start, halves[h].stop) for h in range(2)]
-        y_acc = [None, multiply(quantise("y1", dealt[1])[0], 7, 0, T)]
-        rest = quantise("y2", dealt[2])
-        y_acc.append(multiply(rest[0], 0, 0, T))
-        y_acc.append(multiply(rest[1], 1, 0, T))
+        y23_weights = quantise("y23", w1_dealt[2])
+        for t in range(2, PACK):
+            y_acc[t] = multiply(y23_weights[t - 2], t - 2, everything)
 
         fresh0 = sb("fresh0", [P, T], F32)
         for h in range(2):
-            nc.vector.scalar_tensor_tensor(fresh0[:, halves[h]], y_first[h][:], 0.0, gate[0][:, halves[h]], ALU.max, ALU.mult)
-        new0 = sb("new0", [P, T], F32, tag="w1_23")
+            nc.vector.scalar_tensor_tensor(
+                fresh0[:, halves[h]], y0_halves[h][:], 0.0, gate[0][:, halves[h]], ALU.max, ALU.mult
+            )
+        new0 = sb("new0", [P, T], F32, reuses="w1_groups23")
         nc.vector.tensor_tensor(new0[:], kept[0][:], fresh0[:], ALU.add)
         nc.vector.tensor_copy(window[0][:].indirect(offsets[:]), new0[:])
         nc.sync.dma_start(out_rows[0], window[0][:])
 
-        new = [None]
+        candidate = {t: sb("candidate%d" % t, [P, T], F32) for t in range(1, PACK)}
         for t in range(1, PACK):
-            cand = sb("cand%d" % t, [P, T], F32)
-            nc.scalar.activation(cand[:], y_acc[t][:], ACT.Relu)
-            fresh = sb("fresh%d" % t, [P, T], F32, tag="kept0")
-            new.append(sb("new%d" % t, [P, T], F32))
-            nc.gpsimd.tensor_tensor(fresh[:], cand[:], gate[t][:], ALU.mult)
-            nc.gpsimd.tensor_tensor(new[t][:], kept[t][:], fresh[:], ALU.add)
-        for t in range(1, PACK):
+            nc.scalar.activation(candidate[t][:], y_acc[t][:], ACT.Relu)
+        fresh1 = sb("fresh1", [P, T], F32, reuses="kept0")
+        new1 = sb("new1", [P, T], F32)
+        nc.gpsimd.tensor_tensor(fresh1[:], candidate[1][:], gate[1][:], ALU.mult)
+        nc.gpsimd.tensor_tensor(new1[:], kept[1][:], fresh1[:], ALU.add)
+        fresh = {2: sb("fresh2", [P, T], F32, reuses="kept0"), 3: sb("fresh3", [P, T], F32, reuses="kept1")}
+        for t in range(2, PACK):
+            nc.gpsimd.tensor_tensor(fresh[t][:], candidate[t][:], gate[t][:], ALU.mult)
+
+        low = sb("low", [P, HALF_U, PACK], BF16)
+        high = sb("high", [P, HALF_U, PACK], BF16)
+
+        def regroup(t):
+            if t == LAST - 1:
+                nc.scalar.copy(
+                    high[:, :, t : t + 2], window[t][:, HALF_U:U].unsqueeze(2).to_broadcast([P, HALF_U, 2])
+                )
+            else:
+                nc.scalar.copy(high[:, :, t], window[t][:, HALF_U:U])
+            nc.scalar.copy(low[:, :, t], window[t][:, 0:HALF_U])
+
+        regroup(0)
+        nc.vector.tensor_copy(window[1][:].indirect(offsets[:]), new1[:])
+        nc.sync.dma_start(out_rows[1], window[1][:])
+        for t in range(2, PACK):
             regroup(t - 1)
-            nc.vector.tensor_copy(window[t][:].indirect(offsets[:]), new[t][:])
+            nc.vector.tensor_tensor(window[t][:].indirect(offsets[:]), kept[t][:], fresh[t][:], ALU.add)
             nc.sync.dma_start(out_rows[t], window[t][:])
 
-        out_plane = sb("out_plane", [P, U], U8)
+        out_scale_tile = sb("out_scale_tile", [P, U], U8)
         out_words = out_1[0].rearrange("p c r -> p (c r)").bitcast(I32)
+        quarters = [slice(i * QUARTER_U, (i + 1) * QUARTER_U) for i in range(2)]
 
-        def pack(name, source, c0, width):
-            codes = sb(name, [P, width], U32)
-            nc.vector.quantize_mx(out=codes[:].bitcast(FP8X4), scales=out_plane[:, c0 : c0 + width], in_=source.rearrange("p c t -> p (c t)"))
-            nc.sync.dma_start(out_words[:, c0 : c0 + width], codes[:].bitcast(I32))
+        def pack(rounded, first_slot, quarter):
+            slots = slice(first_slot + quarter.start, first_slot + quarter.stop)
+            codes = sb("out_codes%d" % slots.start, [P, QUARTER_U], U32)
+            nc.vector.quantize_mx(
+                out=codes[:].bitcast(FP8X4),
+                scales=out_scale_tile[:, slots],
+                in_=rounded[:, quarter, :].rearrange("p c t -> p (c t)"),
+            )
+            nc.sync.dma_start(out_words[:, slots], codes[:].bitcast(I32))
 
-        nc.scalar.copy(low[:, 0:QUARTER, last], window[last][:, 0:QUARTER])
-        nc.scalar.copy(low[:, QUARTER:HALF, last], window[last][:, QUARTER:HALF])
-        nc.vector.tensor_copy(high[:, :, last], window[last][:, HALF:U])
-        pack("codes0", low[:, 0:QUARTER], 0, QUARTER)
-        pack("codes2", high[:], HALF, HALF)
-        pack("codes1", low[:, QUARTER:HALF], QUARTER, QUARTER)
-        for q in range(4):
+        for quarter in quarters:
+            nc.scalar.copy(low[:, quarter, LAST], window[LAST][:, quarter])
+        for quarter in quarters:
+            nc.vector.tensor_copy(
+                high[:, quarter, LAST], window[LAST][:, HALF_U + quarter.start : HALF_U + quarter.stop]
+            )
+        for quarter in quarters:
+            pack(high, HALF_U, quarter)
+            pack(low, 0, quarter)
+        for q in range(QUADRANTS):
             queue = nc.scalar if q % 2 else nc.sync
-            queue.dma_start(out_2[0, 4 * q : 4 * q + 4, :].bitcast(I32), out_plane[32 * q : 32 * q + 4, :].bitcast(I32))
+            queue.dma_start(
+                out_2[0, 4 * q : 4 * q + 4, :].bitcast(I32), out_scale_tile[32 * q : 32 * q + 4, :].bitcast(I32)
+            )

@@ -22,6 +22,7 @@ QUADRANTS = 4
 ENTRIES_PER_COLUMN = 16
 HALF_T = T // 2
 HALF_U = U // 2
+SPLIT_M = 96
 QUARTER_U = U // 4
 
 
@@ -37,16 +38,18 @@ def tile_picked_wgmem_relu_lo_kernel(tc, x_words, x_scales, mem, w1, w2, slot, o
         offsets = keep.tile([P, T // ENTRIES_PER_COLUMN], U16, name="offsets")
         x_codes = sb("x_codes", [P, T], U32)
         x_scale_tile = sb("x_scale_tile", [P, T], U8)
-        w1_raw = [sb("w1_raw%d" % h, [P, 2, N], F32) for h in range(2)]
+        w1_whole = sb("w1_raw1", [P, PACK, N], F32)
+        w1_raw = [w1_whole[:, 2 * h : 2 * h + 2, :] for h in range(2)]
         w2_raw = [sb("w2_raw%d" % h, [P, 2, N], F32) for h in range(2)]
         window = [sb("window%d" % t, [P, U], F32) for t in range(PACK)]
         mem_rows = mem.rearrange("(p t) u -> t p u", t=PACK)
         out_rows = out_0.rearrange("(p t) u -> t p u", t=PACK)
 
         def load_weight(raw, w, h):
-            nc.sync.dma_start(raw[h][:], w.rearrange("(p j) n -> p j n", j=PACK)[:, 2 * h : 2 * h + 2, :])
+            nc.sync.dma_start(raw[h][:, :, :], w.rearrange("(p j) n -> p j n", j=PACK)[:, 2 * h : 2 * h + 2, :])
 
         nc.vector.memset(x_scale_tile[:].bitcast(I32), 0)
+        nc.sync.dma_start(window[LAST][:], mem_rows[LAST])
         nc.sync.dma_start(offsets[:], slot)
         load_weight(w2_raw, w2, 0)
         for q in range(QUADRANTS):
@@ -58,7 +61,6 @@ def tile_picked_wgmem_relu_lo_kernel(tc, x_words, x_scales, mem, w1, w2, slot, o
         for t in range(LAST):
             nc.sync.dma_start(window[t][:], mem_rows[t])
         load_weight(w1_raw, w1, 0)
-        nc.sync.dma_start(window[LAST][:], mem_rows[LAST])
         load_weight(w1_raw, w1, 1)
 
         def dealt_tiles(name):
@@ -68,18 +70,18 @@ def tile_picked_wgmem_relu_lo_kernel(tc, x_words, x_scales, mem, w1, w2, slot, o
                 sb(name + "_groups23", [P, 2, P, PACK], BF16),
             ]
 
-        def deal(engine_copy, dealt, raw, h, t0):
+        def deal(engine_copy, dealt, raw, h, t0, columns=slice(0, P)):
             engine_copy(
-                dealt[:, :, :, 2 * h : 2 * h + 2].rearrange("p t m j -> p m t j"),
-                raw[h][:].rearrange("p j (m t) -> p m t j", t=PACK)[:, :, t0 : t0 + dealt.shape[1], :],
+                dealt[:, :, columns, 2 * h : 2 * h + 2].rearrange("p t m j -> p m t j"),
+                raw[h][:, :, :].rearrange("p j (m t) -> p m t j", t=PACK)[:, columns, t0 : t0 + dealt.shape[1], :],
             )
 
-        def quantise(name, dealt):
+        def quantise(name, dealt, after=None):
             groups = dealt.shape[1]
-            codes = sb(name + "_codes", [P, groups * P], U32)
+            codes = sb(name + "_codes", [P, groups * P], U32, reuses=after)
             scales = sb(name + "_scales", [P, groups * P], U8)
             nc.vector.quantize_mx(
-                out=codes[:].bitcast(FP8X4), scales=scales[:], in_=dealt[:].rearrange("p t m j -> p (t m j)")
+                out=codes[:].bitcast(FP8X4), scales=scales[:], in_=dealt[:, :, :, :].rearrange("p t m j -> p (t m j)")
             )
             return [(codes[:, i * P : (i + 1) * P], scales[:, i * P : (i + 1) * P]) for i in range(groups)]
 
@@ -102,73 +104,85 @@ def tile_picked_wgmem_relu_lo_kernel(tc, x_words, x_scales, mem, w1, w2, slot, o
             offsets[:, half.start // ENTRIES_PER_COLUMN : half.stop // ENTRIES_PER_COLUMN] for half in halves
         ]
 
+        old3 = sb("old3", [P, T], F32)
+        nc.vector.tensor_copy(old3[:], window[LAST][:].indirect(offsets[:]))
+        warm = sb("warm", [P, 2], F32)
+        nc.gpsimd.memset(warm[:, 0:1], 0.0)
+        nc.scalar.activation(warm[:, 1:2], warm[:, 0:1], ACT.Sigmoid)
         w2_dealt = dealt_tiles("w2")
-        for i in range(len(w2_dealt)):
-            deal(nc.vector.tensor_copy, w2_dealt[i], w2_raw, 0, i)
-        for i in range(2):
-            deal(nc.vector.tensor_copy, w2_dealt[i], w2_raw, 1, i)
+        for h in range(2):
+            for i in range(2):
+                deal(nc.vector.tensor_copy, w2_dealt[i], w2_raw, h, i)
+            deal(nc.scalar.copy, w2_dealt[2], w2_raw, h, 2)
         u_weights = quantise("u0", w2_dealt[0])
         u0_halves = [multiply(u_weights[0], h, halves[h]) for h in range(2)]
         u_weights = u_weights + quantise("u1", w2_dealt[1])
-        for t in range(2, PACK):
-            deal(nc.vector.tensor_copy, w2_dealt[2][:, t - 2 : t - 1], w2_raw, 1, t)
         u_weights = u_weights + quantise("u23", w2_dealt[2])
         u_acc = {t: multiply(u_weights[t], t + 1, everything) for t in range(1, PACK)}
-        stay = [sb("stay%d" % t, [P, T], F32) for t in range(PACK)]
-        gate = [sb("gate%d" % t, [P, T], F32) for t in range(2)]
+        stay = [sb("stay%d" % t, [P, T], F32) for t in range(LAST)]
+        gate0 = [sb("gate0_%d" % h, [P, HALF_T], F32) for h in range(2)]
         for h in range(2):
             nc.scalar.activation(stay[0][:, halves[h]], u0_halves[h][:], ACT.Sigmoid, scale=-1.0)
-        for t in range(1, PACK):
+        for t in range(1, LAST):
             nc.scalar.activation(stay[t][:], u_acc[t][:], ACT.Sigmoid, scale=-1.0)
         for h in range(2):
-            nc.scalar.activation(gate[0][:, halves[h]], u0_halves[h][:], ACT.Sigmoid)
+            nc.scalar.activation(gate0[h][:], u0_halves[h][:], ACT.Sigmoid)
 
-        kept = [sb("kept%d" % t, [P, T], F32) for t in range(PACK)]
+        kept = [sb("kept%d" % t, [P, T], F32) for t in range(LAST)]
         for h in range(2):
             nc.vector.tensor_tensor(
                 kept[0][:, halves[h]], window[0][:].indirect(offset_halves[h]), stay[0][:, halves[h]], ALU.mult
             )
-        for t in range(1, PACK):
+        for t in range(1, LAST):
             nc.vector.tensor_tensor(kept[t][:], window[t][:].indirect(offsets[:]), stay[t][:], ALU.mult)
 
-        w1_dealt = dealt_tiles("w1")
-        for i in range(len(w1_dealt)):
-            deal(nc.scalar.copy, w1_dealt[i], w1_raw, 0, i)
-        deal(nc.vector.tensor_copy, w1_dealt[0], w1_raw, 1, 0)
-        deal(nc.vector.tensor_copy, w1_dealt[1], w1_raw, 1, 1)
-        deal(nc.scalar.copy, w1_dealt[2], w1_raw, 1, 2)
-        nc.scalar.activation(gate[1][:], u_acc[1][:], ACT.Sigmoid)
+        w1_all = sb("w1_groups23", [P, PACK, P, PACK], BF16)
+        w1_dealt = [w1_all[:, 0:1], w1_all[:, 1:2], w1_all[:, 2:4]]
+        gate = {1: sb("gate1", [P, T], F32)[:]}
+        nc.scalar.activation(gate[1], u_acc[1][:], ACT.Sigmoid)
+        deal(nc.scalar.copy, w1_all[:, 0:2], w1_raw, 0, 0)
+        deal(nc.vector.tensor_copy, w1_dealt[0], w1_raw, 1, 0, slice(0, SPLIT_M))
+        deal(nc.scalar.copy, w1_dealt[0], w1_raw, 1, 0, slice(SPLIT_M, P))
+        deal(nc.scalar.copy, w1_dealt[1], w1_raw, 1, 1)
+        nc.scalar.copy(
+            w1_dealt[2].rearrange("p t m j -> p m t j"),
+            w1_whole[:].rearrange("p j (m t) -> p m t j", t=PACK)[:, :, 2:4, :],
+        )
         y0_weights = quantise("y0", w1_dealt[0])[0]
         y0_halves = [multiply(y0_weights, 5 + h, halves[h]) for h in range(2)]
         y_acc = {1: multiply(quantise("y1", w1_dealt[1])[0], 7, everything)}
-        gate.append(sb("gate2", [P, T], F32, reuses="w1_raw1"))
-        gate.append(sb("gate3", [P, T], F32, reuses="w1_group1"))
-        for t in range(2, PACK):
-            nc.scalar.activation(gate[t][:], u_acc[t][:], ACT.Sigmoid)
-        y23_weights = quantise("y23", w1_dealt[2])
-        for t in range(2, PACK):
-            y_acc[t] = multiply(y23_weights[t - 2], t - 2, everything)
-
         fresh0 = sb("fresh0", [P, T], F32)
         for h in range(2):
             nc.vector.scalar_tensor_tensor(
-                fresh0[:, halves[h]], y0_halves[h][:], 0.0, gate[0][:, halves[h]], ALU.max, ALU.mult
+                fresh0[:, halves[h]], y0_halves[h][:], 0.0, gate0[h][:], ALU.max, ALU.mult
             )
-        new0 = sb("new0", [P, T], F32, reuses="w1_groups23")
-        nc.vector.tensor_tensor(new0[:], kept[0][:], fresh0[:], ALU.add)
+        new0 = sb("new0", [P, T], F32)
+        for h in range(2):
+            nc.vector.tensor_tensor(new0[:, halves[h]], kept[0][:, halves[h]], fresh0[:, halves[h]], ALU.add)
+        y23_weights = quantise("y23", w1_dealt[2], after="gate0_0")
+        for t in range(2, PACK):
+            y_acc[t] = multiply(y23_weights[t - 2], t - 2, everything)
         nc.vector.tensor_copy(window[0][:].indirect(offsets[:]), new0[:])
         nc.sync.dma_start(out_rows[0], window[0][:])
 
+        late_gates = sb("late_gates", [P, 2, T], F32, reuses="w1_raw1")
+        for t in range(2, PACK):
+            gate[t] = late_gates[:, t - 2, :]
         candidate = {t: sb("candidate%d" % t, [P, T], F32) for t in range(1, PACK)}
         for t in range(1, PACK):
+            if t > 1:
+                nc.scalar.activation(gate[t], u_acc[t][:], ACT.Sigmoid)
             nc.scalar.activation(candidate[t][:], y_acc[t][:], ACT.Relu)
-        fresh1 = sb("fresh1", [P, T], F32, reuses="kept0")
-        new1 = sb("new1", [P, T], F32)
-        nc.gpsimd.tensor_tensor(fresh1[:], candidate[1][:], gate[1][:], ALU.mult)
-        nc.gpsimd.tensor_tensor(new1[:], kept[1][:], fresh1[:], ALU.add)
-        fresh = {2: sb("fresh2", [P, T], F32, reuses="kept0"), 3: sb("fresh3", [P, T], F32, reuses="kept1")}
-        for t in range(2, PACK):
-            nc.gpsimd.tensor_tensor(fresh[t][:], candidate[t][:], gate[t][:], ALU.mult)
+        new = {}
+        for t in range(1, LAST):
+            fresh = sb("fresh%d" % t, [P, T], F32, reuses={1: "w1_groups23", 2: "kept1"}[t])
+            new[t] = sb("new%d" % t, [P, T], F32)
+            nc.gpsimd.tensor_tensor(fresh[:], candidate[t][:], gate[t], ALU.mult)
+            nc.gpsimd.tensor_tensor(new[t][:], kept[t][:], fresh[:], ALU.add)
+        gap3 = sb("gap3", [P, T], F32, reuses="kept2")
+        step3 = sb("step3", [P, T], F32)
+        nc.gpsimd.tensor_tensor(gap3[:], candidate[LAST][:], old3[:], ALU.subtract)
+        nc.gpsimd.tensor_tensor(step3[:], gap3[:], gate[LAST], ALU.mult)
 
         low = sb("low", [P, HALF_U, PACK], BF16)
         high = sb("high", [P, HALF_U, PACK], BF16)
@@ -182,12 +196,12 @@ def tile_picked_wgmem_relu_lo_kernel(tc, x_words, x_scales, mem, w1, w2, slot, o
                 nc.scalar.copy(high[:, :, t], window[t][:, HALF_U:U])
             nc.scalar.copy(low[:, :, t], window[t][:, 0:HALF_U])
 
-        regroup(0)
-        nc.vector.tensor_copy(window[1][:].indirect(offsets[:]), new1[:])
-        nc.sync.dma_start(out_rows[1], window[1][:])
-        for t in range(2, PACK):
+        for t in range(1, PACK):
             regroup(t - 1)
-            nc.vector.tensor_tensor(window[t][:].indirect(offsets[:]), kept[t][:], fresh[t][:], ALU.add)
+            if t < LAST:
+                nc.vector.tensor_copy(window[t][:].indirect(offsets[:]), new[t][:])
+            else:
+                nc.vector.tensor_tensor(window[t][:].indirect(offsets[:]), old3[:], step3[:], ALU.add)
             nc.sync.dma_start(out_rows[t], window[t][:])
 
         out_scale_tile = sb("out_scale_tile", [P, U], U8)

@@ -21,9 +21,9 @@ LAST = PACK - 1
 QUADRANTS = 4
 ENTRIES_PER_COLUMN = 16
 HALF_T = T // 2
-HALF_U = U // 2
 SPLIT_M = 96
 QUARTER_U = U // 4
+EIGHTH_U = U // 8
 
 
 def tile_picked_wgmem_relu_lo_kernel(tc, x_words, x_scales, mem, w1, w2, slot, out_0, out_1, out_2):
@@ -184,17 +184,20 @@ def tile_picked_wgmem_relu_lo_kernel(tc, x_words, x_scales, mem, w1, w2, slot, o
         nc.gpsimd.tensor_tensor(gap3[:], candidate[LAST][:], old3[:], ALU.subtract)
         nc.gpsimd.tensor_tensor(step3[:], gap3[:], gate[LAST], ALU.mult)
 
-        low = sb("low", [P, HALF_U, PACK], BF16)
-        high = sb("high", [P, HALF_U, PACK], BF16)
+        by_vector = sb("by_vector", [P, 2, QUARTER_U, PACK], BF16)
+        by_scalar = sb("by_scalar", [P, 2, QUARTER_U, PACK], BF16)
+
+        def quarters_of(t, parity):
+            return window[t][:].rearrange("p (i h c) -> p i h c", i=2, h=2)[:, :, parity, :]
 
         def regroup(t):
             if t == LAST - 1:
                 nc.scalar.copy(
-                    high[:, :, t : t + 2], window[t][:, HALF_U:U].unsqueeze(2).to_broadcast([P, HALF_U, 2])
+                    by_vector[:, :, :, t : t + 2], quarters_of(t, 0).unsqueeze(3).to_broadcast([P, 2, QUARTER_U, 2])
                 )
             else:
-                nc.scalar.copy(high[:, :, t], window[t][:, HALF_U:U])
-            nc.scalar.copy(low[:, :, t], window[t][:, 0:HALF_U])
+                nc.scalar.copy(by_vector[:, :, :, t], quarters_of(t, 0))
+            nc.scalar.copy(by_scalar[:, :, :, t], quarters_of(t, 1))
 
         for t in range(1, PACK):
             regroup(t - 1)
@@ -205,28 +208,33 @@ def tile_picked_wgmem_relu_lo_kernel(tc, x_words, x_scales, mem, w1, w2, slot, o
             nc.sync.dma_start(out_rows[t], window[t][:])
 
         out_scale_tile = sb("out_scale_tile", [P, U], U8)
+        out_codes = sb("out_codes", [P, U], U32)
         out_words = out_1[0].rearrange("p c r -> p (c r)").bitcast(I32)
-        quarters = [slice(i * QUARTER_U, (i + 1) * QUARTER_U) for i in range(2)]
 
-        def pack(rounded, first_slot, quarter):
-            slots = slice(first_slot + quarter.start, first_slot + quarter.stop)
-            codes = sb("out_codes%d" % slots.start, [P, QUARTER_U], U32)
+        def pack(rounded, first_slot):
+            slots = slice(first_slot, first_slot + rounded.shape[1])
             nc.vector.quantize_mx(
-                out=codes[:].bitcast(FP8X4),
+                out=out_codes[:, slots].bitcast(FP8X4),
                 scales=out_scale_tile[:, slots],
-                in_=rounded[:, quarter, :].rearrange("p c t -> p (c t)"),
+                in_=rounded.rearrange("p c t -> p (c t)"),
             )
-            nc.sync.dma_start(out_words[:, slots], codes[:].bitcast(I32))
 
-        for quarter in quarters:
-            nc.scalar.copy(low[:, quarter, LAST], window[LAST][:, quarter])
-        for quarter in quarters:
-            nc.vector.tensor_copy(
-                high[:, quarter, LAST], window[LAST][:, HALF_U + quarter.start : HALF_U + quarter.stop]
-            )
-        for quarter in quarters:
-            pack(high, HALF_U, quarter)
-            pack(low, 0, quarter)
+        def store_words(start, stop):
+            nc.sync.dma_start(out_words[:, start:stop], out_codes[:, start:stop].bitcast(I32))
+
+        for i in range(2):
+            nc.scalar.copy(by_scalar[:, i, :, LAST], quarters_of(LAST, 1)[:, i, :])
+        for i in range(2):
+            nc.vector.tensor_copy(by_vector[:, i, :, LAST], quarters_of(LAST, 0)[:, i, :])
+        cut = 2 * QUARTER_U + EIGHTH_U
+        pack(by_vector[:, 0], 0)
+        store_words(0, QUARTER_U)
+        pack(by_scalar[:, 0], QUARTER_U)
+        pack(by_vector[:, 1, 0:EIGHTH_U], 2 * QUARTER_U)
+        store_words(QUARTER_U, cut)
+        pack(by_vector[:, 1, EIGHTH_U:QUARTER_U], cut)
+        pack(by_scalar[:, 1], 3 * QUARTER_U)
+        store_words(cut, U)
         for q in range(QUADRANTS):
             queue = nc.scalar if q % 2 else nc.sync
             queue.dma_start(

@@ -18,12 +18,14 @@ ACT = mybir.ActivationFunctionType
 P = 128
 PACK = 4
 LAST = PACK - 1
+EARLY = 2
 QUADRANTS = 4
 ENTRIES_PER_COLUMN = 16
 HALF_T = T // 2
+FILL_T = T // 4
 SPLIT_M = 96
+HALF_U = U // 2
 QUARTER_U = U // 4
-EIGHTH_U = U // 8
 
 
 def tile_picked_wgmem_relu_lo_kernel(tc, x_words, x_scales, mem, w1, w2, slot, out_0, out_1, out_2):
@@ -49,19 +51,20 @@ def tile_picked_wgmem_relu_lo_kernel(tc, x_words, x_scales, mem, w1, w2, slot, o
             nc.sync.dma_start(raw[h][:, :, :], w.rearrange("(p j) n -> p j n", j=PACK)[:, 2 * h : 2 * h + 2, :])
 
         nc.vector.memset(x_scale_tile[:].bitcast(I32), 0)
-        nc.sync.dma_start(window[LAST][:], mem_rows[LAST])
-        nc.sync.dma_start(offsets[:], slot)
         load_weight(w2_raw, w2, 0)
+        nc.sync.dma_start(offsets[:], slot)
         for q in range(QUADRANTS):
             nc.sync.dma_start(
                 x_scale_tile[32 * q : 32 * q + 4, :].bitcast(I32), x_scales[0, 4 * q : 4 * q + 4, :].bitcast(I32)
             )
         load_weight(w2_raw, w2, 1)
         nc.sync.dma_start(x_codes[:].bitcast(I32), x_words[0].rearrange("p n r -> p (n r)").bitcast(I32))
-        for t in range(LAST):
+        for t in range(EARLY):
             nc.sync.dma_start(window[t][:], mem_rows[t])
         load_weight(w1_raw, w1, 0)
         load_weight(w1_raw, w1, 1)
+        for t in range(EARLY, PACK):
+            nc.sync.dma_start(window[t][:], mem_rows[t])
 
         def dealt_tiles(name):
             return [
@@ -104,8 +107,6 @@ def tile_picked_wgmem_relu_lo_kernel(tc, x_words, x_scales, mem, w1, w2, slot, o
             offsets[:, half.start // ENTRIES_PER_COLUMN : half.stop // ENTRIES_PER_COLUMN] for half in halves
         ]
 
-        old3 = sb("old3", [P, T], F32)
-        nc.vector.tensor_copy(old3[:], window[LAST][:].indirect(offsets[:]))
         warm = sb("warm", [P, 2], F32)
         nc.gpsimd.memset(warm[:, 0:1], 0.0)
         nc.scalar.activation(warm[:, 1:2], warm[:, 0:1], ACT.Sigmoid)
@@ -119,21 +120,23 @@ def tile_picked_wgmem_relu_lo_kernel(tc, x_words, x_scales, mem, w1, w2, slot, o
         u_weights = u_weights + quantise("u1", w2_dealt[1])
         u_weights = u_weights + quantise("u23", w2_dealt[2])
         u_acc = {t: multiply(u_weights[t], t + 1, everything) for t in range(1, PACK)}
-        stay = [sb("stay%d" % t, [P, T], F32) for t in range(LAST)]
-        gate0 = [sb("gate0_%d" % h, [P, HALF_T], F32) for h in range(2)]
+        stay = [sb("stay%d" % t, [P, T], F32) for t in range(EARLY)]
+        old = {t: sb("old%d" % t, [P, T], F32) for t in range(EARLY, PACK)}
+        gate0 = [sb("gate0_0", [P, HALF_T], F32)[:], old[EARLY][:, halves[1]]]
+        first_columns = FILL_T // ENTRIES_PER_COLUMN
         for h in range(2):
             nc.scalar.activation(stay[0][:, halves[h]], u0_halves[h][:], ACT.Sigmoid, scale=-1.0)
-        for t in range(1, LAST):
+        for t in range(1, EARLY):
             nc.scalar.activation(stay[t][:], u_acc[t][:], ACT.Sigmoid, scale=-1.0)
         for h in range(2):
-            nc.scalar.activation(gate0[h][:], u0_halves[h][:], ACT.Sigmoid)
+            nc.scalar.activation(gate0[h], u0_halves[h][:], ACT.Sigmoid)
 
-        kept = [sb("kept%d" % t, [P, T], F32) for t in range(LAST)]
+        kept = [sb("kept%d" % t, [P, T], F32) for t in range(EARLY)]
         for h in range(2):
             nc.vector.tensor_tensor(
                 kept[0][:, halves[h]], window[0][:].indirect(offset_halves[h]), stay[0][:, halves[h]], ALU.mult
             )
-        for t in range(1, LAST):
+        for t in range(1, EARLY):
             nc.vector.tensor_tensor(kept[t][:], window[t][:].indirect(offsets[:]), stay[t][:], ALU.mult)
 
         w1_all = sb("w1_groups23", [P, PACK, P, PACK], BF16)
@@ -151,18 +154,21 @@ def tile_picked_wgmem_relu_lo_kernel(tc, x_words, x_scales, mem, w1, w2, slot, o
         y0_weights = quantise("y0", w1_dealt[0])[0]
         y0_halves = [multiply(y0_weights, 5 + h, halves[h]) for h in range(2)]
         y_acc = {1: multiply(quantise("y1", w1_dealt[1])[0], 7, everything)}
+        nc.vector.tensor_copy(old[EARLY][:, 0:FILL_T], window[EARLY][:].indirect(offsets[:, 0:first_columns]))
         fresh0 = sb("fresh0", [P, T], F32)
         for h in range(2):
             nc.vector.scalar_tensor_tensor(
-                fresh0[:, halves[h]], y0_halves[h][:], 0.0, gate0[h][:], ALU.max, ALU.mult
+                fresh0[:, halves[h]], y0_halves[h][:], 0.0, gate0[h], ALU.max, ALU.mult
             )
-        new0 = sb("new0", [P, T], F32)
-        for h in range(2):
-            nc.vector.tensor_tensor(new0[:, halves[h]], kept[0][:, halves[h]], fresh0[:, halves[h]], ALU.add)
         y23_weights = quantise("y23", w1_dealt[2], after="gate0_0")
         for t in range(2, PACK):
             y_acc[t] = multiply(y23_weights[t - 2], t - 2, everything)
-        nc.vector.tensor_copy(window[0][:].indirect(offsets[:]), new0[:])
+        nc.vector.tensor_copy(old[EARLY][:, FILL_T:T], window[EARLY][:].indirect(offsets[:, first_columns:]))
+        nc.vector.tensor_copy(old[LAST][:], window[LAST][:].indirect(offsets[:]))
+        first_sums = sb("first_sums", [P, 2, T], F32, reuses="w1_groups23")
+        new0 = first_sums[:, 0, :]
+        nc.gpsimd.tensor_tensor(new0, kept[0][:], fresh0[:], ALU.add)
+        nc.vector.tensor_copy(window[0][:].indirect(offsets[:]), new0)
         nc.sync.dma_start(out_rows[0], window[0][:])
 
         late_gates = sb("late_gates", [P, 2, T], F32, reuses="w1_raw1")
@@ -173,68 +179,62 @@ def tile_picked_wgmem_relu_lo_kernel(tc, x_words, x_scales, mem, w1, w2, slot, o
             if t > 1:
                 nc.scalar.activation(gate[t], u_acc[t][:], ACT.Sigmoid)
             nc.scalar.activation(candidate[t][:], y_acc[t][:], ACT.Relu)
-        new = {}
-        for t in range(1, LAST):
-            fresh = sb("fresh%d" % t, [P, T], F32, reuses={1: "w1_groups23", 2: "kept1"}[t])
-            new[t] = sb("new%d" % t, [P, T], F32)
-            nc.gpsimd.tensor_tensor(fresh[:], candidate[t][:], gate[t], ALU.mult)
-            nc.gpsimd.tensor_tensor(new[t][:], kept[t][:], fresh[:], ALU.add)
-        gap3 = sb("gap3", [P, T], F32, reuses="kept2")
-        step3 = sb("step3", [P, T], F32)
-        nc.gpsimd.tensor_tensor(gap3[:], candidate[LAST][:], old3[:], ALU.subtract)
-        nc.gpsimd.tensor_tensor(step3[:], gap3[:], gate[LAST], ALU.mult)
+        new = {t: sb("new%d" % t, [P, T], F32) for t in range(1, LAST)}
+        fresh1 = first_sums[:, 1, :]
+        nc.gpsimd.tensor_tensor(fresh1, candidate[1][:], gate[1], ALU.mult)
+        nc.gpsimd.tensor_tensor(new[1][:], kept[1][:], fresh1, ALU.add)
+        step = {}
+        for t in range(EARLY, PACK):
+            gap = sb("gap%d" % t, [P, T], F32, reuses={2: "kept1", 3: "old2"}[t])
+            step[t] = sb("step%d" % t, [P, T], F32)
+            nc.gpsimd.tensor_tensor(gap[:], candidate[t][:], old[t][:], ALU.subtract)
+            nc.gpsimd.tensor_tensor(step[t][:], gap[:], gate[t], ALU.mult)
+            if t < LAST:
+                nc.gpsimd.tensor_tensor(new[t][:], old[t][:], step[t][:], ALU.add)
 
-        by_vector = sb("by_vector", [P, 2, QUARTER_U, PACK], BF16)
-        by_scalar = sb("by_scalar", [P, 2, QUARTER_U, PACK], BF16)
-
-        def quarters_of(t, parity):
-            return window[t][:].rearrange("p (i h c) -> p i h c", i=2, h=2)[:, :, parity, :]
+        low = sb("low", [P, HALF_U, PACK], BF16)
+        high = sb("high", [P, HALF_U, PACK], BF16)
 
         def regroup(t):
             if t == LAST - 1:
                 nc.scalar.copy(
-                    by_vector[:, :, :, t : t + 2], quarters_of(t, 0).unsqueeze(3).to_broadcast([P, 2, QUARTER_U, 2])
+                    high[:, :, t : t + 2], window[t][:, HALF_U:U].unsqueeze(2).to_broadcast([P, HALF_U, 2])
                 )
             else:
-                nc.scalar.copy(by_vector[:, :, :, t], quarters_of(t, 0))
-            nc.scalar.copy(by_scalar[:, :, :, t], quarters_of(t, 1))
+                nc.scalar.copy(high[:, :, t], window[t][:, HALF_U:U])
+            nc.scalar.copy(low[:, :, t], window[t][:, 0:HALF_U])
 
         for t in range(1, PACK):
             regroup(t - 1)
             if t < LAST:
                 nc.vector.tensor_copy(window[t][:].indirect(offsets[:]), new[t][:])
             else:
-                nc.vector.tensor_tensor(window[t][:].indirect(offsets[:]), old3[:], step3[:], ALU.add)
+                nc.vector.tensor_tensor(window[t][:].indirect(offsets[:]), old[t][:], step[t][:], ALU.add)
             nc.sync.dma_start(out_rows[t], window[t][:])
 
         out_scale_tile = sb("out_scale_tile", [P, U], U8)
-        out_codes = sb("out_codes", [P, U], U32)
         out_words = out_1[0].rearrange("p c r -> p (c r)").bitcast(I32)
+        quarters = [slice(i * QUARTER_U, (i + 1) * QUARTER_U) for i in range(2)]
 
-        def pack(rounded, first_slot):
-            slots = slice(first_slot, first_slot + rounded.shape[1])
+        def pack(rounded, first_slot, quarter):
+            slots = slice(first_slot + quarter.start, first_slot + quarter.stop)
+            codes = sb("out_codes%d" % slots.start, [P, QUARTER_U], U32)
             nc.vector.quantize_mx(
-                out=out_codes[:, slots].bitcast(FP8X4),
+                out=codes[:].bitcast(FP8X4),
                 scales=out_scale_tile[:, slots],
-                in_=rounded.rearrange("p c t -> p (c t)"),
+                in_=rounded[:, quarter, :].rearrange("p c t -> p (c t)"),
             )
+            nc.sync.dma_start(out_words[:, slots], codes[:].bitcast(I32))
 
-        def store_words(start, stop):
-            nc.sync.dma_start(out_words[:, start:stop], out_codes[:, start:stop].bitcast(I32))
-
-        for i in range(2):
-            nc.scalar.copy(by_scalar[:, i, :, LAST], quarters_of(LAST, 1)[:, i, :])
-        for i in range(2):
-            nc.vector.tensor_copy(by_vector[:, i, :, LAST], quarters_of(LAST, 0)[:, i, :])
-        cut = 2 * QUARTER_U + EIGHTH_U
-        pack(by_vector[:, 0], 0)
-        store_words(0, QUARTER_U)
-        pack(by_scalar[:, 0], QUARTER_U)
-        pack(by_vector[:, 1, 0:EIGHTH_U], 2 * QUARTER_U)
-        store_words(QUARTER_U, cut)
-        pack(by_vector[:, 1, EIGHTH_U:QUARTER_U], cut)
-        pack(by_scalar[:, 1], 3 * QUARTER_U)
-        store_words(cut, U)
+        for quarter in quarters:
+            nc.scalar.copy(low[:, quarter, LAST], window[LAST][:, quarter])
+        for quarter in quarters:
+            nc.vector.tensor_copy(
+                high[:, quarter, LAST], window[LAST][:, HALF_U + quarter.start : HALF_U + quarter.stop]
+            )
+        for quarter in quarters:
+            pack(high, HALF_U, quarter)
+            pack(low, 0, quarter)
         for q in range(QUADRANTS):
             queue = nc.scalar if q % 2 else nc.sync
             queue.dma_start(

@@ -52,15 +52,15 @@ def tile_picked_wgmem_relu_lo_kernel(tc, x_words, x_scales, mem, w1, w2, slot, o
 
         nc.vector.memset(x_scale_tile[:].bitcast(I32), 0)
         load_weight(w2_raw, w2, 0)
-        nc.sync.dma_start(offsets[:], slot)
         for q in range(QUADRANTS):
             nc.sync.dma_start(
                 x_scale_tile[32 * q : 32 * q + 4, :].bitcast(I32), x_scales[0, 4 * q : 4 * q + 4, :].bitcast(I32)
             )
         load_weight(w2_raw, w2, 1)
         nc.sync.dma_start(x_codes[:].bitcast(I32), x_words[0].rearrange("p n r -> p (n r)").bitcast(I32))
-        for t in range(EARLY):
-            nc.sync.dma_start(window[t][:], mem_rows[t])
+        nc.sync.dma_start(window[0][:], mem_rows[0])
+        nc.sync.dma_start(offsets[:], slot)
+        nc.sync.dma_start(window[1][:], mem_rows[1])
         load_weight(w1_raw, w1, 0)
         load_weight(w1_raw, w1, 1)
         for t in range(EARLY, PACK):

@@ -1,6 +1,7 @@
 from contextlib import ExitStack
 
 import concourse.mybir as mybir
+from concourse.masks import make_identity
 
 K, T, N, U = 512, 512, 512, 1024
 FLOPS = 2 * 2 * K * N * T
@@ -101,6 +102,34 @@ def tile_picked_wgmem_relu_lo_kernel(tc, x_words, x_scales, mem, w1, w2, slot, o
             )
             return acc
 
+        identity = sb("identity", [P, P], F32)
+        make_identity(nc, identity[:])
+        blocks = [slice(b * P, (b + 1) * P) for b in range(T // P)]
+
+        def turn(terms, bank):
+            width = terms[0].shape[1]
+            acc = psum.tile([P, width], F32, name="acc", tag="bank%d" % bank)
+            for block in blocks[0 : width // P]:
+                for i, term in enumerate(terms):
+                    nc.tensor.matmul(
+                        acc[:, block], term[:, block], identity[:], start=i == 0, stop=i == len(terms) - 1, is_transpose=True
+                    )
+            return acc
+
+        def multiply_turned(weights, bank):
+            acc = psum.tile([P, T], F32, name="acc", tag="bank%d" % bank)
+            for block in blocks:
+                nc.tensor.matmul_mx(
+                    out=acc[:, block],
+                    lhsT=x_codes[:, block].bitcast(FP8X4),
+                    lhsT_scale=x_scale_tile[:, block],
+                    rhs=weights[0].bitcast(FP8X4),
+                    rhs_scale=weights[1],
+                    start=True,
+                    stop=True,
+                )
+            return acc
+
         everything = slice(0, T)
         halves = [slice(h * HALF_T, (h + 1) * HALF_T) for h in range(2)]
         offset_halves = [
@@ -141,8 +170,7 @@ def tile_picked_wgmem_relu_lo_kernel(tc, x_words, x_scales, mem, w1, w2, slot, o
 
         w1_all = sb("w1_groups23", [P, PACK, P, PACK], BF16)
         w1_dealt = [w1_all[:, 0:1], w1_all[:, 1:2], w1_all[:, 2:4]]
-        gate = {1: sb("gate1", [P, T], F32)[:]}
-        nc.scalar.activation(gate[1], u_acc[1][:], ACT.Sigmoid)
+        stay1_turned = turn([stay[1][:]], 2)
         deal(nc.scalar.copy, w1_all[:, 0:2], w1_raw, 0, 0)
         deal(nc.vector.tensor_copy, w1_dealt[0], w1_raw, 1, 0, slice(0, SPLIT_M))
         deal(nc.scalar.copy, w1_dealt[0], w1_raw, 1, 0, slice(SPLIT_M, P))
@@ -153,7 +181,7 @@ def tile_picked_wgmem_relu_lo_kernel(tc, x_words, x_scales, mem, w1, w2, slot, o
         )
         y0_weights = quantise("y0", w1_dealt[0])[0]
         y0_halves = [multiply(y0_weights, 5 + h, halves[h]) for h in range(2)]
-        y_acc = {1: multiply(quantise("y1", w1_dealt[1])[0], 7, everything)}
+        y_acc = {1: multiply_turned(quantise("y1", w1_dealt[1])[0], 7)}
         nc.vector.tensor_copy(old[EARLY][:, 0:FILL_T], window[EARLY][:].indirect(offsets[:, 0:first_columns]))
         fresh0 = sb("fresh0", [P, T], F32)
         for h in range(2):
@@ -171,29 +199,36 @@ def tile_picked_wgmem_relu_lo_kernel(tc, x_words, x_scales, mem, w1, w2, slot, o
         nc.vector.tensor_copy(window[0][:].indirect(offsets[:]), new0)
         nc.sync.dma_start(out_rows[0], window[0][:])
 
-        late_gates = sb("late_gates", [P, 2, T], F32, reuses="w1_raw1")
-        for t in range(2, PACK):
-            gate[t] = late_gates[:, t - 2, :]
+        late_gates = sb("late_gates", [P, LAST, T], F32, reuses="w1_raw1")
+        gate = {t: late_gates[:, t - 1, :] for t in range(1, PACK)}
+        kept1_turned = sb("kept1_turned", [P, T], F32)[:]
         candidate = {t: sb("candidate%d" % t, [P, T], F32) for t in range(1, PACK)}
-        for t in range(1, PACK):
-            if t > 1:
-                nc.scalar.activation(gate[t], u_acc[t][:], ACT.Sigmoid)
+        nc.scalar.activation(candidate[1][:], y_acc[1][:], ACT.Relu)
+        nc.scalar.activation(gate[1], stay1_turned[:], ACT.Copy, scale=-1.0, bias=1.0)
+        nc.scalar.copy(kept1_turned, turn([kept[1][:]], 5)[:])
+
+        def empty_banks(t):
             nc.scalar.activation(candidate[t][:], y_acc[t][:], ACT.Relu)
+            nc.scalar.activation(gate[t], u_acc[t][:], ACT.Sigmoid)
+
+        empty_banks(EARLY)
         new = {t: sb("new%d" % t, [P, T], F32) for t in range(1, LAST)}
         fresh1 = first_sums[:, 1, :]
         nc.gpsimd.tensor_tensor(fresh1, candidate[1][:], gate[1], ALU.mult)
-        nc.gpsimd.tensor_tensor(new[1][:], kept[1][:], fresh1, ALU.add)
+        for h in range(2):
+            nc.scalar.copy(new[1][:, halves[h]], turn([kept1_turned[:, halves[h]], fresh1[:, halves[h]]], 6 - h)[:])
+        empty_banks(LAST)
         step = {}
         for t in range(EARLY, PACK):
-            gap = sb("gap%d" % t, [P, T], F32, reuses={2: "kept1", 3: "old2"}[t])
-            step[t] = sb("step%d" % t, [P, T], F32)
+            gap = sb("gap%d" % t, [P, T], F32, reuses={2: None, 3: "old2"}[t])
+            step[t] = sb("step%d" % t, [P, T], F32, reuses={2: "identity", 3: None}[t])
             nc.gpsimd.tensor_tensor(gap[:], candidate[t][:], old[t][:], ALU.subtract)
             nc.gpsimd.tensor_tensor(step[t][:], gap[:], gate[t], ALU.mult)
             if t < LAST:
                 nc.gpsimd.tensor_tensor(new[t][:], old[t][:], step[t][:], ALU.add)
 
-        low = sb("low", [P, HALF_U, PACK], BF16)
-        high = sb("high", [P, HALF_U, PACK], BF16)
+        low = sb("low", [P, HALF_U, PACK], BF16, reuses="kept1_turned")
+        high = sb("high", [P, HALF_U, PACK], BF16, reuses="w1_groups23")
 
         def regroup(t):
             if t == LAST - 1:

@@ -41,7 +41,7 @@ def tile_picked_wgmem_relu_lo_kernel(tc, x_words, x_scales, mem, w1, w2, slot, o
         offsets = keep.tile([P, T // ENTRIES_PER_COLUMN], U16, name="offsets")
         x_codes = sb("x_codes", [P, T], U32)
         x_scale_tile = sb("x_scale_tile", [P, T], U8)
-        w1_whole = sb("w1_raw1", [P, PACK, N], F32)
+        w1_whole = sb("w1_whole", [P, PACK, N], F32)
         w1_raw = [w1_whole[:, 2 * h : 2 * h + 2, :] for h in range(2)]
         w2_raw = [sb("w2_raw%d" % h, [P, 2, N], F32) for h in range(2)]
         window = [sb("window%d" % t, [P, U], F32) for t in range(PACK)]
@@ -103,7 +103,6 @@ def tile_picked_wgmem_relu_lo_kernel(tc, x_words, x_scales, mem, w1, w2, slot, o
             return acc
 
         identity = sb("identity", [P, P], F32)
-        make_identity(nc, identity[:])
         blocks = [slice(b * P, (b + 1) * P) for b in range(T // P)]
 
         def turn(terms, bank):
@@ -139,6 +138,8 @@ def tile_picked_wgmem_relu_lo_kernel(tc, x_words, x_scales, mem, w1, w2, slot, o
         warm = sb("warm", [P, 2], F32)
         nc.gpsimd.memset(warm[:, 0:1], 0.0)
         nc.scalar.activation(warm[:, 1:2], warm[:, 0:1], ACT.Sigmoid)
+        make_identity(nc, identity[:])
+
         w2_dealt = dealt_tiles("w2")
         for h in range(2):
             for i in range(2):
@@ -155,8 +156,7 @@ def tile_picked_wgmem_relu_lo_kernel(tc, x_words, x_scales, mem, w1, w2, slot, o
         first_columns = FILL_T // ENTRIES_PER_COLUMN
         for h in range(2):
             nc.scalar.activation(stay[0][:, halves[h]], u0_halves[h][:], ACT.Sigmoid, scale=-1.0)
-        for t in range(1, EARLY):
-            nc.scalar.activation(stay[t][:], u_acc[t][:], ACT.Sigmoid, scale=-1.0)
+        nc.scalar.activation(stay[1][:], u_acc[1][:], ACT.Sigmoid, scale=-1.0)
         for h in range(2):
             nc.scalar.activation(gate0[h], u0_halves[h][:], ACT.Sigmoid)
 
@@ -165,12 +165,13 @@ def tile_picked_wgmem_relu_lo_kernel(tc, x_words, x_scales, mem, w1, w2, slot, o
             nc.vector.tensor_tensor(
                 kept[0][:, halves[h]], window[0][:].indirect(offset_halves[h]), stay[0][:, halves[h]], ALU.mult
             )
-        for t in range(1, EARLY):
-            nc.vector.tensor_tensor(kept[t][:], window[t][:].indirect(offsets[:]), stay[t][:], ALU.mult)
+        nc.vector.tensor_tensor(kept[1][:], window[1][:].indirect(offsets[:]), stay[1][:], ALU.mult)
 
-        w1_all = sb("w1_groups23", [P, PACK, P, PACK], BF16)
+        w1_all = sb("w1_all", [P, PACK, P, PACK], BF16)
         w1_dealt = [w1_all[:, 0:1], w1_all[:, 1:2], w1_all[:, 2:4]]
         stay1_turned = turn([stay[1][:]], 2)
+        gate = {LAST: sb("gate3", [P, T], F32)[:]}
+        nc.scalar.activation(gate[LAST], u_acc[LAST][:], ACT.Sigmoid)
         deal(nc.scalar.copy, w1_all[:, 0:2], w1_raw, 0, 0)
         deal(nc.vector.tensor_copy, w1_dealt[0], w1_raw, 1, 0, slice(0, SPLIT_M))
         deal(nc.scalar.copy, w1_dealt[0], w1_raw, 1, 0, slice(SPLIT_M, P))
@@ -193,42 +194,39 @@ def tile_picked_wgmem_relu_lo_kernel(tc, x_words, x_scales, mem, w1, w2, slot, o
             y_acc[t] = multiply(y23_weights[t - 2], t - 2, everything)
         nc.vector.tensor_copy(old[EARLY][:, FILL_T:T], window[EARLY][:].indirect(offsets[:, first_columns:]))
         nc.vector.tensor_copy(old[LAST][:], window[LAST][:].indirect(offsets[:]))
-        first_sums = sb("first_sums", [P, 2, T], F32, reuses="w1_groups23")
-        new0 = first_sums[:, 0, :]
+        first_results = sb("first_results", [P, 2, T], F32, reuses="w1_all")
+        new0 = first_results[:, 0, :]
         nc.gpsimd.tensor_tensor(new0, kept[0][:], fresh0[:], ALU.add)
         nc.vector.tensor_copy(window[0][:].indirect(offsets[:]), new0)
         nc.sync.dma_start(out_rows[0], window[0][:])
 
-        late_gates = sb("late_gates", [P, LAST, T], F32, reuses="w1_raw1")
-        gate = {t: late_gates[:, t - 1, :] for t in range(1, PACK)}
+        late_gates = sb("late_gates", [P, 2, T], F32, reuses="w1_whole")
+        for t in range(1, LAST):
+            gate[t] = late_gates[:, t - 1, :]
         kept1_turned = sb("kept1_turned", [P, T], F32)[:]
         candidate = {t: sb("candidate%d" % t, [P, T], F32) for t in range(1, PACK)}
         nc.scalar.activation(candidate[1][:], y_acc[1][:], ACT.Relu)
         nc.scalar.activation(gate[1], stay1_turned[:], ACT.Copy, scale=-1.0, bias=1.0)
         nc.scalar.copy(kept1_turned, turn([kept[1][:]], 5)[:])
-
-        def empty_banks(t):
-            nc.scalar.activation(candidate[t][:], y_acc[t][:], ACT.Relu)
-            nc.scalar.activation(gate[t], u_acc[t][:], ACT.Sigmoid)
-
-        empty_banks(EARLY)
+        nc.scalar.activation(candidate[EARLY][:], y_acc[EARLY][:], ACT.Relu)
+        nc.scalar.activation(gate[EARLY], u_acc[EARLY][:], ACT.Sigmoid)
         new = {t: sb("new%d" % t, [P, T], F32) for t in range(1, LAST)}
-        fresh1 = first_sums[:, 1, :]
+        fresh1 = first_results[:, 1, :]
         nc.gpsimd.tensor_tensor(fresh1, candidate[1][:], gate[1], ALU.mult)
         for h in range(2):
             nc.scalar.copy(new[1][:, halves[h]], turn([kept1_turned[:, halves[h]], fresh1[:, halves[h]]], 6 - h)[:])
-        empty_banks(LAST)
+        nc.scalar.activation(candidate[LAST][:], y_acc[LAST][:], ACT.Relu)
         step = {}
         for t in range(EARLY, PACK):
-            gap = sb("gap%d" % t, [P, T], F32, reuses={2: None, 3: "old2"}[t])
-            step[t] = sb("step%d" % t, [P, T], F32, reuses={2: "identity", 3: None}[t])
+            gap = sb("gap%d" % t, [P, T], F32, reuses="old2" if t == LAST else None)
+            step[t] = sb("step%d" % t, [P, T], F32)
             nc.gpsimd.tensor_tensor(gap[:], candidate[t][:], old[t][:], ALU.subtract)
             nc.gpsimd.tensor_tensor(step[t][:], gap[:], gate[t], ALU.mult)
             if t < LAST:
                 nc.gpsimd.tensor_tensor(new[t][:], old[t][:], step[t][:], ALU.add)
 
         low = sb("low", [P, HALF_U, PACK], BF16, reuses="kept1_turned")
-        high = sb("high", [P, HALF_U, PACK], BF16, reuses="w1_groups23")
+        high = sb("high", [P, HALF_U, PACK], BF16, reuses="w1_all")
 
         def regroup(t):
             if t == LAST - 1:

@@ -19,12 +19,9 @@ ACT = mybir.ActivationFunctionType
 P = 128
 PACK = 4
 LAST = PACK - 1
-EARLY = 2
 QUADRANTS = 4
 ENTRIES_PER_COLUMN = 16
 HALF_T = T // 2
-FILL_T = T // 4
-SPLIT_M = 96
 HALF_U = U // 2
 QUARTER_U = U // 4
 
@@ -61,10 +58,9 @@ def tile_picked_wgmem_relu_lo_kernel(tc, x_words, x_scales, mem, w1, w2, slot, o
         nc.sync.dma_start(x_codes[:].bitcast(I32), x_words[0].rearrange("p n r -> p (n r)").bitcast(I32))
         nc.sync.dma_start(window[0][:], mem_rows[0])
         nc.sync.dma_start(offsets[:], slot)
-        nc.sync.dma_start(window[1][:], mem_rows[1])
         load_weight(w1_raw, w1, 0)
         load_weight(w1_raw, w1, 1)
-        for t in range(EARLY, PACK):
+        for t in range(1, PACK):
             nc.sync.dma_start(window[t][:], mem_rows[t])
 
         def dealt_tiles(name):
@@ -74,15 +70,15 @@ def tile_picked_wgmem_relu_lo_kernel(tc, x_words, x_scales, mem, w1, w2, slot, o
                 sb(name + "_groups23", [P, 2, P, PACK], BF16),
             ]
 
-        def deal(engine_copy, dealt, raw, h, t0, columns=slice(0, P)):
+        def deal(engine_copy, dealt, raw, h, t0):
             engine_copy(
-                dealt[:, :, columns, 2 * h : 2 * h + 2].rearrange("p t m j -> p m t j"),
-                raw[h][:, :, :].rearrange("p j (m t) -> p m t j", t=PACK)[:, columns, t0 : t0 + dealt.shape[1], :],
+                dealt[:, :, :, 2 * h : 2 * h + 2].rearrange("p t m j -> p m t j"),
+                raw[h][:, :, :].rearrange("p j (m t) -> p m t j", t=PACK)[:, :, t0 : t0 + dealt.shape[1], :],
             )
 
-        def quantise(name, dealt, after=None):
+        def quantise(name, dealt):
             groups = dealt.shape[1]
-            codes = sb(name + "_codes", [P, groups * P], U32, reuses=after)
+            codes = sb(name + "_codes", [P, groups * P], U32)
             scales = sb(name + "_scales", [P, groups * P], U8)
             nc.vector.quantize_mx(
                 out=codes[:].bitcast(FP8X4), scales=scales[:], in_=dealt[:, :, :, :].rearrange("p t m j -> p (t m j)")
@@ -150,83 +146,90 @@ def tile_picked_wgmem_relu_lo_kernel(tc, x_words, x_scales, mem, w1, w2, slot, o
         u_weights = u_weights + quantise("u1", w2_dealt[1])
         u_weights = u_weights + quantise("u23", w2_dealt[2])
         u_acc = {t: multiply(u_weights[t], t + 1, everything) for t in range(1, PACK)}
-        stay = [sb("stay%d" % t, [P, T], F32) for t in range(EARLY)]
-        old = {t: sb("old%d" % t, [P, T], F32) for t in range(EARLY, PACK)}
-        gate0 = [sb("gate0_0", [P, HALF_T], F32)[:], old[EARLY][:, halves[1]]]
-        first_columns = FILL_T // ENTRIES_PER_COLUMN
+        stay0 = sb("stay0", [P, T], F32)
+        gate0 = sb("gate0", [P, T], F32)
+        kept0 = sb("kept0", [P, T], F32)
         for h in range(2):
-            nc.scalar.activation(stay[0][:, halves[h]], u0_halves[h][:], ACT.Sigmoid, scale=-1.0)
-        nc.scalar.activation(stay[1][:], u_acc[1][:], ACT.Sigmoid, scale=-1.0)
+            nc.scalar.activation(stay0[:, halves[h]], u0_halves[h][:], ACT.Sigmoid, scale=-1.0)
         for h in range(2):
-            nc.scalar.activation(gate0[h], u0_halves[h][:], ACT.Sigmoid)
-
-        kept = [sb("kept%d" % t, [P, T], F32) for t in range(EARLY)]
+            nc.scalar.activation(gate0[:, halves[h]], u0_halves[h][:], ACT.Sigmoid)
         for h in range(2):
             nc.vector.tensor_tensor(
-                kept[0][:, halves[h]], window[0][:].indirect(offset_halves[h]), stay[0][:, halves[h]], ALU.mult
+                kept0[:, halves[h]], window[0][:].indirect(offset_halves[h]), stay0[:, halves[h]], ALU.mult
             )
-        nc.vector.tensor_tensor(kept[1][:], window[1][:].indirect(offsets[:]), stay[1][:], ALU.mult)
 
         w1_all = sb("w1_all", [P, PACK, P, PACK], BF16)
         w1_dealt = [w1_all[:, 0:1], w1_all[:, 1:2], w1_all[:, 2:4]]
-        stay1_turned = turn([stay[1][:]], 2)
-        gate = {LAST: sb("gate3", [P, T], F32)[:]}
-        nc.scalar.activation(gate[LAST], u_acc[LAST][:], ACT.Sigmoid)
-        deal(nc.scalar.copy, w1_all[:, 0:2], w1_raw, 0, 0)
-        deal(nc.vector.tensor_copy, w1_dealt[0], w1_raw, 1, 0, slice(0, SPLIT_M))
-        deal(nc.scalar.copy, w1_dealt[0], w1_raw, 1, 0, slice(SPLIT_M, P))
-        deal(nc.scalar.copy, w1_dealt[1], w1_raw, 1, 1)
-        nc.scalar.copy(
-            w1_dealt[2].rearrange("p t m j -> p m t j"),
-            w1_whole[:].rearrange("p j (m t) -> p m t j", t=PACK)[:, :, 2:4, :],
-        )
+        deal(nc.vector.tensor_copy, w1_all[:, 0:2], w1_raw, 0, 0)
+        deal(nc.scalar.copy, w1_dealt[2], w1_raw, 0, 2)
+        for i in range(2):
+            deal(nc.vector.tensor_copy, w1_dealt[i], w1_raw, 1, i)
+        deal(nc.scalar.copy, w1_dealt[2], w1_raw, 1, 2)
         y0_weights = quantise("y0", w1_dealt[0])[0]
-        y0_halves = [multiply(y0_weights, 5 + h, halves[h]) for h in range(2)]
-        y_acc = {1: multiply_turned(quantise("y1", w1_dealt[1])[0], 7)}
-        nc.vector.tensor_copy(old[EARLY][:, 0:FILL_T], window[EARLY][:].indirect(offsets[:, 0:first_columns]))
-        fresh0 = sb("fresh0", [P, T], F32)
+        y0_halves = [multiply(y0_weights, (1, 5)[h], halves[h]) for h in range(2)]
+        y_acc = {1: multiply_turned(quantise("y1", w1_dealt[1])[0], 6)}
+        y23_weights = quantise("y23", w1_dealt[2])
+        y_acc[2] = multiply_turned(y23_weights[0], 7)
+        y_acc[LAST] = multiply(y23_weights[1], 0, everything)
+        old = {t: sb("old%d" % t, [P, T], F32) for t in range(1, PACK)}
+        for t in range(1, PACK):
+            nc.vector.tensor_copy(old[t][:], window[t][:].indirect(offsets[:]))
+
+        gate = {1: sb("gate1", [P, T], F32, reuses="w1_whole")}
+        nc.scalar.activation(gate[1][:], u_acc[1][:], ACT.Sigmoid)
+        candidate = {t: sb("candidate%d" % t, [P, T], F32) for t in range(2)}
+        new = {t: sb("new%d" % t, [P, T], F32) for t in range(1, LAST)}
         for h in range(2):
-            nc.vector.scalar_tensor_tensor(
-                fresh0[:, halves[h]], y0_halves[h][:], 0.0, gate0[h], ALU.max, ALU.mult
-            )
-        y23_weights = quantise("y23", w1_dealt[2], after="gate0_0")
-        for t in range(2, PACK):
-            y_acc[t] = multiply(y23_weights[t - 2], t - 2, everything)
-        nc.vector.tensor_copy(old[EARLY][:, FILL_T:T], window[EARLY][:].indirect(offsets[:, first_columns:]))
-        nc.vector.tensor_copy(old[LAST][:], window[LAST][:].indirect(offsets[:]))
-        first_results = sb("first_results", [P, 2, T], F32, reuses="w1_all")
-        new0 = first_results[:, 0, :]
-        nc.gpsimd.tensor_tensor(new0, kept[0][:], fresh0[:], ALU.add)
-        nc.vector.tensor_copy(window[0][:].indirect(offsets[:]), new0)
+            nc.scalar.activation(candidate[0][:, halves[h]], y0_halves[h][:], ACT.Relu)
+
+        def form_fresh0(h):
+            fresh = sb("fresh0", [P, HALF_T], F32, reuses="w1_all")
+            nc.gpsimd.tensor_tensor(fresh[:], candidate[0][:, halves[h]], gate0[:, halves[h]], ALU.mult)
+            return fresh
+
+        def scatter0(h, fresh, reuses=None):
+            new0 = sb("new0_%d" % h, [P, HALF_T], F32, reuses=reuses)
+            nc.gpsimd.tensor_tensor(new0[:], kept0[:, halves[h]], fresh[:], ALU.add)
+            nc.vector.tensor_copy(window[0][:].indirect(offset_halves[h]), new0[:])
+
+        scatter0(0, form_fresh0(0))
+        second_fresh0 = form_fresh0(1)
+
+        gap = {t: sb("gap%d" % t, [P, T], F32) for t in range(1, LAST)}
+        nc.scalar.activation(candidate[1][:], y_acc[1][:], ACT.Relu)
+        gate[2] = sb("gate2", [P, T], F32, reuses="y0_codes")
+        nc.scalar.activation(gate[2][:], u_acc[2][:], ACT.Sigmoid)
+        old1_turned = turn([old[1][:]], 5)
+        minus_old1 = [sb("minus_old1_%d" % h, [P, HALF_T], F32) for h in range(2)]
+        for h in range(2):
+            nc.scalar.activation(minus_old1[h][:], old1_turned[:, halves[h]], ACT.Copy, scale=-1.0)
+        for h in range(2):
+            nc.scalar.copy(gap[1][:, halves[h]], turn([candidate[1][:, halves[h]], minus_old1[h][:]], (2, 1)[h])[:])
+        scatter0(1, second_fresh0, reuses="minus_old1_0")
         nc.sync.dma_start(out_rows[0], window[0][:])
 
-        late_gates = sb("late_gates", [P, 2, T], F32, reuses="w1_whole")
-        for t in range(1, LAST):
-            gate[t] = late_gates[:, t - 1, :]
-        kept1_turned = sb("kept1_turned", [P, T], F32)[:]
-        candidate = {t: sb("candidate%d" % t, [P, T], F32) for t in range(1, PACK)}
-        nc.scalar.activation(candidate[1][:], y_acc[1][:], ACT.Relu)
-        nc.scalar.activation(gate[1], stay1_turned[:], ACT.Copy, scale=-1.0, bias=1.0)
-        nc.scalar.copy(kept1_turned, turn([kept[1][:]], 5)[:])
-        nc.scalar.activation(candidate[EARLY][:], y_acc[EARLY][:], ACT.Relu)
-        nc.scalar.activation(gate[EARLY], u_acc[EARLY][:], ACT.Sigmoid)
-        new = {t: sb("new%d" % t, [P, T], F32) for t in range(1, LAST)}
-        fresh1 = first_results[:, 1, :]
-        nc.gpsimd.tensor_tensor(fresh1, candidate[1][:], gate[1], ALU.mult)
-        for h in range(2):
-            nc.scalar.copy(new[1][:, halves[h]], turn([kept1_turned[:, halves[h]], fresh1[:, halves[h]]], 6 - h)[:])
+        later = sb("later", [P, 3, T], F32, reuses="minus_old1_1")
+        candidate[2], candidate[LAST], gate[LAST] = (later[:, i, :] for i in range(3))
+        nc.scalar.activation(candidate[2][:], y_acc[2][:], ACT.Relu)
+        minus_old2 = sb("minus_old2", [P, T], F32)
+        nc.scalar.activation(minus_old2[:], turn([old[2][:]], 5)[:], ACT.Copy, scale=-1.0)
+        gap2_sum = turn([candidate[2], minus_old2[:]], 2)
         nc.scalar.activation(candidate[LAST][:], y_acc[LAST][:], ACT.Relu)
+        nc.scalar.activation(gate[LAST][:], u_acc[LAST][:], ACT.Sigmoid)
+        nc.scalar.copy(gap[2][:], gap2_sum[:])
+
         step = {}
-        for t in range(EARLY, PACK):
-            gap = sb("gap%d" % t, [P, T], F32, reuses="old2" if t == LAST else None)
-            step[t] = sb("step%d" % t, [P, T], F32)
-            nc.gpsimd.tensor_tensor(gap[:], candidate[t][:], old[t][:], ALU.subtract)
-            nc.gpsimd.tensor_tensor(step[t][:], gap[:], gate[t], ALU.mult)
+        for t in range(1, PACK):
+            if t == LAST:
+                gap[t] = sb("gap%d" % t, [P, T], F32, reuses="old2")
+                nc.gpsimd.tensor_tensor(gap[t][:], candidate[t][:], old[t][:], ALU.subtract)
+            step[t] = sb("step%d" % t, [P, T], F32, reuses="old1" if t == 2 else None)
+            nc.gpsimd.tensor_tensor(step[t][:], gap[t][:], gate[t][:], ALU.mult)
             if t < LAST:
                 nc.gpsimd.tensor_tensor(new[t][:], old[t][:], step[t][:], ALU.add)
 
-        low = sb("low", [P, HALF_U, PACK], BF16, reuses="kept1_turned")
-        high = sb("high", [P, HALF_U, PACK], BF16, reuses="w1_all")
+        low = sb("low", [P, HALF_U, PACK], BF16, reuses="minus_old2")
+        high = sb("high", [P, HALF_U, PACK], BF16, reuses="identity")
 
         def regroup(t):
             if t == LAST - 1:

@@ -38,8 +38,7 @@ def tile_picked_wgmem_relu_lo_kernel(tc, x_words, x_scales, mem, w1, w2, slot, o
         offsets = keep.tile([P, T // ENTRIES_PER_COLUMN], U16, name="offsets")
         x_codes = sb("x_codes", [P, T], U32)
         x_scale_tile = sb("x_scale_tile", [P, T], U8)
-        w1_whole = sb("w1_whole", [P, PACK, N], F32)
-        w1_raw = [w1_whole[:, 2 * h : 2 * h + 2, :] for h in range(2)]
+        w1_raw = [sb("w1_raw%d" % h, [P, 2, N], F32) for h in range(2)]
         w2_raw = [sb("w2_raw%d" % h, [P, 2, N], F32) for h in range(2)]
         window = [sb("window%d" % t, [P, U], F32) for t in range(PACK)]
         mem_rows = mem.rearrange("(p t) u -> t p u", t=PACK)
@@ -49,26 +48,22 @@ def tile_picked_wgmem_relu_lo_kernel(tc, x_words, x_scales, mem, w1, w2, slot, o
             nc.sync.dma_start(raw[h][:, :, :], w.rearrange("(p j) n -> p j n", j=PACK)[:, 2 * h : 2 * h + 2, :])
 
         nc.vector.memset(x_scale_tile[:].bitcast(I32), 0)
-        load_weight(w2_raw, w2, 0)
+        nc.sync.dma_start(window[0][:], mem_rows[0])
+        nc.sync.dma_start(offsets[:], slot)
+        load_weight(w1_raw, w1, 0)
         for q in range(QUADRANTS):
             nc.sync.dma_start(
                 x_scale_tile[32 * q : 32 * q + 4, :].bitcast(I32), x_scales[0, 4 * q : 4 * q + 4, :].bitcast(I32)
             )
-        load_weight(w2_raw, w2, 1)
-        nc.sync.dma_start(x_codes[:].bitcast(I32), x_words[0].rearrange("p n r -> p (n r)").bitcast(I32))
-        nc.sync.dma_start(window[0][:], mem_rows[0])
-        nc.sync.dma_start(offsets[:], slot)
-        load_weight(w1_raw, w1, 0)
         load_weight(w1_raw, w1, 1)
+        nc.sync.dma_start(x_codes[:].bitcast(I32), x_words[0].rearrange("p n r -> p (n r)").bitcast(I32))
+        load_weight(w2_raw, w2, 0)
+        load_weight(w2_raw, w2, 1)
         for t in range(1, PACK):
             nc.sync.dma_start(window[t][:], mem_rows[t])
 
         def dealt_tiles(name):
-            return [
-                sb(name + "_group0", [P, 1, P, PACK], BF16),
-                sb(name + "_group1", [P, 1, P, PACK], BF16),
-                sb(name + "_groups23", [P, 2, P, PACK], BF16),
-            ]
+            return [sb(name + "_groups01", [P, 2, P, PACK], BF16), sb(name + "_groups23", [P, 2, P, PACK], BF16)]
 
         def deal(engine_copy, dealt, raw, h, t0):
             engine_copy(
@@ -136,84 +131,76 @@ def tile_picked_wgmem_relu_lo_kernel(tc, x_words, x_scales, mem, w1, w2, slot, o
         nc.scalar.activation(warm[:, 1:2], warm[:, 0:1], ACT.Sigmoid)
         make_identity(nc, identity[:])
 
-        w2_dealt = dealt_tiles("w2")
-        for h in range(2):
-            for i in range(2):
-                deal(nc.vector.tensor_copy, w2_dealt[i], w2_raw, h, i)
-            deal(nc.scalar.copy, w2_dealt[2], w2_raw, h, 2)
-        u_weights = quantise("u0", w2_dealt[0])
-        u0_halves = [multiply(u_weights[0], h, halves[h]) for h in range(2)]
-        u_weights = u_weights + quantise("u1", w2_dealt[1])
-        u_weights = u_weights + quantise("u23", w2_dealt[2])
-        u_acc = {t: multiply(u_weights[t], t + 1, everything) for t in range(1, PACK)}
-        stay0 = sb("stay0", [P, T], F32)
-        gate0 = sb("gate0", [P, T], F32)
-        kept0 = sb("kept0", [P, T], F32)
-        for h in range(2):
-            nc.scalar.activation(stay0[:, halves[h]], u0_halves[h][:], ACT.Sigmoid, scale=-1.0)
-        for h in range(2):
-            nc.scalar.activation(gate0[:, halves[h]], u0_halves[h][:], ACT.Sigmoid)
-        for h in range(2):
-            nc.vector.tensor_tensor(
-                kept0[:, halves[h]], window[0][:].indirect(offset_halves[h]), stay0[:, halves[h]], ALU.mult
-            )
+        old = {t: sb("old%d" % t, [P, T], F32) for t in range(PACK)}
+        nc.vector.tensor_copy(old[0][:], window[0][:].indirect(offsets[:]))
 
-        w1_all = sb("w1_all", [P, PACK, P, PACK], BF16)
-        w1_dealt = [w1_all[:, 0:1], w1_all[:, 1:2], w1_all[:, 2:4]]
-        deal(nc.vector.tensor_copy, w1_all[:, 0:2], w1_raw, 0, 0)
-        deal(nc.scalar.copy, w1_dealt[2], w1_raw, 0, 2)
-        for i in range(2):
-            deal(nc.vector.tensor_copy, w1_dealt[i], w1_raw, 1, i)
-        deal(nc.scalar.copy, w1_dealt[2], w1_raw, 1, 2)
-        y0_weights = quantise("y0", w1_dealt[0])[0]
-        y0_halves = [multiply(y0_weights, (1, 5)[h], halves[h]) for h in range(2)]
-        y_acc = {1: multiply_turned(quantise("y1", w1_dealt[1])[0], 6)}
-        y23_weights = quantise("y23", w1_dealt[2])
+        w1_dealt = dealt_tiles("w1")
+        for h in range(2):
+            deal(nc.vector.tensor_copy, w1_dealt[0], w1_raw, h, 0)
+            deal(nc.scalar.copy, w1_dealt[1], w1_raw, h, 2)
+        y01_weights = quantise("y01", w1_dealt[0])
+        y_acc = {0: multiply(y01_weights[0], 0, everything)}
+        y_acc[1] = multiply_turned(y01_weights[1], 6)
+        y23_weights = quantise("y23", w1_dealt[1])
         y_acc[2] = multiply_turned(y23_weights[0], 7)
-        y_acc[LAST] = multiply(y23_weights[1], 0, everything)
-        old = {t: sb("old%d" % t, [P, T], F32) for t in range(1, PACK)}
+        y_acc[LAST] = multiply(y23_weights[1], 4, everything)
+
+        gap = {t: sb("gap%d" % t, [P, T], F32) for t in range(LAST)}
+        w2_dealt = dealt_tiles("w2")
+        w2_groups = [w2_dealt[0][:, 0:1], w2_dealt[0][:, 1:2]]
+        deal(nc.vector.tensor_copy, w2_dealt[0], w2_raw, 0, 0)
+        deal(nc.scalar.copy, w2_dealt[1], w2_raw, 0, 2)
+        nc.vector.scalar_tensor_tensor(gap[0][:], y_acc[0][:], 0.0, old[0][:], ALU.max, ALU.subtract)
+        for i in range(2):
+            deal(nc.vector.tensor_copy, w2_groups[i], w2_raw, 1, i)
+        deal(nc.scalar.copy, w2_dealt[1], w2_raw, 1, 2)
+        u0_weights = quantise("u0", w2_groups[0])[0]
+        u0_halves = [multiply(u0_weights, (1, 5)[h], halves[h]) for h in range(2)]
+        u_acc = {1: multiply(quantise("u1", w2_groups[1])[0], 2, everything)}
+        u23_weights = quantise("u23", w2_dealt[1])
+        u_acc[2] = multiply(u23_weights[0], 3, everything)
         for t in range(1, PACK):
             nc.vector.tensor_copy(old[t][:], window[t][:].indirect(offsets[:]))
 
-        gate = {1: sb("gate1", [P, T], F32, reuses="w1_whole")}
-        nc.scalar.activation(gate[1][:], u_acc[1][:], ACT.Sigmoid)
-        candidate = {t: sb("candidate%d" % t, [P, T], F32) for t in range(2)}
+        gate = {t: sb("gate%d" % t, [P, T], F32) for t in range(LAST)}
+        candidate = {1: sb("candidate1", [P, T], F32, reuses="w2_raw1")}
         new = {t: sb("new%d" % t, [P, T], F32) for t in range(1, LAST)}
+        nc.scalar.activation(candidate[1][:], y_acc[1][:], ACT.Relu)
         for h in range(2):
-            nc.scalar.activation(candidate[0][:, halves[h]], y0_halves[h][:], ACT.Relu)
+            nc.scalar.activation(gate[0][:, halves[h]], u0_halves[h][:], ACT.Sigmoid)
 
-        def form_fresh0(h):
-            fresh = sb("fresh0", [P, HALF_T], F32, reuses="w1_all")
-            nc.gpsimd.tensor_tensor(fresh[:], candidate[0][:, halves[h]], gate0[:, halves[h]], ALU.mult)
-            return fresh
+        def form_step0(h):
+            step0 = sb("step0", [P, HALF_T], F32)
+            nc.gpsimd.tensor_tensor(step0[:], gap[0][:, halves[h]], gate[0][:, halves[h]], ALU.mult)
+            return step0
 
-        def scatter0(h, fresh, reuses=None):
+        def scatter0(h, step0, reuses=None):
             new0 = sb("new0_%d" % h, [P, HALF_T], F32, reuses=reuses)
-            nc.gpsimd.tensor_tensor(new0[:], kept0[:, halves[h]], fresh[:], ALU.add)
+            nc.gpsimd.tensor_tensor(new0[:], old[0][:, halves[h]], step0[:], ALU.add)
             nc.vector.tensor_copy(window[0][:].indirect(offset_halves[h]), new0[:])
 
-        scatter0(0, form_fresh0(0))
-        second_fresh0 = form_fresh0(1)
+        scatter0(0, form_step0(0))
+        second_step0 = form_step0(1)
 
-        gap = {t: sb("gap%d" % t, [P, T], F32) for t in range(1, LAST)}
-        nc.scalar.activation(candidate[1][:], y_acc[1][:], ACT.Relu)
-        gate[2] = sb("gate2", [P, T], F32, reuses="y0_codes")
-        nc.scalar.activation(gate[2][:], u_acc[2][:], ACT.Sigmoid)
-        old1_turned = turn([old[1][:]], 5)
+        nc.scalar.activation(gate[1][:], u_acc[1][:], ACT.Sigmoid)
+        candidate[2] = sb("candidate2", [P, T], F32, reuses="u0_codes")
+        nc.scalar.activation(candidate[2][:], y_acc[2][:], ACT.Relu)
+        old1_turned = turn([old[1][:]], 6)
         minus_old1 = [sb("minus_old1_%d" % h, [P, HALF_T], F32) for h in range(2)]
         for h in range(2):
             nc.scalar.activation(minus_old1[h][:], old1_turned[:, halves[h]], ACT.Copy, scale=-1.0)
         for h in range(2):
-            nc.scalar.copy(gap[1][:, halves[h]], turn([candidate[1][:, halves[h]], minus_old1[h][:]], (2, 1)[h])[:])
-        scatter0(1, second_fresh0, reuses="minus_old1_0")
+            nc.scalar.copy(gap[1][:, halves[h]], turn([candidate[1][:, halves[h]], minus_old1[h][:]], (5, 0)[h])[:])
+        scatter0(1, second_step0, reuses="minus_old1_0")
         nc.sync.dma_start(out_rows[0], window[0][:])
 
-        later = sb("later", [P, 3, T], F32, reuses="minus_old1_1")
-        candidate[2], candidate[LAST], gate[LAST] = (later[:, i, :] for i in range(3))
-        nc.scalar.activation(candidate[2][:], y_acc[2][:], ACT.Relu)
+        nc.scalar.activation(gate[2][:], u_acc[2][:], ACT.Sigmoid)
+        later = sb("later", [P, 2, T], F32, reuses="minus_old1_1")
+        candidate[LAST], gate[LAST] = (later[:, i, :] for i in range(2))
         minus_old2 = sb("minus_old2", [P, T], F32)
-        nc.scalar.activation(minus_old2[:], turn([old[2][:]], 5)[:], ACT.Copy, scale=-1.0)
-        gap2_sum = turn([candidate[2], minus_old2[:]], 2)
+        nc.scalar.activation(minus_old2[:], turn([old[2][:]], 6)[:], ACT.Copy, scale=-1.0)
+        gap2_sum = turn([candidate[2][:], minus_old2[:]], 1)
+        u_acc[LAST] = multiply(u23_weights[1], 5, everything)
         nc.scalar.activation(candidate[LAST][:], y_acc[LAST][:], ACT.Relu)
         nc.scalar.activation(gate[LAST][:], u_acc[LAST][:], ACT.Sigmoid)
         nc.scalar.copy(gap[2][:], gap2_sum[:])

@@ -143,7 +143,6 @@ def tile_picked_wgmem_relu_lo_kernel(tc, x_words, x_scales, mem, w1, w2, slot, o
         y_acc[1] = multiply_turned(y01_weights[1], 6)
         y23_weights = quantise("y23", w1_dealt[1])
         y_acc[2] = multiply_turned(y23_weights[0], 7)
-        y_acc[LAST] = multiply(y23_weights[1], 4, everything)
 
         gap = {t: sb("gap%d" % t, [P, T], F32) for t in range(LAST)}
         w2_dealt = dealt_tiles("w2")
@@ -162,7 +161,7 @@ def tile_picked_wgmem_relu_lo_kernel(tc, x_words, x_scales, mem, w1, w2, slot, o
         for t in range(1, PACK):
             nc.vector.tensor_copy(old[t][:], window[t][:].indirect(offsets[:]))
 
-        gate = {t: sb("gate%d" % t, [P, T], F32) for t in range(LAST)}
+        gate = {t: sb("gate%d" % t, [P, T], F32) for t in range(2)}
         candidate = {1: sb("candidate1", [P, T], F32, reuses="w2_raw1")}
         new = {t: sb("new%d" % t, [P, T], F32) for t in range(1, LAST)}
         nc.scalar.activation(candidate[1][:], y_acc[1][:], ACT.Relu)
@@ -185,25 +184,26 @@ def tile_picked_wgmem_relu_lo_kernel(tc, x_words, x_scales, mem, w1, w2, slot, o
         nc.scalar.activation(gate[1][:], u_acc[1][:], ACT.Sigmoid)
         candidate[2] = sb("candidate2", [P, T], F32, reuses="u0_codes")
         nc.scalar.activation(candidate[2][:], y_acc[2][:], ACT.Relu)
-        old1_turned = turn([old[1][:]], 6)
+        old1_turned = [turn([old[1][:, halves[h]]], (6, 4)[h]) for h in range(2)]
+        y_acc[LAST] = multiply(y23_weights[1], 2, everything)
         minus_old1 = [sb("minus_old1_%d" % h, [P, HALF_T], F32) for h in range(2)]
         for h in range(2):
-            nc.scalar.activation(minus_old1[h][:], old1_turned[:, halves[h]], ACT.Copy, scale=-1.0)
+            nc.scalar.activation(minus_old1[h][:], old1_turned[h][:], ACT.Copy, scale=-1.0)
         for h in range(2):
             nc.scalar.copy(gap[1][:, halves[h]], turn([candidate[1][:, halves[h]], minus_old1[h][:]], (5, 0)[h])[:])
         scatter0(1, second_step0, reuses="minus_old1_0")
         nc.sync.dma_start(out_rows[0], window[0][:])
 
-        nc.scalar.activation(gate[2][:], u_acc[2][:], ACT.Sigmoid)
-        later = sb("later", [P, 2, T], F32, reuses="minus_old1_1")
-        candidate[LAST], gate[LAST] = (later[:, i, :] for i in range(2))
+        later = sb("later", [P, 3, T], F32, reuses="minus_old1_1")
+        gate[2], candidate[LAST], gate[LAST] = (later[:, i, :] for i in range(3))
         minus_old2 = sb("minus_old2", [P, T], F32)
         nc.scalar.activation(minus_old2[:], turn([old[2][:]], 6)[:], ACT.Copy, scale=-1.0)
         gap2_sum = turn([candidate[2][:], minus_old2[:]], 1)
         u_acc[LAST] = multiply(u23_weights[1], 5, everything)
+        nc.scalar.activation(gate[2][:], u_acc[2][:], ACT.Sigmoid)
         nc.scalar.activation(candidate[LAST][:], y_acc[LAST][:], ACT.Relu)
-        nc.scalar.activation(gate[LAST][:], u_acc[LAST][:], ACT.Sigmoid)
         nc.scalar.copy(gap[2][:], gap2_sum[:])
+        nc.scalar.activation(gate[LAST][:], u_acc[LAST][:], ACT.Sigmoid)
 
         step = {}
         for t in range(1, PACK):

@@ -154,8 +154,9 @@ def tile_picked_wgmem_relu_lo_kernel(tc, x_words, x_scales, mem, w1, w2, slot, o
             deal(nc.vector.tensor_copy, w2_groups[i], w2_raw, 1, i)
         deal(nc.scalar.copy, w2_dealt[1], w2_raw, 1, 2)
         u0_weights = quantise("u0", w2_groups[0])[0]
-        u0_halves = [multiply(u0_weights, (1, 5)[h], halves[h]) for h in range(2)]
+        u0_halves = [multiply(u0_weights, 1, halves[0])]
         u_acc = {1: multiply(quantise("u1", w2_groups[1])[0], 2, everything)}
+        u0_halves.append(multiply(u0_weights, 5, halves[1]))
         u23_weights = quantise("u23", w2_dealt[1])
         u_acc[2] = multiply(u23_weights[0], 3, everything)
         for t in range(1, PACK):
@@ -165,11 +166,12 @@ def tile_picked_wgmem_relu_lo_kernel(tc, x_words, x_scales, mem, w1, w2, slot, o
         candidate = {1: sb("candidate1", [P, T], F32, reuses="w2_raw1")}
         new = {t: sb("new%d" % t, [P, T], F32) for t in range(1, LAST)}
         nc.scalar.activation(candidate[1][:], y_acc[1][:], ACT.Relu)
-        for h in range(2):
-            nc.scalar.activation(gate[0][:, halves[h]], u0_halves[h][:], ACT.Sigmoid)
+        nc.scalar.activation(gate[0][:, halves[0]], u0_halves[0][:], ACT.Sigmoid)
+        nc.scalar.activation(gate[1][:], u_acc[1][:], ACT.Sigmoid)
+        nc.scalar.activation(gate[0][:, halves[1]], u0_halves[1][:], ACT.Sigmoid)
 
         def form_step0(h):
-            step0 = sb("step0", [P, HALF_T], F32)
+            step0 = sb("step0_%d" % h, [P, HALF_T], F32)
             nc.gpsimd.tensor_tensor(step0[:], gap[0][:, halves[h]], gate[0][:, halves[h]], ALU.mult)
             return step0
 
@@ -181,9 +183,8 @@ def tile_picked_wgmem_relu_lo_kernel(tc, x_words, x_scales, mem, w1, w2, slot, o
         scatter0(0, form_step0(0))
         second_step0 = form_step0(1)
 
-        nc.scalar.activation(gate[1][:], u_acc[1][:], ACT.Sigmoid)
         candidate[2] = sb("candidate2", [P, T], F32, reuses="u0_codes")
-        nc.scalar.activation(candidate[2][:], y_acc[2][:], ACT.Relu)
+        nc.scalar.activation(candidate[2][:, halves[0]], y_acc[2][:, halves[0]], ACT.Relu)
         old1_turned = [turn([old[1][:, halves[h]]], (6, 4)[h]) for h in range(2)]
         y_acc[LAST] = multiply(y23_weights[1], 2, everything)
         minus_old1 = [sb("minus_old1_%d" % h, [P, HALF_T], F32) for h in range(2)]
@@ -191,6 +192,7 @@ def tile_picked_wgmem_relu_lo_kernel(tc, x_words, x_scales, mem, w1, w2, slot, o
             nc.scalar.activation(minus_old1[h][:], old1_turned[h][:], ACT.Copy, scale=-1.0)
         for h in range(2):
             nc.scalar.copy(gap[1][:, halves[h]], turn([candidate[1][:, halves[h]], minus_old1[h][:]], (5, 0)[h])[:])
+        nc.scalar.activation(candidate[2][:, halves[1]], y_acc[2][:, halves[1]], ACT.Relu)
         scatter0(1, second_step0, reuses="minus_old1_0")
         nc.sync.dma_start(out_rows[0], window[0][:])
 
@@ -210,7 +212,7 @@ def tile_picked_wgmem_relu_lo_kernel(tc, x_words, x_scales, mem, w1, w2, slot, o
             if t == LAST:
                 gap[t] = sb("gap%d" % t, [P, T], F32, reuses="old2")
                 nc.gpsimd.tensor_tensor(gap[t][:], candidate[t][:], old[t][:], ALU.subtract)
-            step[t] = sb("step%d" % t, [P, T], F32, reuses="old1" if t == 2 else None)
+            step[t] = sb("step%d" % t, [P, T], F32)
             nc.gpsimd.tensor_tensor(step[t][:], gap[t][:], gate[t][:], ALU.mult)
             if t < LAST:
                 nc.gpsimd.tensor_tensor(new[t][:], old[t][:], step[t][:], ALU.add)

@@ -38,24 +38,25 @@ def tile_picked_wgmem_relu_lo_kernel(tc, x_words, x_scales, mem, w1, w2, slot, o
         offsets = keep.tile([P, T // ENTRIES_PER_COLUMN], U16, name="offsets")
         x_codes = sb("x_codes", [P, T], U32)
         x_scale_tile = sb("x_scale_tile", [P, T], U8)
-        w1_raw = [sb("w1_raw%d" % h, [P, 2, N], F32) for h in range(2)]
-        w2_raw = [sb("w2_raw%d" % h, [P, 2, N], F32) for h in range(2)]
+        w1_raw = [sb("w1_raw%d" % pair, [P, 2, N], F32) for pair in range(2)]
+        w2_raw = [sb("w2_raw%d" % pair, [P, 2, N], F32) for pair in range(2)]
         window = [sb("window%d" % t, [P, U], F32) for t in range(PACK)]
         mem_rows = mem.rearrange("(p t) u -> t p u", t=PACK)
         out_rows = out_0.rearrange("(p t) u -> t p u", t=PACK)
 
-        def load_weight(raw, w, h):
-            nc.sync.dma_start(raw[h][:, :, :], w.rearrange("(p j) n -> p j n", j=PACK)[:, 2 * h : 2 * h + 2, :])
+        def load_weight(raw, w, pair):
+            nc.sync.dma_start(raw[pair][:, :, :], w.rearrange("(p j) n -> p j n", j=PACK)[:, 2 * pair : 2 * pair + 2, :])
 
         nc.vector.memset(x_scale_tile[:].bitcast(I32), 0)
         nc.sync.dma_start(window[0][:], mem_rows[0])
         nc.sync.dma_start(offsets[:], slot)
         load_weight(w1_raw, w1, 0)
-        for q in range(QUADRANTS):
-            nc.sync.dma_start(
-                x_scale_tile[32 * q : 32 * q + 4, :].bitcast(I32), x_scales[0, 4 * q : 4 * q + 4, :].bitcast(I32)
-            )
         load_weight(w1_raw, w1, 1)
+        for quadrant in range(QUADRANTS):
+            nc.sync.dma_start(
+                x_scale_tile[32 * quadrant : 32 * quadrant + 4, :].bitcast(I32),
+                x_scales[0, 4 * quadrant : 4 * quadrant + 4, :].bitcast(I32),
+            )
         nc.sync.dma_start(x_codes[:].bitcast(I32), x_words[0].rearrange("p n r -> p (n r)").bitcast(I32))
         load_weight(w2_raw, w2, 0)
         load_weight(w2_raw, w2, 1)
@@ -65,10 +66,10 @@ def tile_picked_wgmem_relu_lo_kernel(tc, x_words, x_scales, mem, w1, w2, slot, o
         def dealt_tiles(name):
             return [sb(name + "_groups01", [P, 2, P, PACK], BF16), sb(name + "_groups23", [P, 2, P, PACK], BF16)]
 
-        def deal(engine_copy, dealt, raw, h, t0):
+        def deal(engine_copy, dealt, raw, pair, t0):
             engine_copy(
-                dealt[:, :, :, 2 * h : 2 * h + 2].rearrange("p t m j -> p m t j"),
-                raw[h][:, :, :].rearrange("p j (m t) -> p m t j", t=PACK)[:, :, t0 : t0 + dealt.shape[1], :],
+                dealt[:, :, :, 2 * pair : 2 * pair + 2].rearrange("p t m j -> p m t j"),
+                raw[pair][:, :, :].rearrange("p j (m t) -> p m t j", t=PACK)[:, :, t0 : t0 + dealt.shape[1], :],
             )
 
         def quantise(name, dealt):
@@ -135,9 +136,9 @@ def tile_picked_wgmem_relu_lo_kernel(tc, x_words, x_scales, mem, w1, w2, slot, o
         nc.vector.tensor_copy(old[0][:], window[0][:].indirect(offsets[:]))
 
         w1_dealt = dealt_tiles("w1")
-        for h in range(2):
-            deal(nc.vector.tensor_copy, w1_dealt[0], w1_raw, h, 0)
-            deal(nc.scalar.copy, w1_dealt[1], w1_raw, h, 2)
+        for pair in range(2):
+            deal(nc.vector.tensor_copy, w1_dealt[0], w1_raw, pair, 0)
+            deal(nc.scalar.copy, w1_dealt[1], w1_raw, pair, 2)
         y01_weights = quantise("y01", w1_dealt[0])
         y_acc = {0: multiply(y01_weights[0], 0, everything)}
         y_acc[1] = multiply_turned(y01_weights[1], 6)
@@ -150,8 +151,8 @@ def tile_picked_wgmem_relu_lo_kernel(tc, x_words, x_scales, mem, w1, w2, slot, o
         deal(nc.vector.tensor_copy, w2_dealt[0], w2_raw, 0, 0)
         deal(nc.scalar.copy, w2_dealt[1], w2_raw, 0, 2)
         nc.vector.scalar_tensor_tensor(gap[0][:], y_acc[0][:], 0.0, old[0][:], ALU.max, ALU.subtract)
-        for i in range(2):
-            deal(nc.vector.tensor_copy, w2_groups[i], w2_raw, 1, i)
+        for t in range(2):
+            deal(nc.vector.tensor_copy, w2_groups[t], w2_raw, 1, t)
         deal(nc.scalar.copy, w2_dealt[1], w2_raw, 1, 2)
         u0_weights = quantise("u0", w2_groups[0])[0]
         u0_halves = [multiply(u0_weights, 1, halves[0])]
@@ -260,8 +261,9 @@ def tile_picked_wgmem_relu_lo_kernel(tc, x_words, x_scales, mem, w1, w2, slot, o
         for quarter in quarters:
             pack(high, HALF_U, quarter)
             pack(low, 0, quarter)
-        for q in range(QUADRANTS):
-            queue = nc.scalar if q % 2 else nc.sync
+        for quadrant in range(QUADRANTS):
+            queue = nc.scalar if quadrant % 2 else nc.sync
             queue.dma_start(
-                out_2[0, 4 * q : 4 * q + 4, :].bitcast(I32), out_scale_tile[32 * q : 32 * q + 4, :].bitcast(I32)
+                out_2[0, 4 * quadrant : 4 * quadrant + 4, :].bitcast(I32),
+                out_scale_tile[32 * quadrant : 32 * quadrant + 4, :].bitcast(I32),
             )

@@ -1,7 +1,6 @@
 from contextlib import ExitStack
 
 import concourse.mybir as mybir
-from concourse.masks import make_identity
 
 K, T, N, U = 512, 512, 512, 1024
 FLOPS = 2 * 2 * K * N * T
@@ -18,11 +17,9 @@ ACT = mybir.ActivationFunctionType
 
 P = 128
 PACK = 4
-LAST = PACK - 1
 QUADRANTS = 4
 ENTRIES_PER_COLUMN = 16
 HALF_T = T // 2
-HALF_U = U // 2
 QUARTER_U = U // 4
 
 
@@ -47,81 +44,63 @@ def tile_picked_wgmem_relu_lo_kernel(tc, x_words, x_scales, mem, w1, w2, slot, o
         def load_weight(raw, w, pair):
             nc.sync.dma_start(raw[pair][:, :, :], w.rearrange("(p j) n -> p j n", j=PACK)[:, 2 * pair : 2 * pair + 2, :])
 
-        nc.vector.memset(x_scale_tile[:].bitcast(I32), 0)
-        nc.sync.dma_start(window[0][:], mem_rows[0])
-        nc.sync.dma_start(offsets[:], slot)
-        load_weight(w1_raw, w1, 0)
-        load_weight(w1_raw, w1, 1)
+        nc.gpsimd.memset(x_scale_tile[:].bitcast(I32), 0)
+        load_weight(w2_raw, w2, 0)
+        load_weight(w2_raw, w2, 1)
+        nc.sync.dma_start(x_codes[:].bitcast(I32), x_words[0].rearrange("p n r -> p (n r)").bitcast(I32))
         for quadrant in range(QUADRANTS):
             nc.sync.dma_start(
                 x_scale_tile[32 * quadrant : 32 * quadrant + 4, :].bitcast(I32),
                 x_scales[0, 4 * quadrant : 4 * quadrant + 4, :].bitcast(I32),
             )
-        nc.sync.dma_start(x_codes[:].bitcast(I32), x_words[0].rearrange("p n r -> p (n r)").bitcast(I32))
-        load_weight(w2_raw, w2, 0)
-        load_weight(w2_raw, w2, 1)
-        for t in range(1, PACK):
+        load_weight(w1_raw, w1, 0)
+        load_weight(w1_raw, w1, 1)
+        nc.sync.dma_start(offsets[:], slot)
+        for t in range(PACK):
             nc.sync.dma_start(window[t][:], mem_rows[t])
 
-        def dealt_tiles(name):
-            return [sb(name + "_groups01", [P, 2, P, PACK], BF16), sb(name + "_groups23", [P, 2, P, PACK], BF16)]
-
-        def deal(engine_copy, dealt, raw, pair, t0):
-            engine_copy(
-                dealt[:, :, :, 2 * pair : 2 * pair + 2].rearrange("p t m j -> p m t j"),
-                raw[pair][:, :, :].rearrange("p j (m t) -> p m t j", t=PACK)[:, :, t0 : t0 + dealt.shape[1], :],
+        def deal(copy, dealt, raw, pair, t0, groups):
+            copy(
+                dealt[:, t0 : t0 + groups, :, 2 * pair : 2 * pair + 2].rearrange("p t m j -> p m t j"),
+                raw[pair][:, :, :].rearrange("p j (m t) -> p m t j", t=PACK)[:, :, t0 : t0 + groups, :],
             )
 
-        def quantise(name, dealt):
-            groups = dealt.shape[1]
+        def quantise(name, dealt, t0, groups):
             codes = sb(name + "_codes", [P, groups * P], U32)
             scales = sb(name + "_scales", [P, groups * P], U8)
             nc.vector.quantize_mx(
-                out=codes[:].bitcast(FP8X4), scales=scales[:], in_=dealt[:, :, :, :].rearrange("p t m j -> p (t m j)")
+                out=codes[:].bitcast(FP8X4),
+                scales=scales[:],
+                in_=dealt[:, t0 : t0 + groups, :, :].rearrange("p t m j -> p (t m j)"),
             )
             return [(codes[:, i * P : (i + 1) * P], scales[:, i * P : (i + 1) * P]) for i in range(groups)]
 
-        def multiply(weights, bank, messages):
-            acc = psum.tile([P, messages.stop - messages.start], F32, name="acc", tag="bank%d" % bank)
+        def multiply(weights, bank):
+            acc = psum.tile([P, T], F32, name="acc", tag="bank%d" % bank)
             nc.tensor.matmul_mx(
                 out=acc[:],
                 lhsT=weights[0].bitcast(FP8X4),
                 lhsT_scale=weights[1],
-                rhs=x_codes[:, messages].bitcast(FP8X4),
-                rhs_scale=x_scale_tile[:, messages],
+                rhs=x_codes[:].bitcast(FP8X4),
+                rhs_scale=x_scale_tile[:],
                 start=True,
                 stop=True,
             )
             return acc
 
-        identity = sb("identity", [P, P], F32)
-        blocks = [slice(b * P, (b + 1) * P) for b in range(T // P)]
+        def project(name, raw, first_bank, copy23):
+            dealt = sb(name + "_dealt", [P, PACK, P, PACK], BF16)
+            deal(nc.vector.tensor_copy, dealt, raw, 0, 0, 2)
+            deal(copy23, dealt, raw, 0, 2, 2)
+            deal(nc.vector.tensor_copy, dealt, raw, 1, 0, 1)
+            deal(nc.vector.tensor_copy, dealt, raw, 1, 1, 1)
+            accs = [multiply(quantise(name + "0", dealt, 0, 1)[0], first_bank)]
+            deal(copy23, dealt, raw, 1, 2, 2)
+            accs.append(multiply(quantise(name + "1", dealt, 1, 1)[0], first_bank + 1))
+            for i, weights in enumerate(quantise(name + "2", dealt, 2, 2)):
+                accs.append(multiply(weights, first_bank + 2 + i))
+            return accs
 
-        def turn(terms, bank):
-            width = terms[0].shape[1]
-            acc = psum.tile([P, width], F32, name="acc", tag="bank%d" % bank)
-            for block in blocks[0 : width // P]:
-                for i, term in enumerate(terms):
-                    nc.tensor.matmul(
-                        acc[:, block], term[:, block], identity[:], start=i == 0, stop=i == len(terms) - 1, is_transpose=True
-                    )
-            return acc
-
-        def multiply_turned(weights, bank):
-            acc = psum.tile([P, T], F32, name="acc", tag="bank%d" % bank)
-            for block in blocks:
-                nc.tensor.matmul_mx(
-                    out=acc[:, block],
-                    lhsT=x_codes[:, block].bitcast(FP8X4),
-                    lhsT_scale=x_scale_tile[:, block],
-                    rhs=weights[0].bitcast(FP8X4),
-                    rhs_scale=weights[1],
-                    start=True,
-                    stop=True,
-                )
-            return acc
-
-        everything = slice(0, T)
         halves = [slice(h * HALF_T, (h + 1) * HALF_T) for h in range(2)]
         offset_halves = [
             offsets[:, half.start // ENTRIES_PER_COLUMN : half.stop // ENTRIES_PER_COLUMN] for half in halves
@@ -130,137 +109,95 @@ def tile_picked_wgmem_relu_lo_kernel(tc, x_words, x_scales, mem, w1, w2, slot, o
         warm = sb("warm", [P, 2], F32)
         nc.gpsimd.memset(warm[:, 0:1], 0.0)
         nc.scalar.activation(warm[:, 1:2], warm[:, 0:1], ACT.Sigmoid)
-        make_identity(nc, identity[:])
 
-        old = {t: sb("old%d" % t, [P, T], F32) for t in range(PACK)}
-        nc.vector.tensor_copy(old[0][:], window[0][:].indirect(offsets[:]))
+        u_acc = project("u", w2_raw, 0, nc.scalar.copy)
+        gate = [sb("gate%d" % t, [P, T], F32) for t in range(PACK)]
+        for t in range(PACK):
+            nc.scalar.activation(gate[t][:], u_acc[t][:], ACT.Sigmoid)
+        y_acc = project("y", w1_raw, PACK, nc.vector.tensor_copy)
 
-        w1_dealt = dealt_tiles("w1")
-        for pair in range(2):
-            deal(nc.vector.tensor_copy, w1_dealt[0], w1_raw, pair, 0)
-            deal(nc.scalar.copy, w1_dealt[1], w1_raw, pair, 2)
-        y01_weights = quantise("y01", w1_dealt[0])
-        y_acc = {0: multiply(y01_weights[0], 0, everything)}
-        y_acc[1] = multiply_turned(y01_weights[1], 6)
-        y23_weights = quantise("y23", w1_dealt[1])
-        y_acc[2] = multiply_turned(y23_weights[0], 7)
+        gap0 = sb("gap0", [P, T], F32)
+        step0 = [sb("step0_%d" % h, [P, HALF_T], F32) for h in range(2)]
+        old0 = sb("old0", [P, T], F32)
+        new = [sb("new%d" % t, [P, T], F32) for t in range(3)]
+        planes = sb("planes", [P, PACK, U], F32)
 
-        gap = {t: sb("gap%d" % t, [P, T], F32) for t in range(LAST)}
-        w2_dealt = dealt_tiles("w2")
-        w2_groups = [w2_dealt[0][:, 0:1], w2_dealt[0][:, 1:2]]
-        deal(nc.vector.tensor_copy, w2_dealt[0], w2_raw, 0, 0)
-        deal(nc.scalar.copy, w2_dealt[1], w2_raw, 0, 2)
-        nc.vector.scalar_tensor_tensor(gap[0][:], y_acc[0][:], 0.0, old[0][:], ALU.max, ALU.subtract)
-        for t in range(2):
-            deal(nc.vector.tensor_copy, w2_groups[t], w2_raw, 1, t)
-        deal(nc.scalar.copy, w2_dealt[1], w2_raw, 1, 2)
-        u0_weights = quantise("u0", w2_groups[0])[0]
-        u0_halves = [multiply(u0_weights, 1, halves[0])]
-        u_acc = {1: multiply(quantise("u1", w2_groups[1])[0], 2, everything)}
-        u0_halves.append(multiply(u0_weights, 5, halves[1]))
-        u23_weights = quantise("u23", w2_dealt[1])
-        u_acc[2] = multiply(u23_weights[0], 3, everything)
-        for t in range(1, PACK):
-            nc.vector.tensor_copy(old[t][:], window[t][:].indirect(offsets[:]))
+        def form_gap(out, t, part, old):
+            nc.vector.scalar_tensor_tensor(out, y_acc[t][:, part], 0.0, old, ALU.max, ALU.subtract)
 
-        gate = {t: sb("gate%d" % t, [P, T], F32) for t in range(2)}
-        candidate = {1: sb("candidate1", [P, T], F32, reuses="w2_raw1")}
-        new = {t: sb("new%d" % t, [P, T], F32) for t in range(1, LAST)}
-        nc.scalar.activation(candidate[1][:], y_acc[1][:], ACT.Relu)
-        nc.scalar.activation(gate[0][:, halves[0]], u0_halves[0][:], ACT.Sigmoid)
-        nc.scalar.activation(gate[1][:], u_acc[1][:], ACT.Sigmoid)
-        nc.scalar.activation(gate[0][:, halves[1]], u0_halves[1][:], ACT.Sigmoid)
-
-        def form_step0(h):
-            step0 = sb("step0_%d" % h, [P, HALF_T], F32)
-            nc.gpsimd.tensor_tensor(step0[:], gap[0][:, halves[h]], gate[0][:, halves[h]], ALU.mult)
-            return step0
-
-        def scatter0(h, step0, reuses=None):
-            new0 = sb("new0_%d" % h, [P, HALF_T], F32, reuses=reuses)
-            nc.gpsimd.tensor_tensor(new0[:], old[0][:, halves[h]], step0[:], ALU.add)
-            nc.vector.tensor_copy(window[0][:].indirect(offset_halves[h]), new0[:])
-
-        scatter0(0, form_step0(0))
-        second_step0 = form_step0(1)
-
-        candidate[2] = sb("candidate2", [P, T], F32, reuses="u0_codes")
-        nc.scalar.activation(candidate[2][:, halves[0]], y_acc[2][:, halves[0]], ACT.Relu)
-        old1_turned = [turn([old[1][:, halves[h]]], (6, 4)[h]) for h in range(2)]
-        y_acc[LAST] = multiply(y23_weights[1], 2, everything)
-        minus_old1 = [sb("minus_old1_%d" % h, [P, HALF_T], F32) for h in range(2)]
-        for h in range(2):
-            nc.scalar.activation(minus_old1[h][:], old1_turned[h][:], ACT.Copy, scale=-1.0)
-        for h in range(2):
-            nc.scalar.copy(gap[1][:, halves[h]], turn([candidate[1][:, halves[h]], minus_old1[h][:]], (5, 0)[h])[:])
-        nc.scalar.activation(candidate[2][:, halves[1]], y_acc[2][:, halves[1]], ACT.Relu)
-        scatter0(1, second_step0, reuses="minus_old1_0")
-        nc.sync.dma_start(out_rows[0], window[0][:])
-
-        later = sb("later", [P, 3, T], F32, reuses="minus_old1_1")
-        gate[2], candidate[LAST], gate[LAST] = (later[:, i, :] for i in range(3))
-        minus_old2 = sb("minus_old2", [P, T], F32)
-        nc.scalar.activation(minus_old2[:], turn([old[2][:]], 6)[:], ACT.Copy, scale=-1.0)
-        gap2_sum = turn([candidate[2][:], minus_old2[:]], 1)
-        u_acc[LAST] = multiply(u23_weights[1], 5, everything)
-        nc.scalar.activation(gate[2][:], u_acc[2][:], ACT.Sigmoid)
-        nc.scalar.activation(candidate[LAST][:], y_acc[LAST][:], ACT.Relu)
-        nc.scalar.copy(gap[2][:], gap2_sum[:])
-        nc.scalar.activation(gate[LAST][:], u_acc[LAST][:], ACT.Sigmoid)
-
-        step = {}
-        for t in range(1, PACK):
-            if t == LAST:
-                gap[t] = sb("gap%d" % t, [P, T], F32, reuses="old2")
-                nc.gpsimd.tensor_tensor(gap[t][:], candidate[t][:], old[t][:], ALU.subtract)
-            step[t] = sb("step%d" % t, [P, T], F32)
-            nc.gpsimd.tensor_tensor(step[t][:], gap[t][:], gate[t][:], ALU.mult)
-            if t < LAST:
-                nc.gpsimd.tensor_tensor(new[t][:], old[t][:], step[t][:], ALU.add)
-
-        low = sb("low", [P, HALF_U, PACK], BF16, reuses="minus_old2")
-        high = sb("high", [P, HALF_U, PACK], BF16, reuses="identity")
-
-        def regroup(t):
-            if t == LAST - 1:
-                nc.scalar.copy(
-                    high[:, :, t : t + 2], window[t][:, HALF_U:U].unsqueeze(2).to_broadcast([P, HALF_U, 2])
-                )
-            else:
-                nc.scalar.copy(high[:, :, t], window[t][:, HALF_U:U])
-            nc.scalar.copy(low[:, :, t], window[t][:, 0:HALF_U])
-
-        for t in range(1, PACK):
-            regroup(t - 1)
-            if t < LAST:
-                nc.vector.tensor_copy(window[t][:].indirect(offsets[:]), new[t][:])
-            else:
-                nc.vector.tensor_tensor(window[t][:].indirect(offsets[:]), old[t][:], step[t][:], ALU.add)
+        def scalar_scatter(t):
+            for h in range(2):
+                nc.scalar.activation(window[t][:].indirect(offset_halves[h]), new[t][:, halves[h]], ACT.Copy)
             nc.sync.dma_start(out_rows[t], window[t][:])
+
+        everything = slice(0, T)
+        for h in range(2):
+            nc.scalar.activation(old0[:, halves[h]], window[0][:].indirect(offset_halves[h]), ACT.Copy)
+        old1 = [sb("old1_0", [P, HALF_T], F32)]
+        nc.scalar.activation(old1[0][:], window[1][:].indirect(offset_halves[0]), ACT.Copy)
+        for h in range(2):
+            form_gap(gap0[:, halves[h]], 0, halves[h], old0[:, halves[h]])
+        for h in range(2):
+            nc.vector.tensor_tensor(step0[h][:], gap0[:, halves[h]], gate[0][:, halves[h]], ALU.mult)
+        for h in range(2):
+            nc.vector.tensor_tensor(new[0][:, halves[h]], old0[:, halves[h]], step0[h][:], ALU.add)
+        scalar_scatter(0)
+        nc.sync.dma_start(planes[:, 0, :], window[0][:])
+
+        gap1 = [sb("gap1_0", [P, HALF_T], F32, reuses="step0_1"), sb("gap1_1", [P, HALF_T], F32)]
+        form_gap(gap1[0][:], 1, halves[0], old1[0][:])
+        old1.append(sb("old1_1", [P, HALF_T], F32, reuses="old0"))
+        nc.vector.tensor_copy(old1[1][:], window[1][:].indirect(offset_halves[1]))
+        form_gap(gap1[1][:], 1, halves[1], old1[1][:])
+        for h in range(2):
+            step1 = sb("step1_%d" % h, [P, HALF_T], F32)
+            nc.gpsimd.tensor_tensor(step1[:], gap1[h][:], gate[1][:, halves[h]], ALU.mult)
+            nc.gpsimd.tensor_tensor(new[1][:, halves[h]], old1[h][:], step1[:], ALU.add)
+        scalar_scatter(1)
+        nc.sync.dma_start(planes[:, 1, :], window[1][:])
+        old, gap = {}, {}
+        step = {t: sb("step%d" % t, [P, T], F32) for t in range(2, PACK)}
+        for t, reuses in ((2, "step0_1"), (3, "gap1_1")):
+            old[t] = sb("old%d" % t, [P, T], F32, reuses=reuses)
+            gap[t] = sb("gap%d" % t, [P, T], F32)
+            nc.vector.tensor_copy(old[t][:], window[t][:].indirect(offsets[:]))
+            form_gap(gap[t][:], t, everything, old[t][:])
+        nc.gpsimd.tensor_tensor(step[2][:], gap[2][:], gate[2][:], ALU.mult)
+        nc.vector.tensor_tensor(step[3][:], gap[3][:], gate[3][:], ALU.mult)
+        nc.vector.tensor_tensor(new[2][:], old[2][:], step[2][:], ALU.add)
+        nc.vector.tensor_tensor(window[3][:].indirect(offsets[:]), old[3][:], step[3][:], ALU.add)
+        nc.sync.dma_start(out_rows[3], window[3][:])
+        nc.vector.tensor_copy(planes[:, 3, :], window[3][:])
+        scalar_scatter(2)
 
         out_scale_tile = sb("out_scale_tile", [P, U], U8)
         out_words = out_1[0].rearrange("p c r -> p (c r)").bitcast(I32)
-        quarters = [slice(i * QUARTER_U, (i + 1) * QUARTER_U) for i in range(2)]
+        quarters = [slice(i * QUARTER_U, (i + 1) * QUARTER_U) for i in range(4)]
+        woven = [sb("woven%d" % i, [P, QUARTER_U, PACK], BF16) for i in range(4)]
 
-        def pack(rounded, first_slot, quarter):
-            slots = slice(first_slot + quarter.start, first_slot + quarter.stop)
-            codes = sb("out_codes%d" % slots.start, [P, QUARTER_U], U32)
+        def weave(copy, i):
+            copy(
+                woven[i][:, :, :].rearrange("p (c i) t -> p c t i", i=4),
+                planes[:, :, quarters[i]].rearrange("p t (c i) -> p c t i", i=4),
+            )
+
+        def pack(i):
+            codes = sb("out_codes%d" % i, [P, QUARTER_U], U32)
             nc.vector.quantize_mx(
                 out=codes[:].bitcast(FP8X4),
-                scales=out_scale_tile[:, slots],
-                in_=rounded[:, quarter, :].rearrange("p c t -> p (c t)"),
+                scales=out_scale_tile[:, quarters[i]],
+                in_=woven[i][:, :, :].rearrange("p c t -> p (c t)"),
             )
-            nc.sync.dma_start(out_words[:, slots], codes[:].bitcast(I32))
+            nc.sync.dma_start(out_words[:, quarters[i]], codes[:].bitcast(I32))
 
-        for quarter in quarters:
-            nc.scalar.copy(low[:, quarter, LAST], window[LAST][:, quarter])
-        for quarter in quarters:
-            nc.vector.tensor_copy(
-                high[:, quarter, LAST], window[LAST][:, HALF_U + quarter.start : HALF_U + quarter.stop]
-            )
-        for quarter in quarters:
-            pack(high, HALF_U, quarter)
-            pack(low, 0, quarter)
+        nc.scalar.copy(planes[:, 2, 0 : U // 2], window[2][:, 0 : U // 2])
+        nc.vector.tensor_copy(planes[:, 2, U // 2 : U], window[2][:, U // 2 : U])
+        weave(nc.scalar.copy, 0)
+        weave(nc.vector.tensor_copy, 2)
+        weave(nc.scalar.copy, 1)
+        weave(nc.vector.tensor_copy, 3)
+        for i in (2, 0, 3, 1):
+            pack(i)
         for quadrant in range(QUADRANTS):
             queue = nc.scalar if quadrant % 2 else nc.sync
             queue.dma_start(

@@ -21,6 +21,7 @@ QUADRANTS = 4
 ENTRIES_PER_COLUMN = 16
 HALF_T = T // 2
 QUARTER_U = U // 4
+VECTOR_PIECE = 128
 
 
 def tile_picked_wgmem_relu_lo_kernel(tc, x_words, x_scales, mem, w1, w2, slot, out_0, out_1, out_2):
@@ -59,19 +60,18 @@ def tile_picked_wgmem_relu_lo_kernel(tc, x_words, x_scales, mem, w1, w2, slot, o
         for t in range(PACK):
             nc.sync.dma_start(window[t][:], mem_rows[t])
 
-        def deal(copy, dealt, raw, pair, t0, groups):
+        def deal(copy, dealt, raw, pair, t0):
             copy(
-                dealt[:, t0 : t0 + groups, :, 2 * pair : 2 * pair + 2].rearrange("p t m j -> p m t j"),
-                raw[pair][:, :, :].rearrange("p j (m t) -> p m t j", t=PACK)[:, :, t0 : t0 + groups, :],
+                dealt[:, :, :, 2 * pair : 2 * pair + 2].rearrange("p t m j -> p m t j"),
+                raw[pair][:, :, :].rearrange("p j (m t) -> p m t j", t=PACK)[:, :, t0 : t0 + dealt.shape[1], :],
             )
 
-        def quantise(name, dealt, t0, groups):
+        def quantise(name, dealt):
+            groups = dealt.shape[1]
             codes = sb(name + "_codes", [P, groups * P], U32)
             scales = sb(name + "_scales", [P, groups * P], U8)
             nc.vector.quantize_mx(
-                out=codes[:].bitcast(FP8X4),
-                scales=scales[:],
-                in_=dealt[:, t0 : t0 + groups, :, :].rearrange("p t m j -> p (t m j)"),
+                out=codes[:].bitcast(FP8X4), scales=scales[:], in_=dealt[:, :, :, :].rearrange("p t m j -> p (t m j)")
             )
             return [(codes[:, i * P : (i + 1) * P], scales[:, i * P : (i + 1) * P]) for i in range(groups)]
 
@@ -88,18 +88,20 @@ def tile_picked_wgmem_relu_lo_kernel(tc, x_words, x_scales, mem, w1, w2, slot, o
             )
             return acc
 
-        def project(name, raw, first_bank, copy23):
-            dealt = sb(name + "_dealt", [P, PACK, P, PACK], BF16)
-            deal(nc.vector.tensor_copy, dealt, raw, 0, 0, 2)
-            deal(copy23, dealt, raw, 0, 2, 2)
-            deal(nc.vector.tensor_copy, dealt, raw, 1, 0, 1)
-            deal(nc.vector.tensor_copy, dealt, raw, 1, 1, 1)
-            accs = [multiply(quantise(name + "0", dealt, 0, 1)[0], first_bank)]
-            deal(copy23, dealt, raw, 1, 2, 2)
-            accs.append(multiply(quantise(name + "1", dealt, 1, 1)[0], first_bank + 1))
-            for i, weights in enumerate(quantise(name + "2", dealt, 2, 2)):
-                accs.append(multiply(weights, first_bank + 2 + i))
-            return accs
+        def project(name, raw, first_bank, copy23, reuses=(None, None)):
+            dealt01 = sb(name + "_dealt01", [P, 2, P, PACK], BF16, reuses=reuses[0])
+            dealt23 = sb(name + "_dealt23", [P, 2, P, PACK], BF16, reuses=reuses[1])
+            deal(nc.vector.tensor_copy, dealt01, raw, 0, 0)
+            deal(copy23, dealt23, raw, 0, 2)
+            for t in range(2):
+                deal(nc.vector.tensor_copy, dealt01[:, t : t + 1], raw, 1, t)
+            deal(copy23, dealt23, raw, 1, 2)
+            weights = [quantise("%s%d" % (name, t), dealt01[:, t : t + 1])[0] for t in range(2)]
+            accs = [multiply(weights[t], first_bank + t) for t in range(2)]
+            return accs, dealt23
+
+        def project23(name, dealt23, first_bank):
+            return [multiply(weights, first_bank + 2 + i) for i, weights in enumerate(quantise(name + "23", dealt23))]
 
         halves = [slice(h * HALF_T, (h + 1) * HALF_T) for h in range(2)]
         offset_halves = [
@@ -110,65 +112,68 @@ def tile_picked_wgmem_relu_lo_kernel(tc, x_words, x_scales, mem, w1, w2, slot, o
         nc.gpsimd.memset(warm[:, 0:1], 0.0)
         nc.scalar.activation(warm[:, 1:2], warm[:, 0:1], ACT.Sigmoid)
 
-        u_acc = project("u", w2_raw, 0, nc.scalar.copy)
+        u_acc, dealt23 = project("u", w2_raw, 0, nc.scalar.copy)
+        u_acc = u_acc + project23("u", dealt23, 0)
         gate = [sb("gate%d" % t, [P, T], F32) for t in range(PACK)]
         for t in range(PACK):
             nc.scalar.activation(gate[t][:], u_acc[t][:], ACT.Sigmoid)
-        y_acc = project("y", w1_raw, PACK, nc.vector.tensor_copy)
+        y_acc, dealt23 = project("y", w1_raw, PACK, nc.vector.tensor_copy, ("u_dealt23", "w2_raw1"))
 
         gap0 = sb("gap0", [P, T], F32)
         step0 = [sb("step0_%d" % h, [P, HALF_T], F32) for h in range(2)]
-        old0 = sb("old0", [P, T], F32)
+        late_old = sb("late_old", [P, HALF_T + T], F32, reuses="w1_raw1")
+        old0 = [sb("old0_0", [P, HALF_T], F32, reuses="u_dealt23"), late_old[:, 0:HALF_T]]
         new = [sb("new%d" % t, [P, T], F32) for t in range(3)]
         planes = sb("planes", [P, PACK, U], F32)
 
         def form_gap(out, t, part, old):
             nc.vector.scalar_tensor_tensor(out, y_acc[t][:, part], 0.0, old, ALU.max, ALU.subtract)
 
-        def scalar_scatter(t):
-            for h in range(2):
-                nc.scalar.activation(window[t][:].indirect(offset_halves[h]), new[t][:, halves[h]], ACT.Copy)
+        def entries(part):
+            return offsets[:, part.start // ENTRIES_PER_COLUMN : part.stop // ENTRIES_PER_COLUMN]
+
+        def scalar_scatter(t, parts=halves):
+            for part in parts:
+                nc.scalar.activation(window[t][:].indirect(entries(part)), new[t][:, part], ACT.Copy)
             nc.sync.dma_start(out_rows[t], window[t][:])
 
         everything = slice(0, T)
+        nc.vector.tensor_copy(old0[0][:], window[0][:].indirect(offset_halves[0]))
+        y_acc = y_acc + project23("y", dealt23, PACK)
+        nc.scalar.activation(old0[1][:], window[0][:].indirect(offset_halves[1]), ACT.Copy)
+        old = {1: late_old[:, HALF_T:]}
+        nc.scalar.activation(old[1][:], window[1][:].indirect(offsets[:]), ACT.Copy)
         for h in range(2):
-            nc.scalar.activation(old0[:, halves[h]], window[0][:].indirect(offset_halves[h]), ACT.Copy)
-        old1 = [sb("old1_0", [P, HALF_T], F32)]
-        nc.scalar.activation(old1[0][:], window[1][:].indirect(offset_halves[0]), ACT.Copy)
-        for h in range(2):
-            form_gap(gap0[:, halves[h]], 0, halves[h], old0[:, halves[h]])
+            form_gap(gap0[:, halves[h]], 0, halves[h], old0[h][:])
         for h in range(2):
             nc.vector.tensor_tensor(step0[h][:], gap0[:, halves[h]], gate[0][:, halves[h]], ALU.mult)
-        for h in range(2):
-            nc.vector.tensor_tensor(new[0][:, halves[h]], old0[:, halves[h]], step0[h][:], ALU.add)
+        for h, engine in enumerate((nc.vector, nc.gpsimd)):
+            engine.tensor_tensor(new[0][:, halves[h]], old0[h][:], step0[h][:], ALU.add)
         scalar_scatter(0)
         nc.sync.dma_start(planes[:, 0, :], window[0][:])
 
-        gap1 = [sb("gap1_0", [P, HALF_T], F32, reuses="step0_1"), sb("gap1_1", [P, HALF_T], F32)]
-        form_gap(gap1[0][:], 1, halves[0], old1[0][:])
-        old1.append(sb("old1_1", [P, HALF_T], F32, reuses="old0"))
-        nc.vector.tensor_copy(old1[1][:], window[1][:].indirect(offset_halves[1]))
-        form_gap(gap1[1][:], 1, halves[1], old1[1][:])
-        for h in range(2):
-            step1 = sb("step1_%d" % h, [P, HALF_T], F32)
-            nc.gpsimd.tensor_tensor(step1[:], gap1[h][:], gate[1][:, halves[h]], ALU.mult)
-            nc.gpsimd.tensor_tensor(new[1][:, halves[h]], old1[h][:], step1[:], ALU.add)
+        gap = {1: sb("gap1", [P, T], F32, reuses="step0_0")}
+        step = {t: sb("step%d" % t, [P, T], F32) for t in range(1, PACK)}
+        form_gap(gap[1][:], 1, everything, old[1][:])
+        nc.gpsimd.tensor_tensor(step[1][:], gap[1][:], gate[1][:], ALU.mult)
+        nc.gpsimd.tensor_tensor(new[1][:], old[1][:], step[1][:], ALU.add)
         scalar_scatter(1)
         nc.sync.dma_start(planes[:, 1, :], window[1][:])
-        old, gap = {}, {}
-        step = {t: sb("step%d" % t, [P, T], F32) for t in range(2, PACK)}
-        for t, reuses in ((2, "step0_1"), (3, "gap1_1")):
+        for t, reuses in ((2, "u_dealt23"), (3, "gate1")):
             old[t] = sb("old%d" % t, [P, T], F32, reuses=reuses)
             gap[t] = sb("gap%d" % t, [P, T], F32)
             nc.vector.tensor_copy(old[t][:], window[t][:].indirect(offsets[:]))
             form_gap(gap[t][:], t, everything, old[t][:])
         nc.gpsimd.tensor_tensor(step[2][:], gap[2][:], gate[2][:], ALU.mult)
         nc.vector.tensor_tensor(step[3][:], gap[3][:], gate[3][:], ALU.mult)
-        nc.vector.tensor_tensor(new[2][:], old[2][:], step[2][:], ALU.add)
+        head, rest = slice(0, VECTOR_PIECE), slice(VECTOR_PIECE, T)
+        nc.vector.tensor_tensor(new[2][:, rest], old[2][:, rest], step[2][:, rest], ALU.add)
+        nc.vector.tensor_tensor(window[2][:].indirect(entries(head)), old[2][:, head], step[2][:, head], ALU.add)
+        scalar_scatter(2, [rest])
         nc.vector.tensor_tensor(window[3][:].indirect(offsets[:]), old[3][:], step[3][:], ALU.add)
         nc.sync.dma_start(out_rows[3], window[3][:])
+        nc.scalar.copy(planes[:, 2, :], window[2][:])
         nc.vector.tensor_copy(planes[:, 3, :], window[3][:])
-        scalar_scatter(2)
 
         out_scale_tile = sb("out_scale_tile", [P, U], U8)
         out_words = out_1[0].rearrange("p c r -> p (c r)").bitcast(I32)
@@ -177,8 +182,8 @@ def tile_picked_wgmem_relu_lo_kernel(tc, x_words, x_scales, mem, w1, w2, slot, o
 
         def weave(copy, i):
             copy(
-                woven[i][:, :, :].rearrange("p (c i) t -> p c t i", i=4),
-                planes[:, :, quarters[i]].rearrange("p t (c i) -> p c t i", i=4),
+                woven[i][:, :, :].rearrange("p (c i) (w t) -> p c w i t", i=4, t=2),
+                planes[:, :, quarters[i]].rearrange("p (w t) (c i) -> p c w i t", i=4, t=2),
             )
 
         def pack(i):
@@ -190,8 +195,6 @@ def tile_picked_wgmem_relu_lo_kernel(tc, x_words, x_scales, mem, w1, w2, slot, o
             )
             nc.sync.dma_start(out_words[:, quarters[i]], codes[:].bitcast(I32))
 
-        nc.scalar.copy(planes[:, 2, 0 : U // 2], window[2][:, 0 : U // 2])
-        nc.vector.tensor_copy(planes[:, 2, U // 2 : U], window[2][:, U // 2 : U])
         weave(nc.scalar.copy, 0)
         weave(nc.vector.tensor_copy, 2)
         weave(nc.scalar.copy, 1)

@@ -50,7 +50,7 @@ def tile_picked_wgmem_relu_lo_kernel(tc, x_words, x_scales, mem, w1, w2, slot, o
         load_weight(w2_raw, w2, 1)
         nc.sync.dma_start(x_codes[:].bitcast(I32), x_words[0].rearrange("p n r -> p (n r)").bitcast(I32))
         for quadrant in range(QUADRANTS):
-            nc.sync.dma_start(
+            nc.scalar.dma_start(
                 x_scale_tile[32 * quadrant : 32 * quadrant + 4, :].bitcast(I32),
                 x_scales[0, 4 * quadrant : 4 * quadrant + 4, :].bitcast(I32),
             )

@@ -21,6 +21,7 @@ QUADRANTS = 4
 ENTRIES_PER_COLUMN = 16
 HALF_T = T // 2
 QUARTER_U = U // 4
+SCALAR_SLOTS = 416
 VECTOR_PIECE = 128
 
 
@@ -50,7 +51,7 @@ def tile_picked_wgmem_relu_lo_kernel(tc, x_words, x_scales, mem, w1, w2, slot, o
         load_weight(w2_raw, w2, 1)
         nc.sync.dma_start(x_codes[:].bitcast(I32), x_words[0].rearrange("p n r -> p (n r)").bitcast(I32))
         for quadrant in range(QUADRANTS):
-            nc.scalar.dma_start(
+            nc.sync.dma_start(
                 x_scale_tile[32 * quadrant : 32 * quadrant + 4, :].bitcast(I32),
                 x_scales[0, 4 * quadrant : 4 * quadrant + 4, :].bitcast(I32),
             )
@@ -142,7 +143,8 @@ def tile_picked_wgmem_relu_lo_kernel(tc, x_words, x_scales, mem, w1, w2, slot, o
         y_acc = y_acc + project23("y", dealt23, PACK)
         nc.scalar.activation(old0[1][:], window[0][:].indirect(offset_halves[1]), ACT.Copy)
         old = {1: late_old[:, HALF_T:]}
-        nc.scalar.activation(old[1][:], window[1][:].indirect(offsets[:]), ACT.Copy)
+        for h in range(2):
+            nc.scalar.activation(old[1][:, halves[h]], window[1][:].indirect(offset_halves[h]), ACT.Copy)
         for h in range(2):
             form_gap(gap0[:, halves[h]], 0, halves[h], old0[h][:])
         for h in range(2):
@@ -154,16 +156,20 @@ def tile_picked_wgmem_relu_lo_kernel(tc, x_words, x_scales, mem, w1, w2, slot, o
 
         gap = {1: sb("gap1", [P, T], F32, reuses="step0_0")}
         step = {t: sb("step%d" % t, [P, T], F32) for t in range(1, PACK)}
-        form_gap(gap[1][:], 1, everything, old[1][:])
-        nc.gpsimd.tensor_tensor(step[1][:], gap[1][:], gate[1][:], ALU.mult)
+        for half in halves:
+            form_gap(gap[1][:, half], 1, half, old[1][:, half])
+        for half in halves:
+            nc.gpsimd.tensor_tensor(step[1][:, half], gap[1][:, half], gate[1][:, half], ALU.mult)
         nc.gpsimd.tensor_tensor(new[1][:], old[1][:], step[1][:], ALU.add)
         scalar_scatter(1)
         nc.sync.dma_start(planes[:, 1, :], window[1][:])
         for t, reuses in ((2, "u_dealt23"), (3, "gate1")):
             old[t] = sb("old%d" % t, [P, T], F32, reuses=reuses)
             gap[t] = sb("gap%d" % t, [P, T], F32)
-            nc.vector.tensor_copy(old[t][:], window[t][:].indirect(offsets[:]))
-            form_gap(gap[t][:], t, everything, old[t][:])
+            for h in range(2):
+                nc.vector.tensor_copy(old[t][:, halves[h]], window[t][:].indirect(offset_halves[h]))
+            for half in halves:
+                form_gap(gap[t][:, half], t, half, old[t][:, half])
         nc.gpsimd.tensor_tensor(step[2][:], gap[2][:], gate[2][:], ALU.mult)
         nc.vector.tensor_tensor(step[3][:], gap[3][:], gate[3][:], ALU.mult)
         head, rest = slice(0, VECTOR_PIECE), slice(VECTOR_PIECE, T)
@@ -172,18 +178,24 @@ def tile_picked_wgmem_relu_lo_kernel(tc, x_words, x_scales, mem, w1, w2, slot, o
         scalar_scatter(2, [rest])
         nc.vector.tensor_tensor(window[3][:].indirect(offsets[:]), old[3][:], step[3][:], ALU.add)
         nc.sync.dma_start(out_rows[3], window[3][:])
-        nc.scalar.copy(planes[:, 2, :], window[2][:])
-        nc.vector.tensor_copy(planes[:, 3, :], window[3][:])
 
         out_scale_tile = sb("out_scale_tile", [P, U], U8)
         out_words = out_1[0].rearrange("p c r -> p (c r)").bitcast(I32)
         quarters = [slice(i * QUARTER_U, (i + 1) * QUARTER_U) for i in range(4)]
         woven = [sb("woven%d" % i, [P, QUARTER_U, PACK], BF16) for i in range(4)]
+        scalar_parts = [quarters[0], slice(QUARTER_U, SCALAR_SLOTS)]
+        vector_parts = [slice(SCALAR_SLOTS, 3 * QUARTER_U), quarters[3]]
 
-        def weave(copy, i):
+        def lay(copy, t, part):
+            copy(planes[:, t, part], window[t][:, part])
+
+        def weave(copy, part):
+            i = part.start // QUARTER_U
             copy(
-                woven[i][:, :, :].rearrange("p (c i) (w t) -> p c w i t", i=4, t=2),
-                planes[:, :, quarters[i]].rearrange("p (w t) (c i) -> p c w i t", i=4, t=2),
+                woven[i][:, part.start - i * QUARTER_U : part.stop - i * QUARTER_U, :].rearrange(
+                    "p (c i) (w t) -> p c w i t", i=4, t=2
+                ),
+                planes[:, :, part].rearrange("p (w t) (c i) -> p c w i t", i=4, t=2),
             )
 
         def pack(i):
@@ -195,10 +207,16 @@ def tile_picked_wgmem_relu_lo_kernel(tc, x_words, x_scales, mem, w1, w2, slot, o
             )
             nc.sync.dma_start(out_words[:, quarters[i]], codes[:].bitcast(I32))
 
-        weave(nc.scalar.copy, 0)
-        weave(nc.vector.tensor_copy, 2)
-        weave(nc.scalar.copy, 1)
-        weave(nc.vector.tensor_copy, 3)
+        lay(nc.scalar.copy, 2, slice(0, SCALAR_SLOTS))
+        lay(nc.vector.tensor_copy, 3, slice(SCALAR_SLOTS, U))
+        for part in scalar_parts:
+            lay(nc.scalar.copy, 3, part)
+        for part in vector_parts:
+            lay(nc.vector.tensor_copy, 2, part)
+        for part in scalar_parts:
+            weave(nc.scalar.copy, part)
+        for part in (quarters[2], quarters[3], slice(SCALAR_SLOTS, 2 * QUARTER_U)):
+            weave(nc.vector.tensor_copy, part)
         for i in (2, 0, 3, 1):
             pack(i)
         for quadrant in range(QUADRANTS):

@@ -1,6 +1,7 @@
 from contextlib import ExitStack
 
 import concourse.mybir as mybir
+from concourse.masks import make_identity
 
 K, T, N, U = 512, 512, 512, 1024
 FLOPS = 2 * 2 * K * N * T
@@ -21,8 +22,9 @@ QUADRANTS = 4
 ENTRIES_PER_COLUMN = 16
 HALF_T = T // 2
 QUARTER_U = U // 4
-SCALAR_SLOTS = 416
-VECTOR_PIECE = 128
+FIRST = 224
+SCALAR_SLOTS = 448
+VECTOR_PIECE = 160
 
 
 def tile_picked_wgmem_relu_lo_kernel(tc, x_words, x_scales, mem, w1, w2, slot, out_0, out_1, out_2):
@@ -89,20 +91,38 @@ def tile_picked_wgmem_relu_lo_kernel(tc, x_words, x_scales, mem, w1, w2, slot, o
             )
             return acc
 
-        def project(name, raw, first_bank, copy23, reuses=(None, None)):
+        def project(name, raw, first_bank, copy23, together, reuses=(None, None)):
             dealt01 = sb(name + "_dealt01", [P, 2, P, PACK], BF16, reuses=reuses[0])
             dealt23 = sb(name + "_dealt23", [P, 2, P, PACK], BF16, reuses=reuses[1])
             deal(nc.vector.tensor_copy, dealt01, raw, 0, 0)
             deal(copy23, dealt23, raw, 0, 2)
-            for t in range(2):
-                deal(nc.vector.tensor_copy, dealt01[:, t : t + 1], raw, 1, t)
+            parts = [dealt01[:, t : t + together] for t in range(0, 2, together)]
+            for i, part in enumerate(parts):
+                deal(nc.vector.tensor_copy, part, raw, 1, i)
             deal(copy23, dealt23, raw, 1, 2)
-            weights = [quantise("%s%d" % (name, t), dealt01[:, t : t + 1])[0] for t in range(2)]
+            weights = [w for i, part in enumerate(parts) for w in quantise("%s%d" % (name, i), part)]
             accs = [multiply(weights[t], first_bank + t) for t in range(2)]
             return accs, dealt23
 
-        def project23(name, dealt23, first_bank):
-            return [multiply(weights, first_bank + 2 + i) for i, weights in enumerate(quantise(name + "23", dealt23))]
+        blocks = [slice(b * P, (b + 1) * P) for b in range(T // P)]
+
+        def multiply_turned(weights, bank):
+            acc = psum.tile([P, T], F32, name="acc", tag="bank%d" % bank)
+            for block in blocks:
+                nc.tensor.matmul_mx(
+                    out=acc[:, block],
+                    lhsT=x_codes[:, block].bitcast(FP8X4),
+                    lhsT_scale=x_scale_tile[:, block],
+                    rhs=weights[0].bitcast(FP8X4),
+                    rhs_scale=weights[1],
+                    start=True,
+                    stop=True,
+                )
+            return acc
+
+        def project23(name, dealt23, first_bank, last_multiply):
+            weights = quantise(name + "23", dealt23)
+            return [multiply(weights[0], first_bank + 2), last_multiply(weights[1], first_bank + 3)]
 
         halves = [slice(h * HALF_T, (h + 1) * HALF_T) for h in range(2)]
         offset_halves = [
@@ -113,17 +133,22 @@ def tile_picked_wgmem_relu_lo_kernel(tc, x_words, x_scales, mem, w1, w2, slot, o
         nc.gpsimd.memset(warm[:, 0:1], 0.0)
         nc.scalar.activation(warm[:, 1:2], warm[:, 0:1], ACT.Sigmoid)
 
-        u_acc, dealt23 = project("u", w2_raw, 0, nc.scalar.copy)
-        u_acc = u_acc + project23("u", dealt23, 0)
+        identity = sb("identity", [P, P], F32)
+        make_identity(nc, identity[:])
+
+        u_acc, dealt23 = project("u", w2_raw, 0, nc.scalar.copy, 1)
+        u_acc = u_acc + project23("u", dealt23, 0, multiply_turned)
         gate = [sb("gate%d" % t, [P, T], F32) for t in range(PACK)]
         for t in range(PACK):
             nc.scalar.activation(gate[t][:], u_acc[t][:], ACT.Sigmoid)
-        y_acc, dealt23 = project("y", w1_raw, PACK, nc.vector.tensor_copy, ("u_dealt23", "w2_raw1"))
+        y_acc, dealt23 = project("y", w1_raw, PACK, nc.vector.tensor_copy, 2, ("u_dealt23", "w2_raw1"))
 
         gap0 = sb("gap0", [P, T], F32)
-        step0 = [sb("step0_%d" % h, [P, HALF_T], F32) for h in range(2)]
-        late_old = sb("late_old", [P, HALF_T + T], F32, reuses="w1_raw1")
-        old0 = [sb("old0_0", [P, HALF_T], F32, reuses="u_dealt23"), late_old[:, 0:HALF_T]]
+        pieces0 = [slice(0, FIRST), slice(FIRST, T)]
+        second = T - FIRST
+        step0 = [sb("step0_%d" % h, [P, part.stop - part.start], F32) for h, part in enumerate(pieces0)]
+        late_old = sb("late_old", [P, second + T], F32, reuses="w1_raw1")
+        old0 = [sb("old0_0", [P, FIRST], F32, reuses="u_dealt23"), late_old[:, 0:second]]
         new = [sb("new%d" % t, [P, T], F32) for t in range(3)]
         planes = sb("planes", [P, PACK, U], F32)
 
@@ -136,23 +161,24 @@ def tile_picked_wgmem_relu_lo_kernel(tc, x_words, x_scales, mem, w1, w2, slot, o
         def scalar_scatter(t, parts=halves):
             for part in parts:
                 nc.scalar.activation(window[t][:].indirect(entries(part)), new[t][:, part], ACT.Copy)
+            if t < 2:
+                nc.sync.dma_start(planes[:, t, :], window[t][:])
             nc.sync.dma_start(out_rows[t], window[t][:])
 
         everything = slice(0, T)
-        nc.vector.tensor_copy(old0[0][:], window[0][:].indirect(offset_halves[0]))
-        y_acc = y_acc + project23("y", dealt23, PACK)
-        nc.scalar.activation(old0[1][:], window[0][:].indirect(offset_halves[1]), ACT.Copy)
-        old = {1: late_old[:, HALF_T:]}
+        nc.vector.tensor_copy(old0[0][:], window[0][:].indirect(entries(pieces0[0])))
+        y_acc = y_acc + project23("y", dealt23, PACK, multiply)
+        nc.scalar.activation(old0[1][:], window[0][:].indirect(entries(pieces0[1])), ACT.Copy)
+        old = {1: late_old[:, second:]}
         for h in range(2):
             nc.scalar.activation(old[1][:, halves[h]], window[1][:].indirect(offset_halves[h]), ACT.Copy)
         for h in range(2):
-            form_gap(gap0[:, halves[h]], 0, halves[h], old0[h][:])
+            form_gap(gap0[:, pieces0[h]], 0, pieces0[h], old0[h][:])
         for h in range(2):
-            nc.vector.tensor_tensor(step0[h][:], gap0[:, halves[h]], gate[0][:, halves[h]], ALU.mult)
+            nc.vector.tensor_tensor(step0[h][:], gap0[:, pieces0[h]], gate[0][:, pieces0[h]], ALU.mult)
         for h, engine in enumerate((nc.vector, nc.gpsimd)):
-            engine.tensor_tensor(new[0][:, halves[h]], old0[h][:], step0[h][:], ALU.add)
-        scalar_scatter(0)
-        nc.sync.dma_start(planes[:, 0, :], window[0][:])
+            engine.tensor_tensor(new[0][:, pieces0[h]], old0[h][:], step0[h][:], ALU.add)
+        scalar_scatter(0, pieces0)
 
         gap = {1: sb("gap1", [P, T], F32, reuses="step0_0")}
         step = {t: sb("step%d" % t, [P, T], F32) for t in range(1, PACK)}
@@ -162,7 +188,6 @@ def tile_picked_wgmem_relu_lo_kernel(tc, x_words, x_scales, mem, w1, w2, slot, o
             nc.gpsimd.tensor_tensor(step[1][:, half], gap[1][:, half], gate[1][:, half], ALU.mult)
         nc.gpsimd.tensor_tensor(new[1][:], old[1][:], step[1][:], ALU.add)
         scalar_scatter(1)
-        nc.sync.dma_start(planes[:, 1, :], window[1][:])
         for t, reuses in ((2, "u_dealt23"), (3, "gate1")):
             old[t] = sb("old%d" % t, [P, T], F32, reuses=reuses)
             gap[t] = sb("gap%d" % t, [P, T], F32)
@@ -170,11 +195,16 @@ def tile_picked_wgmem_relu_lo_kernel(tc, x_words, x_scales, mem, w1, w2, slot, o
                 nc.vector.tensor_copy(old[t][:, halves[h]], window[t][:].indirect(offset_halves[h]))
             for half in halves:
                 form_gap(gap[t][:, half], t, half, old[t][:, half])
-        nc.gpsimd.tensor_tensor(step[2][:], gap[2][:], gate[2][:], ALU.mult)
-        nc.vector.tensor_tensor(step[3][:], gap[3][:], gate[3][:], ALU.mult)
         head, rest = slice(0, VECTOR_PIECE), slice(VECTOR_PIECE, T)
-        nc.vector.tensor_tensor(new[2][:, rest], old[2][:, rest], step[2][:, rest], ALU.add)
-        nc.vector.tensor_tensor(window[2][:].indirect(entries(head)), old[2][:, head], step[2][:, head], ALU.add)
+        for part in (head, rest):
+            nc.gpsimd.tensor_tensor(step[2][:, part], gap[2][:, part], gate[2][:, part], ALU.mult)
+            nc.gpsimd.tensor_tensor(new[2][:, part], old[2][:, part], step[2][:, part], ALU.add)
+        gate3 = psum.tile([P, T], F32, name="acc", tag="bank4")
+        for block in blocks:
+            nc.tensor.transpose(gate3[:, block], gate[3][:, block], identity[:])
+        for half in halves:
+            nc.vector.tensor_tensor(step[3][:, half], gap[3][:, half], gate3[:, half], ALU.mult)
+        nc.vector.tensor_copy(window[2][:].indirect(entries(head)), new[2][:, head])
         scalar_scatter(2, [rest])
         nc.vector.tensor_tensor(window[3][:].indirect(offsets[:]), old[3][:], step[3][:], ALU.add)
         nc.sync.dma_start(out_rows[3], window[3][:])

@@ -138,14 +138,14 @@ def tile_picked_wgmem_relu_lo_kernel(tc, x_words, x_scales, mem, w1, w2, slot, o
 
         u_acc, dealt23 = project("u", w2_raw, 0, nc.scalar.copy, 1)
         u_acc = u_acc + project23("u", dealt23, 0, multiply_turned)
-        gate = [sb("gate%d" % t, [P, T], F32) for t in range(PACK)]
-        for t in range(PACK):
+        gate = [sb("gate%d" % t, [P, T], F32) for t in range(3)]
+        for t in range(3):
             nc.scalar.activation(gate[t][:], u_acc[t][:], ACT.Sigmoid)
         y_acc, dealt23 = project("y", w1_raw, PACK, nc.vector.tensor_copy, 2, ("u_dealt23", "w2_raw1"))
 
-        gap0 = sb("gap0", [P, T], F32)
         pieces0 = [slice(0, FIRST), slice(FIRST, T)]
         second = T - FIRST
+        gap0 = [sb("gap0_%d" % h, [P, part.stop - part.start], F32) for h, part in enumerate(pieces0)]
         step0 = [sb("step0_%d" % h, [P, part.stop - part.start], F32) for h, part in enumerate(pieces0)]
         late_old = sb("late_old", [P, second + T], F32, reuses="w1_raw1")
         old0 = [sb("old0_0", [P, FIRST], F32, reuses="u_dealt23"), late_old[:, 0:second]]
@@ -173,9 +173,11 @@ def tile_picked_wgmem_relu_lo_kernel(tc, x_words, x_scales, mem, w1, w2, slot, o
         for h in range(2):
             nc.scalar.activation(old[1][:, halves[h]], window[1][:].indirect(offset_halves[h]), ACT.Copy)
         for h in range(2):
-            form_gap(gap0[:, pieces0[h]], 0, pieces0[h], old0[h][:])
+            form_gap(gap0[h][:], 0, pieces0[h], old0[h][:])
         for h in range(2):
-            nc.vector.tensor_tensor(step0[h][:], gap0[:, pieces0[h]], gate[0][:, pieces0[h]], ALU.mult)
+            nc.vector.tensor_tensor(step0[h][:], gap0[h][:], gate[0][:, pieces0[h]], ALU.mult)
+        gate.append(sb("gate3", [P, T], F32, reuses="gap0_0"))
+        nc.scalar.activation(gate[3][:], u_acc[3][:], ACT.Sigmoid)
         for h, engine in enumerate((nc.vector, nc.gpsimd)):
             engine.tensor_tensor(new[0][:, pieces0[h]], old0[h][:], step0[h][:], ALU.add)
         scalar_scatter(0, pieces0)

@@ -22,7 +22,7 @@ QUADRANTS = 4
 ENTRIES_PER_COLUMN = 16
 HALF_T = T // 2
 QUARTER_U = U // 4
-FIRST = 224
+FIRST = 256
 SCALAR_SLOTS = 448
 VECTOR_PIECE = 160
 
@@ -78,14 +78,14 @@ def tile_picked_wgmem_relu_lo_kernel(tc, x_words, x_scales, mem, w1, w2, slot, o
             )
             return [(codes[:, i * P : (i + 1) * P], scales[:, i * P : (i + 1) * P]) for i in range(groups)]
 
-        def multiply(weights, bank):
-            acc = psum.tile([P, T], F32, name="acc", tag="bank%d" % bank)
+        def multiply(weights, bank, messages=slice(0, T)):
+            acc = psum.tile([P, messages.stop - messages.start], F32, name="acc", tag="bank%d" % bank)
             nc.tensor.matmul_mx(
                 out=acc[:],
                 lhsT=weights[0].bitcast(FP8X4),
                 lhsT_scale=weights[1],
-                rhs=x_codes[:].bitcast(FP8X4),
-                rhs_scale=x_scale_tile[:],
+                rhs=x_codes[:, messages].bitcast(FP8X4),
+                rhs_scale=x_scale_tile[:, messages],
                 start=True,
                 stop=True,
             )
@@ -101,8 +101,7 @@ def tile_picked_wgmem_relu_lo_kernel(tc, x_words, x_scales, mem, w1, w2, slot, o
                 deal(nc.vector.tensor_copy, part, raw, 1, i)
             deal(copy23, dealt23, raw, 1, 2)
             weights = [w for i, part in enumerate(parts) for w in quantise("%s%d" % (name, i), part)]
-            accs = [multiply(weights[t], first_bank + t) for t in range(2)]
-            return accs, dealt23
+            return weights, dealt23
 
         blocks = [slice(b * P, (b + 1) * P) for b in range(T // P)]
 
@@ -120,9 +119,6 @@ def tile_picked_wgmem_relu_lo_kernel(tc, x_words, x_scales, mem, w1, w2, slot, o
                 )
             return acc
 
-        def project23(name, dealt23, first_bank, last_multiply):
-            weights = quantise(name + "23", dealt23)
-            return [multiply(weights[0], first_bank + 2), last_multiply(weights[1], first_bank + 3)]
 
         halves = [slice(h * HALF_T, (h + 1) * HALF_T) for h in range(2)]
         offset_halves = [
@@ -136,12 +132,16 @@ def tile_picked_wgmem_relu_lo_kernel(tc, x_words, x_scales, mem, w1, w2, slot, o
         identity = sb("identity", [P, P], F32)
         make_identity(nc, identity[:])
 
-        u_acc, dealt23 = project("u", w2_raw, 0, nc.scalar.copy, 1)
-        u_acc = u_acc + project23("u", dealt23, 0, multiply_turned)
+        u_weights, dealt23 = project("u", w2_raw, 0, nc.scalar.copy, 1)
+        u_acc = [multiply(u_weights[t], t) for t in range(2)]
+        u_weights = u_weights + quantise("u23", dealt23)
+        u_acc.append(multiply(u_weights[2], 2))
         gate = [sb("gate%d" % t, [P, T], F32) for t in range(3)]
         for t in range(3):
             nc.scalar.activation(gate[t][:], u_acc[t][:], ACT.Sigmoid)
-        y_acc, dealt23 = project("y", w1_raw, PACK, nc.vector.tensor_copy, 2, ("u_dealt23", "w2_raw1"))
+        y_weights, dealt23 = project("y", w1_raw, PACK, nc.vector.tensor_copy, 2, ("u_dealt23", "w2_raw1"))
+        y0_halves = [multiply(y_weights[0], 3 + h, halves[h]) for h in range(2)]
+        y_acc = {1: multiply(y_weights[1], 5)}
 
         pieces0 = [slice(0, FIRST), slice(FIRST, T)]
         second = T - FIRST
@@ -152,8 +152,8 @@ def tile_picked_wgmem_relu_lo_kernel(tc, x_words, x_scales, mem, w1, w2, slot, o
         new = [sb("new%d" % t, [P, T], F32) for t in range(3)]
         planes = sb("planes", [P, PACK, U], F32)
 
-        def form_gap(out, t, part, old):
-            nc.vector.scalar_tensor_tensor(out, y_acc[t][:, part], 0.0, old, ALU.max, ALU.subtract)
+        def form_gap(out, y, old):
+            nc.vector.scalar_tensor_tensor(out, y, 0.0, old, ALU.max, ALU.subtract)
 
         def entries(part):
             return offsets[:, part.start // ENTRIES_PER_COLUMN : part.stop // ENTRIES_PER_COLUMN]
@@ -167,17 +167,18 @@ def tile_picked_wgmem_relu_lo_kernel(tc, x_words, x_scales, mem, w1, w2, slot, o
 
         everything = slice(0, T)
         nc.vector.tensor_copy(old0[0][:], window[0][:].indirect(entries(pieces0[0])))
-        y_acc = y_acc + project23("y", dealt23, PACK, multiply)
+        for i, weights in enumerate(quantise("y23", dealt23)):
+            y_acc[2 + i] = multiply(weights, 6 + i)
         nc.scalar.activation(old0[1][:], window[0][:].indirect(entries(pieces0[1])), ACT.Copy)
         old = {1: late_old[:, second:]}
         for h in range(2):
             nc.scalar.activation(old[1][:, halves[h]], window[1][:].indirect(offset_halves[h]), ACT.Copy)
         for h in range(2):
-            form_gap(gap0[h][:], 0, pieces0[h], old0[h][:])
+            form_gap(gap0[h][:], y0_halves[h][:], old0[h][:])
         for h in range(2):
             nc.vector.tensor_tensor(step0[h][:], gap0[h][:], gate[0][:, pieces0[h]], ALU.mult)
-        gate.append(sb("gate3", [P, T], F32, reuses="gap0_0"))
-        nc.scalar.activation(gate[3][:], u_acc[3][:], ACT.Sigmoid)
+        gate.append(sb("gate3", [P, T], F32))
+        nc.scalar.activation(gate[3][:], multiply_turned(u_weights[3], 3)[:], ACT.Sigmoid)
         for h, engine in enumerate((nc.vector, nc.gpsimd)):
             engine.tensor_tensor(new[0][:, pieces0[h]], old0[h][:], step0[h][:], ALU.add)
         scalar_scatter(0, pieces0)
@@ -185,7 +186,7 @@ def tile_picked_wgmem_relu_lo_kernel(tc, x_words, x_scales, mem, w1, w2, slot, o
         gap = {1: sb("gap1", [P, T], F32, reuses="step0_0")}
         step = {t: sb("step%d" % t, [P, T], F32) for t in range(1, PACK)}
         for half in halves:
-            form_gap(gap[1][:, half], 1, half, old[1][:, half])
+            form_gap(gap[1][:, half], y_acc[1][:, half], old[1][:, half])
         for half in halves:
             nc.gpsimd.tensor_tensor(step[1][:, half], gap[1][:, half], gate[1][:, half], ALU.mult)
         nc.gpsimd.tensor_tensor(new[1][:], old[1][:], step[1][:], ALU.add)
@@ -196,7 +197,7 @@ def tile_picked_wgmem_relu_lo_kernel(tc, x_words, x_scales, mem, w1, w2, slot, o
             for h in range(2):
                 nc.vector.tensor_copy(old[t][:, halves[h]], window[t][:].indirect(offset_halves[h]))
             for half in halves:
-                form_gap(gap[t][:, half], t, half, old[t][:, half])
+                form_gap(gap[t][:, half], y_acc[t][:, half], old[t][:, half])
         head, rest = slice(0, VECTOR_PIECE), slice(VECTOR_PIECE, T)
         for part in (head, rest):
             nc.gpsimd.tensor_tensor(step[2][:, part], gap[2][:, part], gate[2][:, part], ALU.mult)

from contextlib import ExitStack

import concourse.mybir as mybir
from concourse.masks import make_identity

K, T, N, U = 512, 512, 512, 1024
FLOPS = 2 * 2 * K * N * T

F32 = mybir.dt.float32
BF16 = mybir.dt.bfloat16
I32 = mybir.dt.int32
U32 = mybir.dt.uint32
U16 = mybir.dt.uint16
U8 = mybir.dt.uint8
FP8X4 = mybir.dt.float8_e4m3fn_x4
ALU = mybir.AluOpType
ACT = mybir.ActivationFunctionType

P = 128
PACK = 4
QUADRANTS = 4
ENTRIES_PER_COLUMN = 16
HALF_T = T // 2
QUARTER_U = U // 4
FIRST = 256
SCALAR_SLOTS = 448
VECTOR_PIECE = 160


def tile_picked_wgmem_relu_lo_kernel(tc, x_words, x_scales, mem, w1, w2, slot, out_0, out_1, out_2):
    nc = tc.nc
    with ExitStack() as ctx:
        keep = ctx.enter_context(tc.tile_pool(name="keep", bufs=1))
        psum = ctx.enter_context(tc.psum_pool(name="psum", bufs=1))

        def sb(name, shape, dtype, reuses=None):
            return keep.tile(shape, dtype, name=name, tag=reuses or name, align_bytes=64)

        offsets = keep.tile([P, T // ENTRIES_PER_COLUMN], U16, name="offsets")
        x_codes = sb("x_codes", [P, T], U32)
        x_scale_tile = sb("x_scale_tile", [P, T], U8)
        w1_raw = [sb("w1_raw%d" % pair, [P, 2, N], F32) for pair in range(2)]
        w2_raw = [sb("w2_raw%d" % pair, [P, 2, N], F32) for pair in range(2)]
        window = [sb("window%d" % t, [P, U], F32) for t in range(PACK)]
        mem_rows = mem.rearrange("(p t) u -> t p u", t=PACK)
        out_rows = out_0.rearrange("(p t) u -> t p u", t=PACK)

        def load_weight(raw, w, pair):
            nc.sync.dma_start(raw[pair][:, :, :], w.rearrange("(p j) n -> p j n", j=PACK)[:, 2 * pair : 2 * pair + 2, :])

        nc.gpsimd.memset(x_scale_tile[:].bitcast(I32), 0)
        load_weight(w2_raw, w2, 0)
        load_weight(w2_raw, w2, 1)
        nc.sync.dma_start(x_codes[:].bitcast(I32), x_words[0].rearrange("p n r -> p (n r)").bitcast(I32))
        for quadrant in range(QUADRANTS):
            nc.sync.dma_start(
                x_scale_tile[32 * quadrant : 32 * quadrant + 4, :].bitcast(I32),
                x_scales[0, 4 * quadrant : 4 * quadrant + 4, :].bitcast(I32),
            )
        load_weight(w1_raw, w1, 0)
        load_weight(w1_raw, w1, 1)
        nc.sync.dma_start(offsets[:], slot)
        for t in range(PACK):
            nc.sync.dma_start(window[t][:], mem_rows[t])

        def deal(copy, dealt, raw, pair, t0):
            copy(
                dealt[:, :, :, 2 * pair : 2 * pair + 2].rearrange("p t m j -> p m t j"),
                raw[pair][:, :, :].rearrange("p j (m t) -> p m t j", t=PACK)[:, :, t0 : t0 + dealt.shape[1], :],
            )

        def quantise(name, dealt):
            groups = dealt.shape[1]
            codes = sb(name + "_codes", [P, groups * P], U32)
            scales = sb(name + "_scales", [P, groups * P], U8)
            nc.vector.quantize_mx(
                out=codes[:].bitcast(FP8X4), scales=scales[:], in_=dealt[:, :, :, :].rearrange("p t m j -> p (t m j)")
            )
            return [(codes[:, i * P : (i + 1) * P], scales[:, i * P : (i + 1) * P]) for i in range(groups)]

        def multiply(weights, bank, messages=slice(0, T)):
            acc = psum.tile([P, messages.stop - messages.start], F32, name="acc", tag="bank%d" % bank)
            nc.tensor.matmul_mx(
                out=acc[:],
                lhsT=weights[0].bitcast(FP8X4),
                lhsT_scale=weights[1],
                rhs=x_codes[:, messages].bitcast(FP8X4),
                rhs_scale=x_scale_tile[:, messages],
                start=True,
                stop=True,
            )
            return acc

        def project(name, raw, first_bank, copy23, together, reuses=(None, None)):
            dealt01 = sb(name + "_dealt01", [P, 2, P, PACK], BF16, reuses=reuses[0])
            dealt23 = sb(name + "_dealt23", [P, 2, P, PACK], BF16, reuses=reuses[1])
            deal(nc.vector.tensor_copy, dealt01, raw, 0, 0)
            deal(copy23, dealt23, raw, 0, 2)
            parts = [dealt01[:, t : t + together] for t in range(0, 2, together)]
            for i, part in enumerate(parts):
                deal(nc.vector.tensor_copy, part, raw, 1, i)
            deal(copy23, dealt23, raw, 1, 2)
            weights = [w for i, part in enumerate(parts) for w in quantise("%s%d" % (name, i), part)]
            return weights, dealt23

        blocks = [slice(b * P, (b + 1) * P) for b in range(T // P)]

        def multiply_turned(weights, bank):
            acc = psum.tile([P, T], F32, name="acc", tag="bank%d" % bank)
            for block in blocks:
                nc.tensor.matmul_mx(
                    out=acc[:, block],
                    lhsT=x_codes[:, block].bitcast(FP8X4),
                    lhsT_scale=x_scale_tile[:, block],
                    rhs=weights[0].bitcast(FP8X4),
                    rhs_scale=weights[1],
                    start=True,
                    stop=True,
                )
            return acc


        halves = [slice(h * HALF_T, (h + 1) * HALF_T) for h in range(2)]
        offset_halves = [
            offsets[:, half.start // ENTRIES_PER_COLUMN : half.stop // ENTRIES_PER_COLUMN] for half in halves
        ]

        warm = sb("warm", [P, 2], F32)
        nc.gpsimd.memset(warm[:, 0:1], 0.0)
        nc.scalar.activation(warm[:, 1:2], warm[:, 0:1], ACT.Sigmoid)

        identity = sb("identity", [P, P], F32)
        make_identity(nc, identity[:])

        u_weights, dealt23 = project("u", w2_raw, 0, nc.scalar.copy, 1)
        u_acc = [multiply(u_weights[t], t) for t in range(2)]
        u_weights = u_weights + quantise("u23", dealt23)
        u_acc.append(multiply(u_weights[2], 2))
        gate = [sb("gate%d" % t, [P, T], F32) for t in range(3)]
        for t in range(3):
            nc.scalar.activation(gate[t][:], u_acc[t][:], ACT.Sigmoid)
        y_weights, dealt23 = project("y", w1_raw, PACK, nc.vector.tensor_copy, 2, ("u_dealt23", "w2_raw1"))
        y0_halves = [multiply(y_weights[0], 3 + h, halves[h]) for h in range(2)]
        y_acc = {1: multiply(y_weights[1], 5)}

        pieces0 = [slice(0, FIRST), slice(FIRST, T)]
        second = T - FIRST
        gap0 = [sb("gap0_%d" % h, [P, part.stop - part.start], F32) for h, part in enumerate(pieces0)]
        step0 = [sb("step0_%d" % h, [P, part.stop - part.start], F32) for h, part in enumerate(pieces0)]
        late_old = sb("late_old", [P, second + T], F32, reuses="w1_raw1")
        old0 = [sb("old0_0", [P, FIRST], F32, reuses="u_dealt23"), late_old[:, 0:second]]
        new = [sb("new%d" % t, [P, T], F32) for t in range(3)]
        planes = sb("planes", [P, PACK, U], F32)

        def form_gap(out, y, old):
            nc.vector.scalar_tensor_tensor(out, y, 0.0, old, ALU.max, ALU.subtract)

        def entries(part):
            return offsets[:, part.start // ENTRIES_PER_COLUMN : part.stop // ENTRIES_PER_COLUMN]

        def scalar_scatter(t, parts=halves):
            for part in parts:
                nc.scalar.activation(window[t][:].indirect(entries(part)), new[t][:, part], ACT.Copy)
            if t < 2:
                nc.sync.dma_start(planes[:, t, :], window[t][:])
            nc.sync.dma_start(out_rows[t], window[t][:])

        everything = slice(0, T)
        nc.vector.tensor_copy(old0[0][:], window[0][:].indirect(entries(pieces0[0])))
        for i, weights in enumerate(quantise("y23", dealt23)):
            y_acc[2 + i] = multiply(weights, 6 + i)
        nc.scalar.activation(old0[1][:], window[0][:].indirect(entries(pieces0[1])), ACT.Copy)
        old = {1: late_old[:, second:]}
        for h in range(2):
            nc.scalar.activation(old[1][:, halves[h]], window[1][:].indirect(offset_halves[h]), ACT.Copy)
        for h in range(2):
            form_gap(gap0[h][:], y0_halves[h][:], old0[h][:])
        for h in range(2):
            nc.vector.tensor_tensor(step0[h][:], gap0[h][:], gate[0][:, pieces0[h]], ALU.mult)
        gate.append(sb("gate3", [P, T], F32))
        nc.scalar.activation(gate[3][:], multiply_turned(u_weights[3], 3)[:], ACT.Sigmoid)
        for h, engine in enumerate((nc.vector, nc.gpsimd)):
            engine.tensor_tensor(new[0][:, pieces0[h]], old0[h][:], step0[h][:], ALU.add)
        scalar_scatter(0, pieces0)

        gap = {1: sb("gap1", [P, T], F32, reuses="step0_0")}
        step = {t: sb("step%d" % t, [P, T], F32) for t in range(1, PACK)}
        for half in halves:
            form_gap(gap[1][:, half], y_acc[1][:, half], old[1][:, half])
        for half in halves:
            nc.gpsimd.tensor_tensor(step[1][:, half], gap[1][:, half], gate[1][:, half], ALU.mult)
        nc.gpsimd.tensor_tensor(new[1][:], old[1][:], step[1][:], ALU.add)
        scalar_scatter(1)
        for t, reuses in ((2, "u_dealt23"), (3, "gate1")):
            old[t] = sb("old%d" % t, [P, T], F32, reuses=reuses)
            gap[t] = sb("gap%d" % t, [P, T], F32)
            for h in range(2):
                nc.vector.tensor_copy(old[t][:, halves[h]], window[t][:].indirect(offset_halves[h]))
            for half in halves:
                form_gap(gap[t][:, half], y_acc[t][:, half], old[t][:, half])
        head, rest = slice(0, VECTOR_PIECE), slice(VECTOR_PIECE, T)
        for part in (head, rest):
            nc.gpsimd.tensor_tensor(step[2][:, part], gap[2][:, part], gate[2][:, part], ALU.mult)
            nc.gpsimd.tensor_tensor(new[2][:, part], old[2][:, part], step[2][:, part], ALU.add)
        gate3 = psum.tile([P, T], F32, name="acc", tag="bank4")
        for block in blocks:
            nc.tensor.transpose(gate3[:, block], gate[3][:, block], identity[:])
        for half in halves:
            nc.vector.tensor_tensor(step[3][:, half], gap[3][:, half], gate3[:, half], ALU.mult)
        nc.vector.tensor_copy(window[2][:].indirect(entries(head)), new[2][:, head])
        scalar_scatter(2, [rest])
        nc.vector.tensor_tensor(window[3][:].indirect(offsets[:]), old[3][:], step[3][:], ALU.add)
        nc.sync.dma_start(out_rows[3], window[3][:])

        out_scale_tile = sb("out_scale_tile", [P, U], U8)
        out_words = out_1[0].rearrange("p c r -> p (c r)").bitcast(I32)
        quarters = [slice(i * QUARTER_U, (i + 1) * QUARTER_U) for i in range(4)]
        woven = [sb("woven%d" % i, [P, QUARTER_U, PACK], BF16) for i in range(4)]
        scalar_parts = [quarters[0], slice(QUARTER_U, SCALAR_SLOTS)]
        vector_parts = [slice(SCALAR_SLOTS, 3 * QUARTER_U), quarters[3]]

        def lay(copy, t, part):
            copy(planes[:, t, part], window[t][:, part])

        def weave(copy, part):
            i = part.start // QUARTER_U
            copy(
                woven[i][:, part.start - i * QUARTER_U : part.stop - i * QUARTER_U, :].rearrange(
                    "p (c i) (w t) -> p c w i t", i=4, t=2
                ),
                planes[:, :, part].rearrange("p (w t) (c i) -> p c w i t", i=4, t=2),
            )

        def pack(i):
            codes = sb("out_codes%d" % i, [P, QUARTER_U], U32)
            nc.vector.quantize_mx(
                out=codes[:].bitcast(FP8X4),
                scales=out_scale_tile[:, quarters[i]],
                in_=woven[i][:, :, :].rearrange("p c t -> p (c t)"),
            )
            nc.sync.dma_start(out_words[:, quarters[i]], codes[:].bitcast(I32))

        lay(nc.scalar.copy, 2, slice(0, SCALAR_SLOTS))
        lay(nc.vector.tensor_copy, 3, slice(SCALAR_SLOTS, U))
        for part in scalar_parts:
            lay(nc.scalar.copy, 3, part)
        for part in vector_parts:
            lay(nc.vector.tensor_copy, 2, part)
        for part in scalar_parts:
            weave(nc.scalar.copy, part)
        for part in (quarters[2], quarters[3], slice(SCALAR_SLOTS, 2 * QUARTER_U)):
            weave(nc.vector.tensor_copy, part)
        for i in (2, 0, 3, 1):
            pack(i)
        for quadrant in range(QUADRANTS):
            queue = nc.scalar if quadrant % 2 else nc.sync
            queue.dma_start(
                out_2[0, 4 * quadrant : 4 * quadrant + 4, :].bitcast(I32),
                out_scale_tile[32 * quadrant : 32 * quadrant + 4, :].bitcast(I32),
            )
